import numpy as np
import ml_dtypes


def mxq(x, axis, fmt="e4m3"):
    dtype, down = {"e4m3": (ml_dtypes.float8_e4m3fn, 7), "e5m2": (ml_dtypes.float8_e5m2, 14)}[fmt]
    v = np.moveaxis(np.asarray(x, np.float32).astype(ml_dtypes.bfloat16).astype(np.float64), axis, -1)
    blocks = v.reshape(v.shape[:-1] + (-1, 32))
    amax = np.abs(blocks).max(-1, keepdims=True)
    byte = np.maximum(np.where(amax > 0, np.frexp(amax)[1] - 1 + 127, 0) - down, 1)
    scale = np.exp2(byte - 127.0)
    codes = (blocks / scale).astype(np.float32).astype(dtype).astype(np.float64)
    return np.moveaxis((codes * scale).reshape(v.shape), -1, axis)


WIDE = False


def mx_kscale(k):
    if not WIDE:
        return np.ones(k)
    levels = np.array([18, -18])
    if k % 512:
        return np.exp2(np.random.permutation(np.resize(levels, k // 32))).repeat(32)
    a = np.empty((k // 512, 16))
    for p in range(k // 512):
        a[p, :8] = np.random.permutation(np.resize(levels, 8))
        for g in range(8):
            far = levels[np.abs(levels - a[p, g]) >= 10]
            a[p, g + 8] = far[np.random.randint(len(far))]
    return np.exp2(a.ravel()).repeat(32)


def f64(x):
    return np.asarray(x).astype(np.float64)


def striped(idx):
    return np.tile(np.asarray(idx).reshape(-1, 16).T, (8, 1)).astype(np.uint16)


def unstriped(offs):
    return offs[:16].T.reshape(-1).astype(np.int64)

def planes(y):
    n, m = y.shape
    v = y.astype(np.float32).astype(ml_dtypes.bfloat16).astype(np.float64).reshape(n // 32, 32, m)
    top = np.abs(v).max(1)
    byte = np.clip(np.where(top > 0, np.frexp(top)[1] - 1 + 127 - 7, 1), 1, 254)
    codes = (v * np.exp2(127.0 - byte)[:, None, :]).reshape(n, m).astype(np.float32).astype(ml_dtypes.float8_e4m3fn).view(np.uint8)
    words = codes.reshape(n // 512, 128, 4, m).transpose(0, 1, 3, 2)
    return np.ascontiguousarray(words), np.ascontiguousarray(byte.astype(np.uint8).reshape(n // 512, 16, m))


def sig(x):
    return 1.0 / (1.0 + np.exp(-x))


def setup_inputs():
    n = np.random.standard_normal
    uni = np.random.uniform
    idx = np.random.permutation(2048)[:512]
    jdx = np.random.permutation(2048)[:512]
    f_d = mx_kscale(512)
    f_j = np.ones(2048)
    f_j[jdx] = mx_kscale(512)
    return {
        "uT": (n((512, 2048)) / np.sqrt(512) * f_d[:, None]).astype(np.float32),
        "vT": (n((512, 2048)) / f_d[:, None] * f_j[None, :]).astype(np.float32),
        "su": np.tile(uni(0.75, 1.3, 2048), (128, 1)).astype(np.float32),
        "sv": np.tile(uni(0.75, 1.3, 2048) / f_j, (128, 1)).astype(np.float32),
        "y": (np.random.randint(0, 2, (512, 512))).astype(np.float32),
        "offs": striped(idx),
        "qoffs": striped(jdx),
    }


def reference(uT, vT, su, sv, y, offs, qoffs):
    idx = unstriped(offs)
    jdx = unstriped(qoffs)
    uT_i = f64(uT)[:, idx]
    vT_j = f64(vT)[:, jdx]
    su_i = f64(su)[:1][:, idx]
    sv_j = f64(sv)[:1][:, jdx]
    suc = su_i.T
    a = mxq(uT_i, 0, "e4m3").T @ mxq(vT_j, 0, "e4m3")
    z = suc * sv_j * a
    g = suc * sv_j * (sig(z) - f64(y))
    du = mxq(vT_j, 1, "e4m3") @ mxq(g, 1, "e5m2").T
    out_0 = np.zeros((512, 2048))
    out_0[:, idx] = du
    return (out_0,) + planes(out_0)

@@ -1,0 +1,269 @@
+from contextlib import ExitStack
+
+import concourse.mybir as mybir
+from concourse.masks import make_identity
+
+F32 = mybir.dt.float32
+BF16 = mybir.dt.bfloat16
+U32 = mybir.dt.uint32
+I32 = mybir.dt.int32
+U16 = mybir.dt.uint16
+U8 = mybir.dt.uint8
+E4M3 = mybir.dt.float8_e4m3fn_x4
+E5M2 = mybir.dt.float8_e5m2_x4
+ACT = mybir.ActivationFunctionType
+ALU = mybir.AluOpType
+
+P = 128
+LANES = 4
+D = 512
+SLOTS = 512
+TABLE = 2048
+LIVE = P - 1
+FLOPS = 2 * 2 * D * SLOTS * SLOTS
+BYTES = 4 * (3 * D * TABLE + SLOTS * SLOTS + 2 * TABLE) + D * TABLE + 16 * TABLE + 2 * 2 * P * 32
+CHUNKS = [(0, 256), (256, 512), (512, 1024), (1024, 1536), (1536, 2048)]
+
+
+def tile_attend_gclip_sg_u_pl_kernel(
+    tc, uT, vT, su, sv, y, offs, qoffs, out_0, out_1, out_2
+):
+    nc = tc.nc
+    with ExitStack() as ctx:
+        keep = ctx.enter_context(tc.tile_pool(name="keep", bufs=1))
+        psum = ctx.enter_context(tc.psum_pool(name="psum", bufs=4))
+
+        def sb(name, shape, dtype, tag=None):
+            return keep.tile(shape, dtype, name=name, tag=tag or name, align_bytes=64)
+
+        def bank(name, tag):
+            return psum.tile([P, LANES, P], F32, name=name, tag=tag)
+
+        y_sb = sb("y_sb", [P, LANES, SLOTS], F32)
+        nc.sync.dma_start(out=y_sb[:], in_=y.rearrange("(q p) j -> p q j", p=P))
+        offs_sb = keep.tile([P, SLOTS // 16], U16, name="offs_sb")
+        qoffs_sb = keep.tile([P, SLOTS // 16], U16, name="qoffs_sb")
+        nc.sync.dma_start(offs_sb[:], offs)
+        nc.sync.dma_start(qoffs_sb[:], qoffs)
+        su_win = sb("su_win", [P, TABLE], F32)
+        sv_win = sb("sv_win", [P, TABLE], F32)
+        for win, src in ((su_win, su), (sv_win, sv)):
+            nc.vector.memset(win[0:LIVE, :], 0.0)
+            nc.scalar.dma_start(out=win[LIVE:P, :], in_=src[0:1, :])
+        v_win = [sb("v_win%d" % t, [P, TABLE], F32) for t in range(LANES)]
+        u_win = [sb("u_win%d" % t, [P, TABLE], F32) for t in range(LANES)]
+        for wins, src in ((v_win, vT), (u_win, uT)):
+            rows = src.rearrange("(p t) c -> t p c", t=LANES)
+            for t in range(LANES):
+                nc.sync.dma_start(out=wins[t][:], in_=rows[t])
+
+        ident = sb("ident", [P, P], F32)
+        make_identity(nc, ident[:])
+        out_win = [sb("out_win%d" % t, [P, TABLE], F32) for t in range(LANES)]
+        for t in range(LANES):
+            nc.gpsimd.memset(out_win[t][:], 0.0)
+
+        warm = sb("warm", [P, 8], F32)
+        nc.scalar.activation(warm[:, 0:1], ident[:, 0:1], ACT.Sigmoid)
+        su_row = sb("su_row", [P, SLOTS], F32)
+        sv_row = sb("sv_row", [P, SLOTS], F32)
+        nc.vector.tensor_copy(su_row[:], su_win[:].indirect(offs_sb[:]))
+        nc.vector.tensor_copy(sv_row[:], sv_win[:].indirect(qoffs_sb[:]))
+        su_ps = bank("su_ps", "b")
+        sv_ps = bank("sv_ps", "b")
+        for q in range(LANES):
+            nc.tensor.transpose(su_ps[:, q, :], su_row[:, q * P : (q + 1) * P], ident[:])
+        for r in range(LANES):
+            nc.tensor.transpose(sv_ps[:, r, :], sv_row[:, r:SLOTS:LANES], ident[:])
+        su_col = sb("su_col", [P, LANES], F32)
+        su_m2 = sb("su_m2", [P, LANES], F32)
+        sv_col = sb("sv_col", [P, LANES], F32)
+        nc.scalar.copy(su_col[:], su_ps[:, :, LIVE])
+        nc.scalar.activation(su_m2[:], su_ps[:, :, LIVE], ACT.Copy, scale=-2.0)
+        nc.scalar.copy(sv_col[:], sv_ps[:, :, LIVE])
+
+        ys = sb("ys", [P, LANES, SLOTS], F32)
+        sgn = sb("sgn", [P, LANES, P, LANES], F32)
+        for q in range(LANES):
+            nc.scalar.activation(
+                ys[:, q, :], y_sb[:, q, :], ACT.Identity,
+                bias=su_col[:, q : q + 1], scale=su_m2[:, q : q + 1],
+            )
+            ys_ps = bank("ys_ps", "a")
+            for r in range(LANES):
+                nc.tensor.transpose(ys_ps[:, r, :], ys[:, q, r:SLOTS:LANES], ident[:])
+            nc.vector.tensor_tensor(
+                sgn[:, q, :, :],
+                ys_ps[:].rearrange("s r i -> s i r"),
+                sv_col[:].unsqueeze(1).to_broadcast([P, P, LANES]),
+                ALU.mult,
+            )
+
+        v_got = sb("v_got", [P, LANES, SLOTS], BF16)
+        for t in range(LANES):
+            nc.vector.tensor_copy(v_got[:, t, :], v_win[t][:].indirect(qoffs_sb[:]))
+        vt_in = sb("vt_in", [P, LANES, P, LANES], BF16)
+        for half in range(2):
+            vt_ps = bank("vt_ps", "b")
+            for tt in range(2):
+                pairs = v_got[:, 2 * half + tt, :].bitcast(F32)
+                for u in range(2):
+                    nc.tensor.transpose(vt_ps[:, 2 * tt + u, :], pairs[:, u : SLOTS // 2 : 2], ident[:])
+            nc.scalar.copy(
+                vt_in[:, 2 * half : 2 * half + 2, :, :].bitcast(F32),
+                vt_ps[:].rearrange("s (tt u) p -> s tt p u", u=2),
+            )
+        vd_in = sb("vd_in", [P, LANES, P, LANES], BF16)
+        nc.scalar.copy(vd_in[:], v_got[:].rearrange("p t (s r) -> p r s t", r=LANES))
+        vd_codes = sb("vd_codes", [P, SLOTS], U32)
+        vd_scales = sb("vd_scales", [P, SLOTS], U8)
+        nc.vector.quantize_mx(
+            out=vd_codes[:].bitcast(E4M3), scales=vd_scales[:],
+            in_=vd_in[:].rearrange("p r s t -> p (r s t)"),
+        )
+        vt_codes = sb("vt_codes", [P, D], U32)
+        vt_scales = sb("vt_scales", [P, D], U8)
+        nc.vector.quantize_mx(
+            out=vt_codes[:].bitcast(E4M3), scales=vt_scales[:],
+            in_=vt_in[:].rearrange("s t p r -> s (t p r)"),
+        )
+
+        u_in = sb("u_in", [P, SLOTS, LANES], BF16)
+        u_codes = sb("u_codes", [P, SLOTS], U32)
+        u_scales = sb("u_scales", [P, SLOTS], U8)
+        for t in range(LANES - 1):
+            nc.vector.tensor_copy(u_in[:, :, t], u_win[t][:].indirect(offs_sb[:]))
+        HALF = SLOTS // 2
+        for h in range(2):
+            cols = slice(h * HALF, (h + 1) * HALF)
+            nc.vector.tensor_copy(
+                u_in[:, cols, LANES - 1],
+                u_win[LANES - 1][:].indirect(offs_sb[:, h * HALF // 16 : (h + 1) * HALF // 16]),
+            )
+        for h in range(2):
+            cols = slice(h * HALF, (h + 1) * HALF)
+            nc.vector.quantize_mx(
+                out=u_codes[:, cols].bitcast(E4M3), scales=u_scales[:, cols],
+                in_=u_in[:, cols, :].rearrange("p i t -> p (i t)"),
+            )
+
+        g_codes = sb("g_codes", [P, HALF + SLOTS], U32)
+        g_scales = sb("g_scales", [P, HALF + SLOTS], U8)
+        nc.gpsimd.memset(g_codes[:, 0:HALF], 0)
+        nc.gpsimd.memset(g_scales[:, 0:HALF], 0)
+        zs = [sb("zs%d" % q, [P, SLOTS], F32) for q in range(LANES)]
+        sg = [sb("sg%d" % q, [P, SLOTS], F32) for q in range(LANES)]
+        g_in = [sb("g_in%d" % q, [P, SLOTS], BF16) for q in range(LANES)]
+
+        def score(q):
+            a_ps = bank("a_ps", "a")
+            cols = slice(q * P, (q + 1) * P)
+            for r in range(LANES):
+                rc = slice(r * P, (r + 1) * P)
+                nc.tensor.matmul_mx(
+                    out=a_ps[:, r, :],
+                    lhsT=vd_codes[:, rc].bitcast(E4M3), lhsT_scale=vd_scales[:, rc],
+                    rhs=u_codes[:, cols].bitcast(E4M3), rhs_scale=u_scales[:, cols],
+                    start=True, stop=True,
+                )
+            nc.vector.tensor_tensor(
+                zs[q][:].rearrange("s (i r) -> s i r", r=LANES),
+                a_ps[:].rearrange("s r i -> s i r"),
+                sgn[:, q, :, :],
+                ALU.mult,
+            )
+            nc.scalar.activation(sg[q][:], zs[q][:], ACT.Sigmoid)
+
+        def grad(q):
+            nc.vector.tensor_tensor(
+                g_in[q][:], sg[q][:], sgn[:, q, :, :].rearrange("s i r -> s (i r)"), ALU.mult
+            )
+
+        def quant(q):
+            cols = slice(HALF + q * P, HALF + (q + 1) * P)
+            nc.vector.quantize_mx(
+                out=g_codes[:, cols].bitcast(E5M2), scales=g_scales[:, cols], in_=g_in[q][:]
+            )
+
+        for step in range(LANES + 2):
+            if step < LANES:
+                score(step)
+            if 1 <= step <= LANES:
+                grad(step - 1)
+            if step >= 2:
+                quant(step - 2)
+
+        out_rows = out_0.rearrange("(p t) c -> t p c", t=LANES)
+        pairs_in = sb("pairs_in", [P, 2 * TABLE], F32)
+
+        def lane(t, lo, hi):
+            first = (t // 2) * TABLE
+            halves = pairs_in[:, first + lo : first + hi].bitcast(BF16)
+            nc.scalar.copy(halves[:, t % 2 : 2 * (hi - lo) : 2], out_win[t][:, lo:hi])
+
+        def product(t, first):
+            du_ps = bank("du_ps", "b")
+            flat = du_ps[:].rearrange("p a b -> p (a b)")
+            tcols = slice(t * P, (t + 1) * P)
+            nc.tensor.matmul_mx(
+                out=flat,
+                lhsT=vt_codes[:, tcols].bitcast(E4M3), lhsT_scale=vt_scales[:, tcols],
+                rhs=g_codes[:, first : first + SLOTS].bitcast(E5M2),
+                rhs_scale=g_scales[:, first : first + SLOTS],
+                start=True, stop=True,
+            )
+            return flat
+
+        du = [sb("du%d" % t, [P, SLOTS], F32) for t in range(LANES)]
+        early = sg[LANES - 1][:, 0:HALF]
+        nc.scalar.copy(early, product(0, 0)[:, HALF:SLOTS])
+        nc.scalar.copy(du[0][:, HALF:SLOTS], product(0, HALF)[:, HALF:SLOTS])
+        for t in range(1, LANES):
+            nc.scalar.copy(du[t][:], product(t, HALF))
+        for t in range(LANES):
+            if t == 0:
+                nc.vector.tensor_copy(out_win[0][:].indirect(offs_sb[:, 0 : HALF // 16]), early)
+                nc.vector.tensor_copy(
+                    out_win[0][:].indirect(offs_sb[:, HALF // 16 : SLOTS // 16]), du[0][:, HALF:SLOTS]
+                )
+            else:
+                nc.vector.tensor_copy(out_win[t][:].indirect(offs_sb[:]), du[t][:])
+            nc.sync.dma_start(out=out_rows[t], in_=out_win[t][:])
+            if t < LANES - 1:
+                lane(t, 0, TABLE)
+        for lo, hi in CHUNKS:
+            lane(LANES - 1, lo, hi)
+
+        o_codes = sb("o_codes", [P, TABLE], U32)
+        o_scales = sb("o_scales", [P, TABLE], U8)
+        words_out = out_1[0].rearrange("p c l -> p (c l)").bitcast(I32)
+        spent = ["v_win0", "v_win1", "v_win2", "v_win3", "su_win", "sv_win"]
+        o_in = [sb("o_in%d" % k, [P, hi - lo, LANES], BF16, spent[k]) for k, (lo, hi) in enumerate(CHUNKS)]
+
+        def weave(k):
+            lo, hi = CHUNKS[k]
+            nc.vector.tensor_copy(
+                o_in[k][:].bitcast(F32),
+                pairs_in[:].rearrange("p (u c) -> p c u", u=2)[:, lo:hi, :],
+            )
+
+        def finish(k):
+            lo, hi = CHUNKS[k]
+            nc.vector.quantize_mx(
+                out=o_codes[:, lo:hi].bitcast(E4M3), scales=o_scales[:, lo:hi],
+                in_=o_in[k][:].rearrange("p c t -> p (c t)"),
+            )
+            nc.sync.dma_start(out=words_out[:, lo:hi], in_=o_codes[:, lo:hi].bitcast(I32))
+
+        for step in range(len(CHUNKS) + 1):
+            if step < len(CHUNKS):
+                weave(step)
+            if step >= 1:
+                finish(step - 1)
+        scales_out = out_2[0].bitcast(I32)
+        for quad in range(4):
+            eng = nc.scalar if quad % 2 else nc.sync
+            eng.dma_start(
+                out=scales_out[4 * quad : 4 * quad + 4, :],
+                in_=o_scales[32 * quad : 32 * quad + 4, :].bitcast(I32),
+            )

@@ -19,10 +19,12 @@ LANES = 4
 D = 512
 SLOTS = 512
 TABLE = 2048
-LIVE = P - 1
+LIVE = 0
+HALF = SLOTS // 2
 FLOPS = 2 * 2 * D * SLOTS * SLOTS
 BYTES = 4 * (3 * D * TABLE + SLOTS * SLOTS + 2 * TABLE) + D * TABLE + 16 * TABLE + 2 * 2 * P * 32
-CHUNKS = [(0, 256), (256, 512), (512, 1024), (1024, 1536), (1536, 2048)]
+CHUNKS = [(0, 256), (256, 768), (768, 1280), (1280, 1536), (1536, 1792), (1792, 2048)]
+ON_VECTOR = 4
 
 
 def tile_attend_gclip_sg_u_pl_kernel(
@@ -47,9 +49,11 @@ def tile_attend_gclip_sg_u_pl_kernel(
         nc.sync.dma_start(qoffs_sb[:], qoffs)
         su_win = sb("su_win", [P, TABLE], F32)
         sv_win = sb("sv_win", [P, TABLE], F32)
-        for win, src in ((su_win, su), (sv_win, sv)):
-            nc.vector.memset(win[0:LIVE, :], 0.0)
-            nc.scalar.dma_start(out=win[LIVE:P, :], in_=src[0:1, :])
+        PER = TABLE // P
+        su_cut = sb("su_cut", [P, PER], F32)
+        sv_cut = sb("sv_cut", [P, PER], F32)
+        for cut, src in ((su_cut, su), (sv_cut, sv)):
+            nc.scalar.dma_start(out=cut[:], in_=src[0].rearrange("(p k) -> p k", k=PER))
         v_win = [sb("v_win%d" % t, [P, TABLE], F32) for t in range(LANES)]
         u_win = [sb("u_win%d" % t, [P, TABLE], F32) for t in range(LANES)]
         for wins, src in ((v_win, vT), (u_win, uT)):
@@ -61,14 +65,37 @@ def tile_attend_gclip_sg_u_pl_kernel(
         make_identity(nc, ident[:])
         out_win = [sb("out_win%d" % t, [P, TABLE], F32) for t in range(LANES)]
         for t in range(LANES):
-            nc.gpsimd.memset(out_win[t][:], 0.0)
+            nc.vector.memset(out_win[t][:].bitcast(I32), 0)
 
+        g_codes = sb("g_codes", [P, HALF + SLOTS], U32)
+        g_scales = sb("g_scales", [P, HALF + SLOTS], U8)
+        nc.vector.memset(g_codes[:, 0:HALF], 0)
+        nc.vector.memset(g_scales[:, 0:HALF].bitcast(U32), 0)
         warm = sb("warm", [P, 8], F32)
         nc.scalar.activation(warm[:, 0:1], ident[:, 0:1], ACT.Sigmoid)
+        for win, cut in ((su_win, su_cut), (sv_win, sv_cut)):
+            for b in range(PER // LANES):
+                rep_ps = bank("rep_ps", "a")
+                for k in range(LANES):
+                    col = LANES * b + k
+                    nc.tensor.transpose(
+                        rep_ps[:, k, :], cut[:, col : col + 1].to_broadcast([P, P]), ident[:]
+                    )
+                nc.scalar.copy(
+                    win[:].rearrange("m (n k) -> m n k", k=PER)[:, :, LANES * b : LANES * (b + 1)],
+                    rep_ps[:].rearrange("m k n -> m n k"),
+                )
         su_row = sb("su_row", [P, SLOTS], F32)
         sv_row = sb("sv_row", [P, SLOTS], F32)
+        v_got = sb("v_got", [P, LANES, SLOTS], BF16)
+
+        def gather_v(t):
+            nc.vector.tensor_copy(v_got[:, t, :], v_win[t][:].indirect(qoffs_sb[:]))
+
         nc.vector.tensor_copy(su_row[:], su_win[:].indirect(offs_sb[:]))
+        gather_v(0)
         nc.vector.tensor_copy(sv_row[:], sv_win[:].indirect(qoffs_sb[:]))
+        gather_v(1)
         su_ps = bank("su_ps", "b")
         sv_ps = bank("sv_ps", "b")
         for q in range(LANES):
@@ -98,10 +125,15 @@ def tile_attend_gclip_sg_u_pl_kernel(
                 sv_col[:].unsqueeze(1).to_broadcast([P, P, LANES]),
                 ALU.mult,
             )
+            if q == 0:
+                gather_v(2)
+        gather_v(3)
 
-        v_got = sb("v_got", [P, LANES, SLOTS], BF16)
-        for t in range(LANES):
-            nc.vector.tensor_copy(v_got[:, t, :], v_win[t][:].indirect(qoffs_sb[:]))
+        vd_in = sb("vd_in", [P, LANES, P, LANES], BF16)
+        nc.scalar.copy(
+            vd_in[:].rearrange("p r s t -> p s t r"),
+            v_got[:].rearrange("p t (s r) -> p s t r", r=LANES),
+        )
         vt_in = sb("vt_in", [P, LANES, P, LANES], BF16)
         for half in range(2):
             vt_ps = bank("vt_ps", "b")
@@ -113,27 +145,20 @@ def tile_attend_gclip_sg_u_pl_kernel(
                 vt_in[:, 2 * half : 2 * half + 2, :, :].bitcast(F32),
                 vt_ps[:].rearrange("s (tt u) p -> s tt p u", u=2),
             )
-        vd_in = sb("vd_in", [P, LANES, P, LANES], BF16)
-        nc.scalar.copy(vd_in[:], v_got[:].rearrange("p t (s r) -> p r s t", r=LANES))
+        u_in = sb("u_in", [P, SLOTS, LANES], BF16)
+        u_codes = sb("u_codes", [P, SLOTS], U32)
+        u_scales = sb("u_scales", [P, SLOTS], U8)
+        u_got = sb("u_got", [P, 2, SLOTS], BF16)
+        for t in range(2):
+            nc.vector.tensor_copy(u_got[:, t, :], u_win[t][:].indirect(offs_sb[:]))
+        nc.scalar.copy(u_in[:, :, 0:2], u_got[:].rearrange("p t i -> p i t"))
         vd_codes = sb("vd_codes", [P, SLOTS], U32)
         vd_scales = sb("vd_scales", [P, SLOTS], U8)
         nc.vector.quantize_mx(
             out=vd_codes[:].bitcast(E4M3), scales=vd_scales[:],
             in_=vd_in[:].rearrange("p r s t -> p (r s t)"),
         )
-        vt_codes = sb("vt_codes", [P, D], U32)
-        vt_scales = sb("vt_scales", [P, D], U8)
-        nc.vector.quantize_mx(
-            out=vt_codes[:].bitcast(E4M3), scales=vt_scales[:],
-            in_=vt_in[:].rearrange("s t p r -> s (t p r)"),
-        )
-
-        u_in = sb("u_in", [P, SLOTS, LANES], BF16)
-        u_codes = sb("u_codes", [P, SLOTS], U32)
-        u_scales = sb("u_scales", [P, SLOTS], U8)
-        for t in range(LANES - 1):
-            nc.vector.tensor_copy(u_in[:, :, t], u_win[t][:].indirect(offs_sb[:]))
-        HALF = SLOTS // 2
+        nc.vector.tensor_copy(u_in[:, :, 2], u_win[2][:].indirect(offs_sb[:]))
         for h in range(2):
             cols = slice(h * HALF, (h + 1) * HALF)
             nc.vector.tensor_copy(
@@ -147,10 +172,13 @@ def tile_attend_gclip_sg_u_pl_kernel(
                 in_=u_in[:, cols, :].rearrange("p i t -> p (i t)"),
             )
 
-        g_codes = sb("g_codes", [P, HALF + SLOTS], U32)
-        g_scales = sb("g_scales", [P, HALF + SLOTS], U8)
-        nc.gpsimd.memset(g_codes[:, 0:HALF], 0)
-        nc.gpsimd.memset(g_scales[:, 0:HALF], 0)
+        vt_codes = sb("vt_codes", [P, D], U32)
+        vt_scales = sb("vt_scales", [P, D], U8)
+        nc.vector.quantize_mx(
+            out=vt_codes[:].bitcast(E4M3), scales=vt_scales[:],
+            in_=vt_in[:].rearrange("s t p r -> s (t p r)"),
+        )
+
         zs = [sb("zs%d" % q, [P, SLOTS], F32) for q in range(LANES)]
         sg = [sb("sg%d" % q, [P, SLOTS], F32) for q in range(LANES)]
         g_in = [sb("g_in%d" % q, [P, SLOTS], BF16) for q in range(LANES)]
@@ -242,7 +270,8 @@ def tile_attend_gclip_sg_u_pl_kernel(
 
         def weave(k):
             lo, hi = CHUNKS[k]
-            nc.vector.tensor_copy(
+            copy = nc.vector.tensor_copy if k < ON_VECTOR else nc.scalar.copy
+            copy(
                 o_in[k][:].bitcast(F32),
                 pairs_in[:].rearrange("p (u c) -> p c u", u=2)[:, lo:hi, :],
             )

@@ -42,7 +42,7 @@ def tile_attend_gclip_sg_u_pl_kernel(
             return psum.tile([P, LANES, P], F32, name=name, tag=tag)
 
         y_sb = sb("y_sb", [P, LANES, SLOTS], F32)
-        nc.sync.dma_start(out=y_sb[:], in_=y.rearrange("(q p) j -> p q j", p=P))
+        nc.sync.dma_start(out=y_sb[:], in_=y.rearrange("(p q) j -> p q j", q=LANES))
         offs_sb = keep.tile([P, SLOTS // 16], U16, name="offs_sb")
         qoffs_sb = keep.tile([P, SLOTS // 16], U16, name="qoffs_sb")
         nc.sync.dma_start(offs_sb[:], offs)
@@ -99,7 +99,7 @@ def tile_attend_gclip_sg_u_pl_kernel(
         su_ps = bank("su_ps", "b")
         sv_ps = bank("sv_ps", "b")
         for q in range(LANES):
-            nc.tensor.transpose(su_ps[:, q, :], su_row[:, q * P : (q + 1) * P], ident[:])
+            nc.tensor.transpose(su_ps[:, q, :], su_row[:, q:SLOTS:LANES], ident[:])
         for r in range(LANES):
             nc.tensor.transpose(sv_ps[:, r, :], sv_row[:, r:SLOTS:LANES], ident[:])
         su_col = sb("su_col", [P, LANES], F32)
@@ -110,7 +110,8 @@ def tile_attend_gclip_sg_u_pl_kernel(
         nc.scalar.copy(sv_col[:], sv_ps[:, :, LIVE])
 
         ys = sb("ys", [P, LANES, SLOTS], F32)
-        sgn = sb("sgn", [P, LANES, P, LANES], F32)
+        sgn = sb("sgn", [P, SLOTS * LANES], F32)
+        sgn_dealt = sgn[:].rearrange("s (p q r) -> s q p r", q=LANES, r=LANES)
         for q in range(LANES):
             nc.scalar.activation(
                 ys[:, q, :], y_sb[:, q, :], ACT.Identity,
@@ -120,7 +121,7 @@ def tile_attend_gclip_sg_u_pl_kernel(
             for r in range(LANES):
                 nc.tensor.transpose(ys_ps[:, r, :], ys[:, q, r:SLOTS:LANES], ident[:])
             nc.vector.tensor_tensor(
-                sgn[:, q, :, :],
+                sgn_dealt[:, q, :, :],
                 ys_ps[:].rearrange("s r i -> s i r"),
                 sv_col[:].unsqueeze(1).to_broadcast([P, P, LANES]),
                 ALU.mult,
@@ -129,11 +130,12 @@ def tile_attend_gclip_sg_u_pl_kernel(
                 gather_v(2)
         gather_v(3)
 
-        vd_in = sb("vd_in", [P, LANES, P, LANES], BF16)
-        nc.scalar.copy(
-            vd_in[:].rearrange("p r s t -> p s t r"),
-            v_got[:].rearrange("p t (s r) -> p s t r", r=LANES),
-        )
+        vd_in = sb("vd_in", [P, LANES, P, LANES], BF16, "staged")
+        for t in (0, 2):
+            nc.scalar.copy(
+                vd_in[:, :, :, t : t + 2],
+                v_got[:, t : t + 2, :].rearrange("p t (s r) -> p r s t", r=LANES),
+            )
         vt_in = sb("vt_in", [P, LANES, P, LANES], BF16)
         for half in range(2):
             vt_ps = bank("vt_ps", "b")
@@ -145,19 +147,19 @@ def tile_attend_gclip_sg_u_pl_kernel(
                 vt_in[:, 2 * half : 2 * half + 2, :, :].bitcast(F32),
                 vt_ps[:].rearrange("s (tt u) p -> s tt p u", u=2),
             )
-        u_in = sb("u_in", [P, SLOTS, LANES], BF16)
-        u_codes = sb("u_codes", [P, SLOTS], U32)
-        u_scales = sb("u_scales", [P, SLOTS], U8)
-        u_got = sb("u_got", [P, 2, SLOTS], BF16)
-        for t in range(2):
-            nc.vector.tensor_copy(u_got[:, t, :], u_win[t][:].indirect(offs_sb[:]))
-        nc.scalar.copy(u_in[:, :, 0:2], u_got[:].rearrange("p t i -> p i t"))
         vd_codes = sb("vd_codes", [P, SLOTS], U32)
         vd_scales = sb("vd_scales", [P, SLOTS], U8)
         nc.vector.quantize_mx(
             out=vd_codes[:].bitcast(E4M3), scales=vd_scales[:],
             in_=vd_in[:].rearrange("p r s t -> p (r s t)"),
         )
+        u_in = sb("u_in", [P, SLOTS, LANES], BF16, "staged")
+        u_codes = sb("u_codes", [P, SLOTS], U32)
+        u_scales = sb("u_scales", [P, SLOTS], U8)
+        u_got = sb("u_got", [P, 2, SLOTS], BF16)
+        for t in range(2):
+            nc.vector.tensor_copy(u_got[:, t, :], u_win[t][:].indirect(offs_sb[:]))
+        nc.scalar.copy(u_in[:, :, 0:2], u_got[:].rearrange("p t i -> p i t"))
         nc.vector.tensor_copy(u_in[:, :, 2], u_win[2][:].indirect(offs_sb[:]))
         for h in range(2):
             cols = slice(h * HALF, (h + 1) * HALF)
@@ -172,7 +174,7 @@ def tile_attend_gclip_sg_u_pl_kernel(
                 in_=u_in[:, cols, :].rearrange("p i t -> p (i t)"),
             )
 
-        vt_codes = sb("vt_codes", [P, D], U32)
+        vt_codes = sb("vt_codes", [P, D], U32, "staged")
         vt_scales = sb("vt_scales", [P, D], U8)
         nc.vector.quantize_mx(
             out=vt_codes[:].bitcast(E4M3), scales=vt_scales[:],
@@ -197,15 +199,19 @@ def tile_attend_gclip_sg_u_pl_kernel(
             nc.vector.tensor_tensor(
                 zs[q][:].rearrange("s (i r) -> s i r", r=LANES),
                 a_ps[:].rearrange("s r i -> s i r"),
-                sgn[:, q, :, :],
+                sgn[:, q * SLOTS : (q + 1) * SLOTS].rearrange("s (i r) -> s i r", r=LANES),
                 ALU.mult,
             )
             nc.scalar.activation(sg[q][:], zs[q][:], ACT.Sigmoid)
 
         def grad(q):
-            nc.vector.tensor_tensor(
-                g_in[q][:], sg[q][:], sgn[:, q, :, :].rearrange("s i r -> s (i r)"), ALU.mult
-            )
+            parts = 2 if q == LANES - 1 else 1
+            width = SLOTS // parts
+            for lo in range(0, SLOTS, width):
+                nc.vector.tensor_tensor(
+                    g_in[q][:, lo : lo + width], sg[q][:, lo : lo + width],
+                    sgn[:, q * SLOTS + lo : q * SLOTS + lo + width], ALU.mult,
+                )
 
         def quant(q):
             cols = slice(HALF + q * P, HALF + (q + 1) * P)
@@ -284,15 +290,16 @@ def tile_attend_gclip_sg_u_pl_kernel(
             )
             nc.sync.dma_start(out=words_out[:, lo:hi], in_=o_codes[:, lo:hi].bitcast(I32))
 
+        def store_scales(lo, hi, queues):
+            for quad in range(4):
+                queues[quad % 2].dma_start(
+                    out=out_2[0, 4 * quad : 4 * quad + 4, lo:hi].bitcast(I32),
+                    in_=o_scales[32 * quad : 32 * quad + 4, lo:hi].bitcast(I32),
+                )
+
         for step in range(len(CHUNKS) + 1):
             if step < len(CHUNKS):
                 weave(step)
             if step >= 1:
                 finish(step - 1)
-        scales_out = out_2[0].bitcast(I32)
-        for quad in range(4):
-            eng = nc.scalar if quad % 2 else nc.sync
-            eng.dma_start(
-                out=scales_out[4 * quad : 4 * quad + 4, :],
-                in_=o_scales[32 * quad : 32 * quad + 4, :].bitcast(I32),
-            )
+        store_scales(0, TABLE, (nc.scalar, nc.sync))

@@ -19,12 +19,12 @@ LANES = 4
 D = 512
 SLOTS = 512
 TABLE = 2048
-LIVE = 0
+LIVE = P - 1
 HALF = SLOTS // 2
 FLOPS = 2 * 2 * D * SLOTS * SLOTS
 BYTES = 4 * (3 * D * TABLE + SLOTS * SLOTS + 2 * TABLE) + D * TABLE + 16 * TABLE + 2 * 2 * P * 32
 CHUNKS = [(0, 256), (256, 768), (768, 1280), (1280, 1536), (1536, 1792), (1792, 2048)]
-ON_VECTOR = 4
+ON_VECTOR = 3
 
 
 def tile_attend_gclip_sg_u_pl_kernel(
@@ -49,11 +49,8 @@ def tile_attend_gclip_sg_u_pl_kernel(
         nc.sync.dma_start(qoffs_sb[:], qoffs)
         su_win = sb("su_win", [P, TABLE], F32)
         sv_win = sb("sv_win", [P, TABLE], F32)
-        PER = TABLE // P
-        su_cut = sb("su_cut", [P, PER], F32)
-        sv_cut = sb("sv_cut", [P, PER], F32)
-        for cut, src in ((su_cut, su), (sv_cut, sv)):
-            nc.scalar.dma_start(out=cut[:], in_=src[0].rearrange("(p k) -> p k", k=PER))
+        for win, src in ((su_win, su), (sv_win, sv)):
+            nc.scalar.dma_start(out=win[LIVE:P, :], in_=src[0:1, :])
         v_win = [sb("v_win%d" % t, [P, TABLE], F32) for t in range(LANES)]
         u_win = [sb("u_win%d" % t, [P, TABLE], F32) for t in range(LANES)]
         for wins, src in ((v_win, vT), (u_win, uT)):
@@ -63,9 +60,14 @@ def tile_attend_gclip_sg_u_pl_kernel(
 
         ident = sb("ident", [P, P], F32)
         make_identity(nc, ident[:])
-        out_win = [sb("out_win%d" % t, [P, TABLE], F32) for t in range(LANES)]
-        for t in range(LANES):
-            nc.vector.memset(out_win[t][:].bitcast(I32), 0)
+        for win in (su_win, sv_win):
+            nc.gpsimd.memset(win[0:LIVE, :], 0.0)
+        out_tags = ["out_win0", "out_win1", "su_win", "sv_win"]
+        out_win = [sb("out_win%d" % t, [P, TABLE], F32, out_tags[t]) for t in range(LANES)]
+        ODD = TABLE // 2 - 1
+        for t in range(2):
+            nc.vector.memset(out_win[t][:, 0:ODD], 0.0)
+            nc.vector.memset(out_win[t][:, ODD:TABLE], 0.0)
 
         g_codes = sb("g_codes", [P, HALF + SLOTS], U32)
         g_scales = sb("g_scales", [P, HALF + SLOTS], U8)
@@ -73,18 +75,6 @@ def tile_attend_gclip_sg_u_pl_kernel(
         nc.vector.memset(g_scales[:, 0:HALF].bitcast(U32), 0)
         warm = sb("warm", [P, 8], F32)
         nc.scalar.activation(warm[:, 0:1], ident[:, 0:1], ACT.Sigmoid)
-        for win, cut in ((su_win, su_cut), (sv_win, sv_cut)):
-            for b in range(PER // LANES):
-                rep_ps = bank("rep_ps", "a")
-                for k in range(LANES):
-                    col = LANES * b + k
-                    nc.tensor.transpose(
-                        rep_ps[:, k, :], cut[:, col : col + 1].to_broadcast([P, P]), ident[:]
-                    )
-                nc.scalar.copy(
-                    win[:].rearrange("m (n k) -> m n k", k=PER)[:, :, LANES * b : LANES * (b + 1)],
-                    rep_ps[:].rearrange("m k n -> m n k"),
-                )
         su_row = sb("su_row", [P, SLOTS], F32)
         sv_row = sb("sv_row", [P, SLOTS], F32)
         v_got = sb("v_got", [P, LANES, SLOTS], BF16)
@@ -96,6 +86,8 @@ def tile_attend_gclip_sg_u_pl_kernel(
         gather_v(0)
         nc.vector.tensor_copy(sv_row[:], sv_win[:].indirect(qoffs_sb[:]))
         gather_v(1)
+        for t in (2, 3):
+            nc.vector.memset(out_win[t][:].bitcast(I32), 0)
         su_ps = bank("su_ps", "b")
         sv_ps = bank("sv_ps", "b")
         for q in range(LANES):
@@ -114,12 +106,14 @@ def tile_attend_gclip_sg_u_pl_kernel(
         sgn_dealt = sgn[:].rearrange("s (p q r) -> s q p r", q=LANES, r=LANES)
         for q in range(LANES):
             nc.scalar.activation(
-                ys[:, q, :], y_sb[:, q, :], ACT.Identity,
+                ys[:, q, :].rearrange("p (r s) -> p s r", r=LANES),
+                y_sb[:, q, :].rearrange("p (s r) -> p s r", r=LANES),
+                ACT.Identity,
                 bias=su_col[:, q : q + 1], scale=su_m2[:, q : q + 1],
             )
             ys_ps = bank("ys_ps", "a")
             for r in range(LANES):
-                nc.tensor.transpose(ys_ps[:, r, :], ys[:, q, r:SLOTS:LANES], ident[:])
+                nc.tensor.transpose(ys_ps[:, r, :], ys[:, q, r * P : (r + 1) * P], ident[:])
             nc.vector.tensor_tensor(
                 sgn_dealt[:, q, :, :],
                 ys_ps[:].rearrange("s r i -> s i r"),
@@ -136,16 +130,18 @@ def tile_attend_gclip_sg_u_pl_kernel(
                 vd_in[:, :, :, t : t + 2],
                 v_got[:, t : t + 2, :].rearrange("p t (s r) -> p r s t", r=LANES),
             )
-        vt_in = sb("vt_in", [P, LANES, P, LANES], BF16)
+        vt_in = sb("vt_in", [P, LANES, P, LANES], BF16, "v_got")
+        vt_ps = [bank("vt_ps", "b") for half in range(2)]
+        for t in range(LANES):
+            pairs = v_got[:, t, :].bitcast(F32)
+            for u in range(2):
+                nc.tensor.transpose(
+                    vt_ps[t // 2][:, 2 * (t % 2) + u, :], pairs[:, u : SLOTS // 2 : 2], ident[:]
+                )
         for half in range(2):
-            vt_ps = bank("vt_ps", "b")
-            for tt in range(2):
-                pairs = v_got[:, 2 * half + tt, :].bitcast(F32)
-                for u in range(2):
-                    nc.tensor.transpose(vt_ps[:, 2 * tt + u, :], pairs[:, u : SLOTS // 2 : 2], ident[:])
             nc.scalar.copy(
                 vt_in[:, 2 * half : 2 * half + 2, :, :].bitcast(F32),
-                vt_ps[:].rearrange("s (tt u) p -> s tt p u", u=2),
+                vt_ps[half][:].rearrange("s (tt u) p -> s tt p u", u=2),
             )
         vd_codes = sb("vd_codes", [P, SLOTS], U32)
         vd_scales = sb("vd_scales", [P, SLOTS], U8)
@@ -182,8 +178,8 @@ def tile_attend_gclip_sg_u_pl_kernel(
         )
 
         zs = [sb("zs%d" % q, [P, SLOTS], F32) for q in range(LANES)]
-        sg = [sb("sg%d" % q, [P, SLOTS], F32) for q in range(LANES)]
-        g_in = [sb("g_in%d" % q, [P, SLOTS], BF16) for q in range(LANES)]
+        sg = sb("sg", [P, LANES * SLOTS], F32)
+        g_in = sb("g_in", [P, LANES * SLOTS], BF16)
 
         def score(q):
             a_ps = bank("a_ps", "a")
@@ -202,30 +198,26 @@ def tile_attend_gclip_sg_u_pl_kernel(
                 sgn[:, q * SLOTS : (q + 1) * SLOTS].rearrange("s (i r) -> s i r", r=LANES),
                 ALU.mult,
             )
-            nc.scalar.activation(sg[q][:], zs[q][:], ACT.Sigmoid)
+            nc.scalar.activation(sg[:, q * SLOTS : (q + 1) * SLOTS], zs[q][:], ACT.Sigmoid)
 
-        def grad(q):
-            parts = 2 if q == LANES - 1 else 1
-            width = SLOTS // parts
-            for lo in range(0, SLOTS, width):
-                nc.vector.tensor_tensor(
-                    g_in[q][:, lo : lo + width], sg[q][:, lo : lo + width],
-                    sgn[:, q * SLOTS + lo : q * SLOTS + lo + width], ALU.mult,
-                )
+        def grad(lo, hi):
+            nc.vector.tensor_tensor(g_in[:, lo:hi], sg[:, lo:hi], sgn[:, lo:hi], ALU.mult)
 
-        def quant(q):
-            cols = slice(HALF + q * P, HALF + (q + 1) * P)
+        def quant(lo, hi):
+            cols = slice(HALF + lo // LANES, HALF + hi // LANES)
             nc.vector.quantize_mx(
-                out=g_codes[:, cols].bitcast(E5M2), scales=g_scales[:, cols], in_=g_in[q][:]
+                out=g_codes[:, cols].bitcast(E5M2), scales=g_scales[:, cols], in_=g_in[:, lo:hi]
             )
 
-        for step in range(LANES + 2):
-            if step < LANES:
-                score(step)
-            if 1 <= step <= LANES:
-                grad(step - 1)
-            if step >= 2:
-                quant(step - 2)
+        for q in range(LANES):
+            score(q)
+        grad(0, 2 * SLOTS)
+        grad(2 * SLOTS, 3 * SLOTS)
+        quant(0, 2 * SLOTS)
+        grad(3 * SLOTS, 3 * SLOTS + HALF)
+        grad(3 * SLOTS + HALF, 4 * SLOTS)
+        quant(2 * SLOTS, 3 * SLOTS)
+        quant(3 * SLOTS, 4 * SLOTS)
 
         out_rows = out_0.rearrange("(p t) c -> t p c", t=LANES)
         pairs_in = sb("pairs_in", [P, 2 * TABLE], F32)
@@ -234,6 +226,9 @@ def tile_attend_gclip_sg_u_pl_kernel(
             first = (t // 2) * TABLE
             halves = pairs_in[:, first + lo : first + hi].bitcast(BF16)
             nc.scalar.copy(halves[:, t % 2 : 2 * (hi - lo) : 2], out_win[t][:, lo:hi])
+
+        HEAD = CHUNKS[0][1]
+        head_in = sb("head_in", [P, LANES * HEAD], BF16)
 
         def product(t, first):
             du_ps = bank("du_ps", "b")
@@ -249,7 +244,7 @@ def tile_attend_gclip_sg_u_pl_kernel(
             return flat
 
         du = [sb("du%d" % t, [P, SLOTS], F32) for t in range(LANES)]
-        early = sg[LANES - 1][:, 0:HALF]
+        early = sg[:, 3 * SLOTS : 3 * SLOTS + HALF]
         nc.scalar.copy(early, product(0, 0)[:, HALF:SLOTS])
         nc.scalar.copy(du[0][:, HALF:SLOTS], product(0, HALF)[:, HALF:SLOTS])
         for t in range(1, LANES):
@@ -263,19 +258,27 @@ def tile_attend_gclip_sg_u_pl_kernel(
             else:
                 nc.vector.tensor_copy(out_win[t][:].indirect(offs_sb[:]), du[t][:])
             nc.sync.dma_start(out=out_rows[t], in_=out_win[t][:])
+            copy = nc.scalar.copy if t < LANES - 1 else nc.vector.tensor_copy
+            copy(head_in[:, t * HEAD : (t + 1) * HEAD], out_win[t][:, 0:HEAD])
             if t < LANES - 1:
-                lane(t, 0, TABLE)
-        for lo, hi in CHUNKS:
+                lane(t, HEAD, TABLE)
+        for lo, hi in CHUNKS[1:ON_VECTOR] + [(CHUNKS[ON_VECTOR][0], TABLE)]:
             lane(LANES - 1, lo, hi)
 
         o_codes = sb("o_codes", [P, TABLE], U32)
         o_scales = sb("o_scales", [P, TABLE], U8)
         words_out = out_1[0].rearrange("p c l -> p (c l)").bitcast(I32)
-        spent = ["v_win0", "v_win1", "v_win2", "v_win3", "su_win", "sv_win"]
+        spent = ["v_win0", "v_win1", "v_win2", "v_win3", "u_win0", "u_win1"]
         o_in = [sb("o_in%d" % k, [P, hi - lo, LANES], BF16, spent[k]) for k, (lo, hi) in enumerate(CHUNKS)]
 
         def weave(k):
             lo, hi = CHUNKS[k]
+            if k == 0:
+                nc.vector.tensor_copy(
+                    o_in[0][:].rearrange("p (c i) t -> p c t i", i=4),
+                    head_in[:].rearrange("p (t c i) -> p c t i", t=LANES, i=4),
+                )
+                return
             copy = nc.vector.tensor_copy if k < ON_VECTOR else nc.scalar.copy
             copy(
                 o_in[k][:].bitcast(F32),

@@ -16,6 +16,7 @@ ALU = mybir.AluOpType
 
 P = 128
 LANES = 4
+BLOCKS = 4
 D = 512
 SLOTS = 512
 TABLE = 2048
@@ -41,88 +42,77 @@ def tile_attend_gclip_sg_u_pl_kernel(
         def bank(name, tag):
             return psum.tile([P, LANES, P], F32, name=name, tag=tag)
 
-        y_sb = sb("y_sb", [P, LANES, SLOTS], F32)
-        nc.sync.dma_start(out=y_sb[:], in_=y.rearrange("(p q) j -> p q j", q=LANES))
         offs_sb = keep.tile([P, SLOTS // 16], U16, name="offs_sb")
         qoffs_sb = keep.tile([P, SLOTS // 16], U16, name="qoffs_sb")
         nc.sync.dma_start(offs_sb[:], offs)
         nc.sync.dma_start(qoffs_sb[:], qoffs)
         su_win = sb("su_win", [P, TABLE], F32)
         sv_win = sb("sv_win", [P, TABLE], F32)
-        for win, src in ((su_win, su), (sv_win, sv)):
-            nc.scalar.dma_start(out=win[LIVE:P, :], in_=src[0:1, :])
+        for win, src in ((sv_win, sv), (su_win, su)):
+            nc.sync.dma_start(out=win[LIVE:P, :], in_=src[0:1, :])
         v_win = [sb("v_win%d" % t, [P, TABLE], F32) for t in range(LANES)]
         u_win = [sb("u_win%d" % t, [P, TABLE], F32) for t in range(LANES)]
         for wins, src in ((v_win, vT), (u_win, uT)):
             rows = src.rearrange("(p t) c -> t p c", t=LANES)
             for t in range(LANES):
                 nc.sync.dma_start(out=wins[t][:], in_=rows[t])
+        y_sb = [sb("y_sb%d" % b, [P, SLOTS], F32) for b in range(BLOCKS)]
+        for b in range(BLOCKS):
+            nc.sync.dma_start(out=y_sb[b][:], in_=y[b * P : (b + 1) * P, :])
 
         ident = sb("ident", [P, P], F32)
         make_identity(nc, ident[:])
-        for win in (su_win, sv_win):
-            nc.gpsimd.memset(win[0:LIVE, :], 0.0)
-        out_tags = ["out_win0", "out_win1", "su_win", "sv_win"]
-        out_win = [sb("out_win%d" % t, [P, TABLE], F32, out_tags[t]) for t in range(LANES)]
+        nc.gpsimd.memset(su_win[0:LIVE, :], 0.0)
         ODD = TABLE // 2 - 1
-        for t in range(2):
-            nc.vector.memset(out_win[t][:, 0:ODD], 0.0)
-            nc.vector.memset(out_win[t][:, ODD:TABLE], 0.0)
+        nc.vector.memset(sv_win[0:LIVE, 0:ODD], 0.0)
+        nc.vector.memset(sv_win[0:LIVE, ODD:TABLE], 0.0)
 
-        g_codes = sb("g_codes", [P, HALF + SLOTS], U32)
-        g_scales = sb("g_scales", [P, HALF + SLOTS], U8)
-        nc.vector.memset(g_codes[:, 0:HALF], 0)
-        nc.vector.memset(g_scales[:, 0:HALF].bitcast(U32), 0)
         warm = sb("warm", [P, 8], F32)
         nc.scalar.activation(warm[:, 0:1], ident[:, 0:1], ACT.Sigmoid)
         su_row = sb("su_row", [P, SLOTS], F32)
         sv_row = sb("sv_row", [P, SLOTS], F32)
         v_got = sb("v_got", [P, LANES, SLOTS], BF16)
-
-        def gather_v(t):
-            nc.vector.tensor_copy(v_got[:, t, :], v_win[t][:].indirect(qoffs_sb[:]))
-
-        nc.vector.tensor_copy(su_row[:], su_win[:].indirect(offs_sb[:]))
-        gather_v(0)
         nc.vector.tensor_copy(sv_row[:], sv_win[:].indirect(qoffs_sb[:]))
-        gather_v(1)
-        for t in (2, 3):
-            nc.vector.memset(out_win[t][:].bitcast(I32), 0)
+        nc.vector.tensor_copy(su_row[:], su_win[:].indirect(offs_sb[:]))
+        for t in range(LANES):
+            nc.vector.tensor_copy(v_got[:, t, :], v_win[t][:].indirect(qoffs_sb[:]))
         su_ps = bank("su_ps", "b")
         sv_ps = bank("sv_ps", "b")
-        for q in range(LANES):
-            nc.tensor.transpose(su_ps[:, q, :], su_row[:, q:SLOTS:LANES], ident[:])
         for r in range(LANES):
             nc.tensor.transpose(sv_ps[:, r, :], sv_row[:, r:SLOTS:LANES], ident[:])
-        su_col = sb("su_col", [P, LANES], F32)
-        su_m2 = sb("su_m2", [P, LANES], F32)
+        for b in range(BLOCKS):
+            nc.tensor.transpose(su_ps[:, b, :], su_row[:, b * P : (b + 1) * P], ident[:])
+        su_col = sb("su_col", [P, BLOCKS], F32)
         sv_col = sb("sv_col", [P, LANES], F32)
-        nc.scalar.copy(su_col[:], su_ps[:, :, LIVE])
-        nc.scalar.activation(su_m2[:], su_ps[:, :, LIVE], ACT.Copy, scale=-2.0)
         nc.scalar.copy(sv_col[:], sv_ps[:, :, LIVE])
+        nc.scalar.copy(su_col[:], su_ps[:, :, LIVE])
+        su_all = bank("su_all", "b")
+        sv_all_ps = bank("sv_all_ps", "b")
+        for b in range(BLOCKS):
+            nc.tensor.transpose(su_all[:, b, :], su_col[:, b : b + 1].to_broadcast([P, P]), ident[:])
+        for r in range(LANES):
+            nc.tensor.transpose(sv_all_ps[:, r, :], sv_col[:, r : r + 1].to_broadcast([P, P]), ident[:])
 
-        ys = sb("ys", [P, LANES, SLOTS], F32)
-        sgn = sb("sgn", [P, SLOTS * LANES], F32)
-        sgn_dealt = sgn[:].rearrange("s (p q r) -> s q p r", q=LANES, r=LANES)
-        for q in range(LANES):
-            nc.scalar.activation(
-                ys[:, q, :].rearrange("p (r s) -> p s r", r=LANES),
-                y_sb[:, q, :].rearrange("p (s r) -> p s r", r=LANES),
-                ACT.Identity,
-                bias=su_col[:, q : q + 1], scale=su_m2[:, q : q + 1],
-            )
-            ys_ps = bank("ys_ps", "a")
-            for r in range(LANES):
-                nc.tensor.transpose(ys_ps[:, r, :], ys[:, q, r * P : (r + 1) * P], ident[:])
+        sv_all = sb("sv_all", [P, SLOTS], F32)
+        nc.scalar.copy(sv_all[:], sv_all_ps[:].rearrange("p r s -> p (r s)"))
+        both = sb("both", [P, SLOTS, LANES], F32)
+
+        def both_scales(b):
             nc.vector.tensor_tensor(
-                sgn_dealt[:, q, :, :],
-                ys_ps[:].rearrange("s r i -> s i r"),
+                both[:, b * P : (b + 1) * P, :],
+                su_all[:, b, :].unsqueeze(2).to_broadcast([P, P, LANES]),
                 sv_col[:].unsqueeze(1).to_broadcast([P, P, LANES]),
                 ALU.mult,
             )
-            if q == 0:
-                gather_v(2)
-        gather_v(3)
+
+        for b in range(BLOCKS):
+            both_scales(b)
+        g_codes = sb("g_codes", [P, HALF + SLOTS], U32, "sv_row")
+        g_scales = sb("g_scales", [P, HALF + SLOTS], U8, "su_row")
+        zero = sb("zero", [P, SLOTS], F32, "v_win0")
+        nc.vector.memset(zero[:], 0.0)
+        nc.vector.memset(g_codes[:, 0:HALF], 0)
+        nc.vector.memset(g_scales[:, 0:HALF].bitcast(U32), 0)
 
         vd_in = sb("vd_in", [P, LANES, P, LANES], BF16, "staged")
         for t in (0, 2):
@@ -149,10 +139,10 @@ def tile_attend_gclip_sg_u_pl_kernel(
             out=vd_codes[:].bitcast(E4M3), scales=vd_scales[:],
             in_=vd_in[:].rearrange("p r s t -> p (r s t)"),
         )
-        u_in = sb("u_in", [P, SLOTS, LANES], BF16, "staged")
+        u_in = sb("u_in", [P, SLOTS, LANES], BF16)
         u_codes = sb("u_codes", [P, SLOTS], U32)
         u_scales = sb("u_scales", [P, SLOTS], U8)
-        u_got = sb("u_got", [P, 2, SLOTS], BF16)
+        u_got = sb("u_got", [P, 2, SLOTS], BF16, "sv_col")
         for t in range(2):
             nc.vector.tensor_copy(u_got[:, t, :], u_win[t][:].indirect(offs_sb[:]))
         nc.scalar.copy(u_in[:, :, 0:2], u_got[:].rearrange("p t i -> p i t"))
@@ -163,45 +153,60 @@ def tile_attend_gclip_sg_u_pl_kernel(
                 u_in[:, cols, LANES - 1],
                 u_win[LANES - 1][:].indirect(offs_sb[:, h * HALF // 16 : (h + 1) * HALF // 16]),
             )
-        for h in range(2):
-            cols = slice(h * HALF, (h + 1) * HALF)
             nc.vector.quantize_mx(
                 out=u_codes[:, cols].bitcast(E4M3), scales=u_scales[:, cols],
                 in_=u_in[:, cols, :].rearrange("p i t -> p (i t)"),
             )
 
-        vt_codes = sb("vt_codes", [P, D], U32, "staged")
+        vt_codes = sb("vt_codes", [P, D], U32)
         vt_scales = sb("vt_scales", [P, D], U8)
         nc.vector.quantize_mx(
             out=vt_codes[:].bitcast(E4M3), scales=vt_scales[:],
             in_=vt_in[:].rearrange("s t p r -> s (t p r)"),
         )
 
-        zs = [sb("zs%d" % q, [P, SLOTS], F32) for q in range(LANES)]
-        sg = sb("sg", [P, LANES * SLOTS], F32)
+        zs = [sb("zs%d" % b, [P, SLOTS], F32) for b in range(BLOCKS)]
+        sg = [sb("sg%d" % b, [P, SLOTS], F32) for b in range(BLOCKS)]
+        ny = [sb("ny%d" % b, [P, LANES, P], F32) for b in range(BLOCKS)]
         g_in = sb("g_in", [P, LANES * SLOTS], BF16)
+        a_ps = [bank("a_ps", "a") for b in range(BLOCKS)]
+        diff = [bank("diff", "a") for b in range(BLOCKS)]
 
-        def score(q):
-            a_ps = bank("a_ps", "a")
-            cols = slice(q * P, (q + 1) * P)
+        def turn(b, src, first):
             for r in range(LANES):
-                rc = slice(r * P, (r + 1) * P)
-                nc.tensor.matmul_mx(
-                    out=a_ps[:, r, :],
-                    lhsT=vd_codes[:, rc].bitcast(E4M3), lhsT_scale=vd_scales[:, rc],
-                    rhs=u_codes[:, cols].bitcast(E4M3), rhs_scale=u_scales[:, cols],
-                    start=True, stop=True,
+                nc.tensor.matmul(
+                    diff[b][:, r, :], lhsT=src[:, r * P : (r + 1) * P], rhs=ident[:], is_transpose=True,
+                    start=(first and r == 0), stop=(not first and r == LANES - 1),
                 )
+
+        def labels(b):
+            nc.scalar.activation(
+                ny[b][:].rearrange("p r s -> p s r"),
+                y_sb[b][:].rearrange("p (s r) -> p s r", r=LANES),
+                ACT.Copy, scale=-1.0,
+            )
+
+        def score(b):
+            cols = slice(b * P, (b + 1) * P)
+            flat = a_ps[b][:].rearrange("p a b -> p (a b)")
+            nc.tensor.matmul_mx(
+                out=flat,
+                lhsT=u_codes[:, cols].bitcast(E4M3), lhsT_scale=u_scales[:, cols],
+                rhs=vd_codes[:].bitcast(E4M3), rhs_scale=vd_scales[:],
+                start=True, stop=True,
+            )
+            nc.vector.tensor_tensor(zs[b][:], flat, sv_all[:], ALU.mult)
+            nc.scalar.activation(sg[b][:], zs[b][:], ACT.Sigmoid, scale=su_col[:, b : b + 1])
+
+        def grad(b):
+            turn(b, ny[b][:].rearrange("p r s -> p (r s)"), True)
+            turn(b, sg[b][:], False)
             nc.vector.tensor_tensor(
-                zs[q][:].rearrange("s (i r) -> s i r", r=LANES),
-                a_ps[:].rearrange("s r i -> s i r"),
-                sgn[:, q * SLOTS : (q + 1) * SLOTS].rearrange("s (i r) -> s i r", r=LANES),
+                g_in[:, b * SLOTS : (b + 1) * SLOTS].rearrange("s (i r) -> s i r", r=LANES),
+                diff[b][:].rearrange("s r i -> s i r"),
+                both[:, b * P : (b + 1) * P, :],
                 ALU.mult,
             )
-            nc.scalar.activation(sg[:, q * SLOTS : (q + 1) * SLOTS], zs[q][:], ACT.Sigmoid)
-
-        def grad(lo, hi):
-            nc.vector.tensor_tensor(g_in[:, lo:hi], sg[:, lo:hi], sgn[:, lo:hi], ALU.mult)
 
         def quant(lo, hi):
             cols = slice(HALF + lo // LANES, HALF + hi // LANES)
@@ -209,15 +214,18 @@ def tile_attend_gclip_sg_u_pl_kernel(
                 out=g_codes[:, cols].bitcast(E5M2), scales=g_scales[:, cols], in_=g_in[:, lo:hi]
             )
 
-        for q in range(LANES):
-            score(q)
-        grad(0, 2 * SLOTS)
-        grad(2 * SLOTS, 3 * SLOTS)
+        for b in range(BLOCKS):
+            labels(b)
+        for b in range(BLOCKS):
+            score(b)
+        grad(0)
+        grad(1)
+        grad(2)
         quant(0, 2 * SLOTS)
-        grad(3 * SLOTS, 3 * SLOTS + HALF)
-        grad(3 * SLOTS + HALF, 4 * SLOTS)
+        grad(3)
         quant(2 * SLOTS, 3 * SLOTS)
         quant(3 * SLOTS, 4 * SLOTS)
+
 
         out_rows = out_0.rearrange("(p t) c -> t p c", t=LANES)
         pairs_in = sb("pairs_in", [P, 2 * TABLE], F32)
@@ -244,19 +252,21 @@ def tile_attend_gclip_sg_u_pl_kernel(
             return flat
 
         du = [sb("du%d" % t, [P, SLOTS], F32) for t in range(LANES)]
-        early = sg[:, 3 * SLOTS : 3 * SLOTS + HALF]
+        out_tags = ["u_in", "g_in", "du0", "du1"]
+        out_win = []
+        early = du[0][:, 0:HALF]
         nc.scalar.copy(early, product(0, 0)[:, HALF:SLOTS])
         nc.scalar.copy(du[0][:, HALF:SLOTS], product(0, HALF)[:, HALF:SLOTS])
         for t in range(1, LANES):
             nc.scalar.copy(du[t][:], product(t, HALF))
         for t in range(LANES):
-            if t == 0:
-                nc.vector.tensor_copy(out_win[0][:].indirect(offs_sb[:, 0 : HALF // 16]), early)
-                nc.vector.tensor_copy(
-                    out_win[0][:].indirect(offs_sb[:, HALF // 16 : SLOTS // 16]), du[0][:, HALF:SLOTS]
+            out_win.append(sb("out_win%d" % t, [P, TABLE], F32, out_tags[t]))
+            nc.gpsimd.memset(out_win[t][:], 0.0)
+            for lo, hi in ((0, HALF), (HALF, SLOTS)) if t == 0 else ((0, SLOTS),):
+                nc.vector.tensor_tensor(
+                    out_win[t][:].indirect(offs_sb[:, lo // 16 : hi // 16]),
+                    du[t][:, lo:hi], zero[:, lo:hi], ALU.add,
                 )
-            else:
-                nc.vector.tensor_copy(out_win[t][:].indirect(offs_sb[:]), du[t][:])
             nc.sync.dma_start(out=out_rows[t], in_=out_win[t][:])
             copy = nc.scalar.copy if t < LANES - 1 else nc.vector.tensor_copy
             copy(head_in[:, t * HEAD : (t + 1) * HEAD], out_win[t][:, 0:HEAD])
@@ -268,7 +278,7 @@ def tile_attend_gclip_sg_u_pl_kernel(
         o_codes = sb("o_codes", [P, TABLE], U32)
         o_scales = sb("o_scales", [P, TABLE], U8)
         words_out = out_1[0].rearrange("p c l -> p (c l)").bitcast(I32)
-        spent = ["v_win0", "v_win1", "v_win2", "v_win3", "u_win0", "u_win1"]
+        spent = ["u_win2", "v_win1", "v_win2", "v_win3", "u_win0", "u_win1"]
         o_in = [sb("o_in%d" % k, [P, hi - lo, LANES], BF16, spent[k]) for k, (lo, hi) in enumerate(CHUNKS)]
 
         def weave(k):

@@ -24,8 +24,9 @@ LIVE = P - 1
 HALF = SLOTS // 2
 FLOPS = 2 * 2 * D * SLOTS * SLOTS
 BYTES = 4 * (3 * D * TABLE + SLOTS * SLOTS + 2 * TABLE) + D * TABLE + 16 * TABLE + 2 * 2 * P * 32
-CHUNKS = [(0, 256), (256, 768), (768, 1280), (1280, 1536), (1536, 1792), (1792, 2048)]
-ON_VECTOR = 3
+CHUNK = 256
+GROUP = 512
+RANGES = [(0, 512), (512, 1024), (1024, 1536), (1536, 1792), (1792, 2048)]
 
 
 def tile_attend_gclip_sg_u_pl_kernel(
@@ -56,9 +57,11 @@ def tile_attend_gclip_sg_u_pl_kernel(
             rows = src.rearrange("(p t) c -> t p c", t=LANES)
             for t in range(LANES):
                 nc.sync.dma_start(out=wins[t][:], in_=rows[t])
-        y_sb = [sb("y_sb%d" % b, [P, SLOTS], F32) for b in range(BLOCKS)]
-        for b in range(BLOCKS):
-            nc.sync.dma_start(out=y_sb[b][:], in_=y[b * P : (b + 1) * P, :])
+        y_sb = [sb("y_sb%d" % h, [P, 2, SLOTS], F32) for h in range(2)]
+        for h in range(2):
+            nc.sync.dma_start(
+                out=y_sb[h][:], in_=y[h * HALF : (h + 1) * HALF, :].rearrange("(b p) j -> p b j", p=P)
+            )
 
         ident = sb("ident", [P, P], F32)
         make_identity(nc, ident[:])
@@ -71,20 +74,32 @@ def tile_attend_gclip_sg_u_pl_kernel(
         nc.scalar.activation(warm[:, 0:1], ident[:, 0:1], ACT.Sigmoid)
         su_row = sb("su_row", [P, SLOTS], F32)
         sv_row = sb("sv_row", [P, SLOTS], F32)
-        v_got = sb("v_got", [P, LANES, SLOTS], BF16)
+        v_got = [sb("v_got0", [P, 2, SLOTS], BF16)]
+
+        def gather_v(t):
+            nc.vector.tensor_copy(v_got[t // 2][:, t % 2, :], v_win[t][:].indirect(qoffs_sb[:]))
+
         nc.vector.tensor_copy(sv_row[:], sv_win[:].indirect(qoffs_sb[:]))
         nc.vector.tensor_copy(su_row[:], su_win[:].indirect(offs_sb[:]))
-        for t in range(LANES):
-            nc.vector.tensor_copy(v_got[:, t, :], v_win[t][:].indirect(qoffs_sb[:]))
+        gather_v(0)
         su_ps = bank("su_ps", "b")
         sv_ps = bank("sv_ps", "b")
         for r in range(LANES):
             nc.tensor.transpose(sv_ps[:, r, :], sv_row[:, r:SLOTS:LANES], ident[:])
         for b in range(BLOCKS):
             nc.tensor.transpose(su_ps[:, b, :], su_row[:, b * P : (b + 1) * P], ident[:])
+        g_codes = sb("g_codes", [P, HALF + SLOTS], U32, "sv_row")
+        g_scales = sb("g_scales", [P, HALF + SLOTS], U8, "su_row")
+        zero = sb("zero", [P, SLOTS], F32, "v_win0")
+        nc.vector.memset(zero[:], 0.0)
+        nc.vector.memset(g_codes[:, 0:HALF], 0)
+        nc.vector.memset(g_scales[:, 0:HALF].bitcast(U32), 0)
+        gather_v(1)
         su_col = sb("su_col", [P, BLOCKS], F32)
-        sv_col = sb("sv_col", [P, LANES], F32)
-        nc.scalar.copy(sv_col[:], sv_ps[:, :, LIVE])
+        sv_cols = [sb("sv_col%d" % h, [P, LANES], F32) for h in range(2)]
+        sv_col = sv_cols[1]
+        for h in range(2):
+            nc.scalar.copy(sv_cols[h][:], sv_ps[:, :, LIVE])
         nc.scalar.copy(su_col[:], su_ps[:, :, LIVE])
         su_all = bank("su_all", "b")
         sv_all_ps = bank("sv_all_ps", "b")
@@ -101,29 +116,28 @@ def tile_attend_gclip_sg_u_pl_kernel(
             nc.vector.tensor_tensor(
                 both[:, b * P : (b + 1) * P, :],
                 su_all[:, b, :].unsqueeze(2).to_broadcast([P, P, LANES]),
-                sv_col[:].unsqueeze(1).to_broadcast([P, P, LANES]),
+                sv_cols[b // 2][:].unsqueeze(1).to_broadcast([P, P, LANES]),
                 ALU.mult,
             )
 
-        for b in range(BLOCKS):
-            both_scales(b)
-        g_codes = sb("g_codes", [P, HALF + SLOTS], U32, "sv_row")
-        g_scales = sb("g_scales", [P, HALF + SLOTS], U8, "su_row")
-        zero = sb("zero", [P, SLOTS], F32, "v_win0")
-        nc.vector.memset(zero[:], 0.0)
-        nc.vector.memset(g_codes[:, 0:HALF], 0)
-        nc.vector.memset(g_scales[:, 0:HALF].bitcast(U32), 0)
+        both_scales(0)
+        both_scales(1)
+        v_got.append(sb("v_got1", [P, 2, SLOTS], BF16, "sv_col0"))
+        gather_v(2)
+        gather_v(3)
+        both_scales(2)
+        both_scales(3)
 
         vd_in = sb("vd_in", [P, LANES, P, LANES], BF16, "staged")
         for t in (0, 2):
             nc.scalar.copy(
-                vd_in[:, :, :, t : t + 2],
-                v_got[:, t : t + 2, :].rearrange("p t (s r) -> p r s t", r=LANES),
+                vd_in[:, :, :, t : t + 2].rearrange("p r s t -> p s t r"),
+                v_got[t // 2][:].rearrange("p t (s r) -> p s t r", r=LANES),
             )
-        vt_in = sb("vt_in", [P, LANES, P, LANES], BF16, "v_got")
+        vt_in = sb("vt_in", [P, LANES, P, LANES], BF16)
         vt_ps = [bank("vt_ps", "b") for half in range(2)]
         for t in range(LANES):
-            pairs = v_got[:, t, :].bitcast(F32)
+            pairs = v_got[t // 2][:, t % 2, :].bitcast(F32)
             for u in range(2):
                 nc.tensor.transpose(
                     vt_ps[t // 2][:, 2 * (t % 2) + u, :], pairs[:, u : SLOTS // 2 : 2], ident[:]
@@ -139,26 +153,34 @@ def tile_attend_gclip_sg_u_pl_kernel(
             out=vd_codes[:].bitcast(E4M3), scales=vd_scales[:],
             in_=vd_in[:].rearrange("p r s t -> p (r s t)"),
         )
-        u_in = sb("u_in", [P, SLOTS, LANES], BF16)
+        u_in = [sb("u_in%d" % h, [P, HALF, LANES], BF16) for h in range(2)]
         u_codes = sb("u_codes", [P, SLOTS], U32)
         u_scales = sb("u_scales", [P, SLOTS], U8)
-        u_got = sb("u_got", [P, 2, SLOTS], BF16, "sv_col")
+        u_got = sb("u_got", [P, 2, SLOTS], BF16, "sv_col1")
         for t in range(2):
             nc.vector.tensor_copy(u_got[:, t, :], u_win[t][:].indirect(offs_sb[:]))
-        nc.scalar.copy(u_in[:, :, 0:2], u_got[:].rearrange("p t i -> p i t"))
-        nc.vector.tensor_copy(u_in[:, :, 2], u_win[2][:].indirect(offs_sb[:]))
-        for h in range(2):
-            cols = slice(h * HALF, (h + 1) * HALF)
+
+        def gather_u(t, h):
             nc.vector.tensor_copy(
-                u_in[:, cols, LANES - 1],
-                u_win[LANES - 1][:].indirect(offs_sb[:, h * HALF // 16 : (h + 1) * HALF // 16]),
-            )
-            nc.vector.quantize_mx(
-                out=u_codes[:, cols].bitcast(E4M3), scales=u_scales[:, cols],
-                in_=u_in[:, cols, :].rearrange("p i t -> p (i t)"),
+                u_in[h][:, :, t], u_win[t][:].indirect(offs_sb[:, h * HALF // 16 : (h + 1) * HALF // 16])
             )
 
-        vt_codes = sb("vt_codes", [P, D], U32)
+        for h in range(2):
+            cols = slice(h * HALF, (h + 1) * HALF)
+            nc.scalar.copy(
+                u_in[h][:, :, 0:2].rearrange("p (c i) t -> p c t i", i=4),
+                u_got[:, :, cols].rearrange("p t (c i) -> p c t i", i=4),
+            )
+            gather_u(2, h)
+        for h in range(2):
+            cols = slice(h * HALF, (h + 1) * HALF)
+            gather_u(3, h)
+            nc.vector.quantize_mx(
+                out=u_codes[:, cols].bitcast(E4M3), scales=u_scales[:, cols],
+                in_=u_in[h][:].rearrange("p i t -> p (i t)"),
+            )
+
+        vt_codes = sb("vt_codes", [P, D], U32, "u_in0")
         vt_scales = sb("vt_scales", [P, D], U8)
         nc.vector.quantize_mx(
             out=vt_codes[:].bitcast(E4M3), scales=vt_scales[:],
@@ -167,10 +189,10 @@ def tile_attend_gclip_sg_u_pl_kernel(
 
         zs = [sb("zs%d" % b, [P, SLOTS], F32) for b in range(BLOCKS)]
         sg = [sb("sg%d" % b, [P, SLOTS], F32) for b in range(BLOCKS)]
-        ny = [sb("ny%d" % b, [P, LANES, P], F32) for b in range(BLOCKS)]
+        ny = [sb("ny%d" % h, [P, 2, LANES, P], F32) for h in range(2)]
         g_in = sb("g_in", [P, LANES * SLOTS], BF16)
         a_ps = [bank("a_ps", "a") for b in range(BLOCKS)]
-        diff = [bank("diff", "a") for b in range(BLOCKS)]
+        diff = [bank("diff", "b") for b in range(BLOCKS)]
 
         def turn(b, src, first):
             for r in range(LANES):
@@ -179,12 +201,15 @@ def tile_attend_gclip_sg_u_pl_kernel(
                     start=(first and r == 0), stop=(not first and r == LANES - 1),
                 )
 
-        def labels(b):
+        def labels(h):
             nc.scalar.activation(
-                ny[b][:].rearrange("p r s -> p s r"),
-                y_sb[b][:].rearrange("p (s r) -> p s r", r=LANES),
+                ny[h][:].rearrange("p b r s -> p b s r"),
+                y_sb[h][:].rearrange("p b (s r) -> p b s r", r=LANES),
                 ACT.Copy, scale=-1.0,
             )
+
+        def turn_labels(b):
+            turn(b, ny[b // 2][:, b % 2].rearrange("p r s -> p (r s)"), True)
 
         def score(b):
             cols = slice(b * P, (b + 1) * P)
@@ -199,7 +224,6 @@ def tile_attend_gclip_sg_u_pl_kernel(
             nc.scalar.activation(sg[b][:], zs[b][:], ACT.Sigmoid, scale=su_col[:, b : b + 1])
 
         def grad(b):
-            turn(b, ny[b][:].rearrange("p r s -> p (r s)"), True)
             turn(b, sg[b][:], False)
             nc.vector.tensor_tensor(
                 g_in[:, b * SLOTS : (b + 1) * SLOTS].rearrange("s (i r) -> s i r", r=LANES),
@@ -214,32 +238,8 @@ def tile_attend_gclip_sg_u_pl_kernel(
                 out=g_codes[:, cols].bitcast(E5M2), scales=g_scales[:, cols], in_=g_in[:, lo:hi]
             )
 
-        for b in range(BLOCKS):
-            labels(b)
-        for b in range(BLOCKS):
-            score(b)
-        grad(0)
-        grad(1)
-        grad(2)
-        quant(0, 2 * SLOTS)
-        grad(3)
-        quant(2 * SLOTS, 3 * SLOTS)
-        quant(3 * SLOTS, 4 * SLOTS)
-
-
-        out_rows = out_0.rearrange("(p t) c -> t p c", t=LANES)
-        pairs_in = sb("pairs_in", [P, 2 * TABLE], F32)
-
-        def lane(t, lo, hi):
-            first = (t // 2) * TABLE
-            halves = pairs_in[:, first + lo : first + hi].bitcast(BF16)
-            nc.scalar.copy(halves[:, t % 2 : 2 * (hi - lo) : 2], out_win[t][:, lo:hi])
-
-        HEAD = CHUNKS[0][1]
-        head_in = sb("head_in", [P, LANES * HEAD], BF16)
-
         def product(t, first):
-            du_ps = bank("du_ps", "b")
+            du_ps = bank("du_ps", "a")
             flat = du_ps[:].rearrange("p a b -> p (a b)")
             tcols = slice(t * P, (t + 1) * P)
             nc.tensor.matmul_mx(
@@ -252,10 +252,36 @@ def tile_attend_gclip_sg_u_pl_kernel(
             return flat
 
         du = [sb("du%d" % t, [P, SLOTS], F32) for t in range(LANES)]
-        out_tags = ["u_in", "g_in", "du0", "du1"]
+        out_tags = ["u_in1", "g_in", "du0", "du1"]
         out_win = []
         early = du[0][:, 0:HALF]
+
+        labels(0)
+        labels(1)
+        for b in range(BLOCKS):
+            score(b)
+        turn_labels(0)
+        grad(0)
+        turn_labels(1)
+        grad(1)
+        quant(0, 2 * SLOTS)
         nc.scalar.copy(early, product(0, 0)[:, HALF:SLOTS])
+        turn_labels(2)
+        grad(2)
+        turn_labels(3)
+        grad(3)
+        quant(2 * SLOTS, 3 * SLOTS)
+        quant(3 * SLOTS, 4 * SLOTS)
+
+
+        out_rows = out_0.rearrange("(p t) c -> t p c", t=LANES)
+        pairs_in = sb("pairs_in", [P, 2 * TABLE], F32)
+
+        def lane(copy, t, lo, hi):
+            first = (t // 2) * TABLE
+            halves = pairs_in[:, first + lo : first + hi].bitcast(BF16)
+            copy(halves[:, t % 2 : 2 * (hi - lo) : 2], out_win[t][:, lo:hi])
+
         nc.scalar.copy(du[0][:, HALF:SLOTS], product(0, HALF)[:, HALF:SLOTS])
         for t in range(1, LANES):
             nc.scalar.copy(du[t][:], product(t, HALF))
@@ -268,51 +294,54 @@ def tile_attend_gclip_sg_u_pl_kernel(
                     du[t][:, lo:hi], zero[:, lo:hi], ALU.add,
                 )
             nc.sync.dma_start(out=out_rows[t], in_=out_win[t][:])
-            copy = nc.scalar.copy if t < LANES - 1 else nc.vector.tensor_copy
-            copy(head_in[:, t * HEAD : (t + 1) * HEAD], out_win[t][:, 0:HEAD])
-            if t < LANES - 1:
-                lane(t, HEAD, TABLE)
-        for lo, hi in CHUNKS[1:ON_VECTOR] + [(CHUNKS[ON_VECTOR][0], TABLE)]:
-            lane(LANES - 1, lo, hi)
+            if t < 2:
+                lane(nc.scalar.copy, t, 0, TABLE)
+            elif t == 2:
+                nc.scalar.copy(
+                    pairs_in[:, TABLE : TABLE + CHUNK].bitcast(BF16).rearrange("p (c e) -> p c e", e=2),
+                    out_win[t][:, 0:CHUNK].unsqueeze(2).to_broadcast([P, CHUNK, 2]),
+                )
+                lane(nc.scalar.copy, t, CHUNK, TABLE)
+        lane(nc.vector.tensor_copy, LANES - 1, 0, CHUNK)
+        lane(nc.scalar.copy, LANES - 1, CHUNK, GROUP)
+        for lo in range(GROUP, TABLE, GROUP):
+            lane(nc.scalar.copy, LANES - 1, lo, lo + GROUP)
 
         o_codes = sb("o_codes", [P, TABLE], U32)
-        o_scales = sb("o_scales", [P, TABLE], U8)
+        o_scales = sb("o_scales", [P, GROUP], U8)
         words_out = out_1[0].rearrange("p c l -> p (c l)").bitcast(I32)
-        spent = ["u_win2", "v_win1", "v_win2", "v_win3", "u_win0", "u_win1"]
-        o_in = [sb("o_in%d" % k, [P, hi - lo, LANES], BF16, spent[k]) for k, (lo, hi) in enumerate(CHUNKS)]
+        spent = ["u_win2", "v_win1", "v_win2", "v_win3", "u_win0"]
+        o_in = [sb("o_in%d" % k, [P, hi - lo, LANES], BF16, spent[k]) for k, (lo, hi) in enumerate(RANGES)]
 
-        def weave(k):
-            lo, hi = CHUNKS[k]
-            if k == 0:
-                nc.vector.tensor_copy(
-                    o_in[0][:].rearrange("p (c i) t -> p c t i", i=4),
-                    head_in[:].rearrange("p (t c i) -> p c t i", t=LANES, i=4),
-                )
-                return
-            copy = nc.vector.tensor_copy if k < ON_VECTOR else nc.scalar.copy
+        def weave(copy, k, lo, hi):
+            first = RANGES[k][0]
             copy(
-                o_in[k][:].bitcast(F32),
-                pairs_in[:].rearrange("p (u c) -> p c u", u=2)[:, lo:hi, :],
+                o_in[k][:, lo - first : hi - first, :].bitcast(F32).rearrange("p (c e) u -> p c u e", e=2),
+                pairs_in[:].rearrange("p (u c e) -> p c u e", u=2, e=2)[:, lo // 2 : hi // 2, :, :],
             )
 
         def finish(k):
-            lo, hi = CHUNKS[k]
+            lo, hi = RANGES[k]
+            group, at = divmod(lo, GROUP)
             nc.vector.quantize_mx(
-                out=o_codes[:, lo:hi].bitcast(E4M3), scales=o_scales[:, lo:hi],
+                out=o_codes[:, lo:hi].bitcast(E4M3),
+                scales=o_scales[4 * group : P, at : at + hi - lo],
                 in_=o_in[k][:].rearrange("p c t -> p (c t)"),
             )
             nc.sync.dma_start(out=words_out[:, lo:hi], in_=o_codes[:, lo:hi].bitcast(I32))
 
-        def store_scales(lo, hi, queues):
-            for quad in range(4):
-                queues[quad % 2].dma_start(
-                    out=out_2[0, 4 * quad : 4 * quad + 4, lo:hi].bitcast(I32),
-                    in_=o_scales[32 * quad : 32 * quad + 4, lo:hi].bitcast(I32),
-                )
-
-        for step in range(len(CHUNKS) + 1):
-            if step < len(CHUNKS):
-                weave(step)
-            if step >= 1:
-                finish(step - 1)
-        store_scales(0, TABLE, (nc.scalar, nc.sync))
+        weave(nc.vector.tensor_copy, 0, 0, CHUNK)
+        weave(nc.vector.tensor_copy, 0, CHUNK, GROUP)
+        weave(nc.vector.tensor_copy, 1, *RANGES[1])
+        finish(0)
+        weave(nc.vector.tensor_copy, 2, *RANGES[2])
+        finish(1)
+        finish(2)
+        for k in (3, 4):
+            weave(nc.scalar.copy, k, *RANGES[k])
+            finish(k)
+        for quad in range(4):
+            (nc.scalar, nc.sync)[quad % 2].dma_start(
+                out=out_2[0, 4 * quad : 4 * quad + 4, :].bitcast(I32).rearrange("r (a c) -> a r c", a=4),
+                in_=o_scales[32 * quad : 32 * quad + 16, :].bitcast(I32),
+            )

@@ -26,6 +26,7 @@ FLOPS = 2 * 2 * D * SLOTS * SLOTS
 BYTES = 4 * (3 * D * TABLE + SLOTS * SLOTS + 2 * TABLE) + D * TABLE + 16 * TABLE + 2 * 2 * P * 32
 CHUNK = 256
 GROUP = 512
+PLANE = 1024
 RANGES = [(0, 512), (512, 1024), (1024, 1536), (1536, 1792), (1792, 2048)]
 
 
@@ -57,11 +58,9 @@ def tile_attend_gclip_sg_u_pl_kernel(
             rows = src.rearrange("(p t) c -> t p c", t=LANES)
             for t in range(LANES):
                 nc.sync.dma_start(out=wins[t][:], in_=rows[t])
-        y_sb = [sb("y_sb%d" % h, [P, 2, SLOTS], F32) for h in range(2)]
-        for h in range(2):
-            nc.sync.dma_start(
-                out=y_sb[h][:], in_=y[h * HALF : (h + 1) * HALF, :].rearrange("(b p) j -> p b j", p=P)
-            )
+        y_sb = [sb("y_sb%d" % b, [P, SLOTS], F32) for b in range(BLOCKS)]
+        for b in range(BLOCKS):
+            nc.sync.dma_start(out=y_sb[b][:], in_=y[b * P : (b + 1) * P, :])
 
         ident = sb("ident", [P, P], F32)
         make_identity(nc, ident[:])
@@ -131,8 +130,8 @@ def tile_attend_gclip_sg_u_pl_kernel(
         vd_in = sb("vd_in", [P, LANES, P, LANES], BF16, "staged")
         for t in (0, 2):
             nc.scalar.copy(
-                vd_in[:, :, :, t : t + 2].rearrange("p r s t -> p s t r"),
-                v_got[t // 2][:].rearrange("p t (s r) -> p s t r", r=LANES),
+                vd_in[:, :, :, t : t + 2],
+                v_got[t // 2][:].rearrange("p t (s r) -> p r s t", r=LANES),
             )
         vt_in = sb("vt_in", [P, LANES, P, LANES], BF16)
         vt_ps = [bank("vt_ps", "b") for half in range(2)]
@@ -167,10 +166,7 @@ def tile_attend_gclip_sg_u_pl_kernel(
 
         for h in range(2):
             cols = slice(h * HALF, (h + 1) * HALF)
-            nc.scalar.copy(
-                u_in[h][:, :, 0:2].rearrange("p (c i) t -> p c t i", i=4),
-                u_got[:, :, cols].rearrange("p t (c i) -> p c t i", i=4),
-            )
+            nc.scalar.copy(u_in[h][:, :, 0:2], u_got[:, :, cols].rearrange("p t i -> p i t"))
             gather_u(2, h)
         for h in range(2):
             cols = slice(h * HALF, (h + 1) * HALF)
@@ -189,10 +185,10 @@ def tile_attend_gclip_sg_u_pl_kernel(
 
         zs = [sb("zs%d" % b, [P, SLOTS], F32) for b in range(BLOCKS)]
         sg = [sb("sg%d" % b, [P, SLOTS], F32) for b in range(BLOCKS)]
-        ny = [sb("ny%d" % h, [P, 2, LANES, P], F32) for h in range(2)]
+        ny = [sb("ny%d" % b, [P, LANES, P], F32) for b in range(BLOCKS)]
         g_in = sb("g_in", [P, LANES * SLOTS], BF16)
         a_ps = [bank("a_ps", "a") for b in range(BLOCKS)]
-        diff = [bank("diff", "b") for b in range(BLOCKS)]
+        diff = [bank("diff", "a") for b in range(BLOCKS)]
 
         def turn(b, src, first):
             for r in range(LANES):
@@ -201,15 +197,12 @@ def tile_attend_gclip_sg_u_pl_kernel(
                     start=(first and r == 0), stop=(not first and r == LANES - 1),
                 )
 
-        def labels(h):
+        def labels(b):
             nc.scalar.activation(
-                ny[h][:].rearrange("p b r s -> p b s r"),
-                y_sb[h][:].rearrange("p b (s r) -> p b s r", r=LANES),
+                ny[b][:].rearrange("p r s -> p s r"),
+                y_sb[b][:].rearrange("p (s r) -> p s r", r=LANES),
                 ACT.Copy, scale=-1.0,
             )
-
-        def turn_labels(b):
-            turn(b, ny[b // 2][:, b % 2].rearrange("p r s -> p (r s)"), True)
 
         def score(b):
             cols = slice(b * P, (b + 1) * P)
@@ -224,6 +217,7 @@ def tile_attend_gclip_sg_u_pl_kernel(
             nc.scalar.activation(sg[b][:], zs[b][:], ACT.Sigmoid, scale=su_col[:, b : b + 1])
 
         def grad(b):
+            turn(b, ny[b][:].rearrange("p r s -> p (r s)"), True)
             turn(b, sg[b][:], False)
             nc.vector.tensor_tensor(
                 g_in[:, b * SLOTS : (b + 1) * SLOTS].rearrange("s (i r) -> s i r", r=LANES),
@@ -239,7 +233,7 @@ def tile_attend_gclip_sg_u_pl_kernel(
             )
 
         def product(t, first):
-            du_ps = bank("du_ps", "a")
+            du_ps = bank("du_ps", "b")
             flat = du_ps[:].rearrange("p a b -> p (a b)")
             tcols = slice(t * P, (t + 1) * P)
             nc.tensor.matmul_mx(
@@ -256,20 +250,16 @@ def tile_attend_gclip_sg_u_pl_kernel(
         out_win = []
         early = du[0][:, 0:HALF]
 
-        labels(0)
-        labels(1)
+        for b in range(BLOCKS):
+            labels(b)
         for b in range(BLOCKS):
             score(b)
-        turn_labels(0)
         grad(0)
-        turn_labels(1)
         grad(1)
-        quant(0, 2 * SLOTS)
-        nc.scalar.copy(early, product(0, 0)[:, HALF:SLOTS])
-        turn_labels(2)
         grad(2)
-        turn_labels(3)
+        quant(0, 2 * SLOTS)
         grad(3)
+        nc.scalar.copy(early, product(0, 0)[:, HALF:SLOTS])
         quant(2 * SLOTS, 3 * SLOTS)
         quant(3 * SLOTS, 4 * SLOTS)
 
@@ -308,7 +298,7 @@ def tile_attend_gclip_sg_u_pl_kernel(
             lane(nc.scalar.copy, LANES - 1, lo, lo + GROUP)
 
         o_codes = sb("o_codes", [P, TABLE], U32)
-        o_scales = sb("o_scales", [P, GROUP], U8)
+        o_scales = sb("o_scales", [P, PLANE], U8)
         words_out = out_1[0].rearrange("p c l -> p (c l)").bitcast(I32)
         spent = ["u_win2", "v_win1", "v_win2", "v_win3", "u_win0"]
         o_in = [sb("o_in%d" % k, [P, hi - lo, LANES], BF16, spent[k]) for k, (lo, hi) in enumerate(RANGES)]
@@ -322,7 +312,7 @@ def tile_attend_gclip_sg_u_pl_kernel(
 
         def finish(k):
             lo, hi = RANGES[k]
-            group, at = divmod(lo, GROUP)
+            group, at = divmod(lo, PLANE)
             nc.vector.quantize_mx(
                 out=o_codes[:, lo:hi].bitcast(E4M3),
                 scales=o_scales[4 * group : P, at : at + hi - lo],
@@ -342,6 +332,6 @@ def tile_attend_gclip_sg_u_pl_kernel(
             finish(k)
         for quad in range(4):
             (nc.scalar, nc.sync)[quad % 2].dma_start(
-                out=out_2[0, 4 * quad : 4 * quad + 4, :].bitcast(I32).rearrange("r (a c) -> a r c", a=4),
-                in_=o_scales[32 * quad : 32 * quad + 16, :].bitcast(I32),
+                out=out_2[0, 4 * quad : 4 * quad + 4, :].bitcast(I32).rearrange("r (a c) -> a r c", a=2),
+                in_=o_scales[32 * quad : 32 * quad + 8, :].bitcast(I32),
             )

@@ -20,14 +20,18 @@ BLOCKS = 4
 D = 512
 SLOTS = 512
 TABLE = 2048
-LIVE = P - 1
 HALF = SLOTS // 2
+PER_COLUMN = 16
+LIVE = P - 1
+ODD = TABLE // 2 - 1
 FLOPS = 2 * 2 * D * SLOTS * SLOTS
 BYTES = 4 * (3 * D * TABLE + SLOTS * SLOTS + 2 * TABLE) + D * TABLE + 16 * TABLE + 2 * 2 * P * 32
-CHUNK = 256
-GROUP = 512
-PLANE = 1024
+
 RANGES = [(0, 512), (512, 1024), (1024, 1536), (1536, 1792), (1792, 2048)]
+ON_VECTOR = 3
+FIRST = 256
+STEP = 512
+PLANE = 1024
 
 
 def tile_attend_gclip_sg_u_pl_kernel(
@@ -36,21 +40,24 @@ def tile_attend_gclip_sg_u_pl_kernel(
     nc = tc.nc
     with ExitStack() as ctx:
         keep = ctx.enter_context(tc.tile_pool(name="keep", bufs=1))
-        psum = ctx.enter_context(tc.psum_pool(name="psum", bufs=4))
+        psum = ctx.enter_context(tc.psum_pool(name="psum", bufs=1))
 
-        def sb(name, shape, dtype, tag=None):
-            return keep.tile(shape, dtype, name=name, tag=tag or name, align_bytes=64)
+        def sb(name, shape, dtype, reuses=None):
+            return keep.tile(shape, dtype, name=name, tag=reuses or name, align_bytes=64)
 
-        def bank(name, tag):
-            return psum.tile([P, LANES, P], F32, name=name, tag=tag)
+        def bank(name, number):
+            return psum.tile([P, LANES, P], F32, name=name, tag="bank%d" % number)
 
-        offs_sb = keep.tile([P, SLOTS // 16], U16, name="offs_sb")
-        qoffs_sb = keep.tile([P, SLOTS // 16], U16, name="qoffs_sb")
+        def entries(lst, lo, hi):
+            return lst[:, lo // PER_COLUMN : hi // PER_COLUMN]
+
+        offs_sb = keep.tile([P, SLOTS // PER_COLUMN], U16, name="offs_sb")
+        qoffs_sb = keep.tile([P, SLOTS // PER_COLUMN], U16, name="qoffs_sb")
         nc.sync.dma_start(offs_sb[:], offs)
         nc.sync.dma_start(qoffs_sb[:], qoffs)
         su_win = sb("su_win", [P, TABLE], F32)
         sv_win = sb("sv_win", [P, TABLE], F32)
-        for win, src in ((sv_win, sv), (su_win, su)):
+        for win, src in ((su_win, su), (sv_win, sv)):
             nc.sync.dma_start(out=win[LIVE:P, :], in_=src[0:1, :])
         v_win = [sb("v_win%d" % t, [P, TABLE], F32) for t in range(LANES)]
         u_win = [sb("u_win%d" % t, [P, TABLE], F32) for t in range(LANES)]
@@ -64,13 +71,13 @@ def tile_attend_gclip_sg_u_pl_kernel(
 
         ident = sb("ident", [P, P], F32)
         make_identity(nc, ident[:])
-        nc.gpsimd.memset(su_win[0:LIVE, :], 0.0)
-        ODD = TABLE // 2 - 1
-        nc.vector.memset(sv_win[0:LIVE, 0:ODD], 0.0)
-        nc.vector.memset(sv_win[0:LIVE, ODD:TABLE], 0.0)
+        nc.gpsimd.memset(sv_win[0:LIVE, :], 0.0)
+        nc.vector.memset(su_win[0:LIVE, 0:ODD], 0.0)
+        nc.vector.memset(su_win[0:LIVE, ODD:TABLE], 0.0)
 
         warm = sb("warm", [P, 8], F32)
         nc.scalar.activation(warm[:, 0:1], ident[:, 0:1], ACT.Sigmoid)
+
         su_row = sb("su_row", [P, SLOTS], F32)
         sv_row = sb("sv_row", [P, SLOTS], F32)
         v_got = [sb("v_got0", [P, 2, SLOTS], BF16)]
@@ -78,15 +85,27 @@ def tile_attend_gclip_sg_u_pl_kernel(
         def gather_v(t):
             nc.vector.tensor_copy(v_got[t // 2][:, t % 2, :], v_win[t][:].indirect(qoffs_sb[:]))
 
-        nc.vector.tensor_copy(sv_row[:], sv_win[:].indirect(qoffs_sb[:]))
         nc.vector.tensor_copy(su_row[:], su_win[:].indirect(offs_sb[:]))
+        nc.vector.tensor_copy(sv_row[:], sv_win[:].indirect(qoffs_sb[:]))
         gather_v(0)
-        su_ps = bank("su_ps", "b")
-        sv_ps = bank("sv_ps", "b")
-        for r in range(LANES):
-            nc.tensor.transpose(sv_ps[:, r, :], sv_row[:, r:SLOTS:LANES], ident[:])
+        su_ps = bank("su_ps", 1)
+        sv_ps = bank("sv_ps", 0)
+        su_all = bank("su_all", 2)
+        sv_all_ps = bank("sv_all_ps", 3)
+        su_col = sb("su_col", [P, BLOCKS], F32)
+        sv_cols = [sb("sv_col%d" % h, [P, LANES], F32) for h in range(2)]
         for b in range(BLOCKS):
             nc.tensor.transpose(su_ps[:, b, :], su_row[:, b * P : (b + 1) * P], ident[:])
+        nc.scalar.copy(su_col[:], su_ps[:, :, LIVE])
+        for r in range(LANES):
+            nc.tensor.transpose(sv_ps[:, r, :], sv_row[:, r:SLOTS:LANES], ident[:])
+        for h in range(2):
+            nc.scalar.copy(sv_cols[h][:], sv_ps[:, :, LIVE])
+        for b in range(BLOCKS):
+            nc.tensor.transpose(su_all[:, b, :], su_col[:, b : b + 1].to_broadcast([P, P]), ident[:])
+        for r in range(LANES):
+            nc.tensor.transpose(sv_all_ps[:, r, :], sv_cols[1][:, r : r + 1].to_broadcast([P, P]), ident[:])
+
         g_codes = sb("g_codes", [P, HALF + SLOTS], U32, "sv_row")
         g_scales = sb("g_scales", [P, HALF + SLOTS], U8, "su_row")
         zero = sb("zero", [P, SLOTS], F32, "v_win0")
@@ -94,18 +113,6 @@ def tile_attend_gclip_sg_u_pl_kernel(
         nc.vector.memset(g_codes[:, 0:HALF], 0)
         nc.vector.memset(g_scales[:, 0:HALF].bitcast(U32), 0)
         gather_v(1)
-        su_col = sb("su_col", [P, BLOCKS], F32)
-        sv_cols = [sb("sv_col%d" % h, [P, LANES], F32) for h in range(2)]
-        sv_col = sv_cols[1]
-        for h in range(2):
-            nc.scalar.copy(sv_cols[h][:], sv_ps[:, :, LIVE])
-        nc.scalar.copy(su_col[:], su_ps[:, :, LIVE])
-        su_all = bank("su_all", "b")
-        sv_all_ps = bank("sv_all_ps", "b")
-        for b in range(BLOCKS):
-            nc.tensor.transpose(su_all[:, b, :], su_col[:, b : b + 1].to_broadcast([P, P]), ident[:])
-        for r in range(LANES):
-            nc.tensor.transpose(sv_all_ps[:, r, :], sv_col[:, r : r + 1].to_broadcast([P, P]), ident[:])
 
         sv_all = sb("sv_all", [P, SLOTS], F32)
         nc.scalar.copy(sv_all[:], sv_all_ps[:].rearrange("p r s -> p (r s)"))
@@ -127,41 +134,42 @@ def tile_attend_gclip_sg_u_pl_kernel(
         both_scales(2)
         both_scales(3)
 
-        vd_in = sb("vd_in", [P, LANES, P, LANES], BF16, "staged")
+        vd_in = sb("vd_in", [P, LANES, P, LANES], BF16)
         for t in (0, 2):
             nc.scalar.copy(
                 vd_in[:, :, :, t : t + 2],
                 v_got[t // 2][:].rearrange("p t (s r) -> p r s t", r=LANES),
             )
         vt_in = sb("vt_in", [P, LANES, P, LANES], BF16)
-        vt_ps = [bank("vt_ps", "b") for half in range(2)]
+        vt_ps = [bank("vt_ps", (3, 0)[half]) for half in range(2)]
         for t in range(LANES):
-            pairs = v_got[t // 2][:, t % 2, :].bitcast(F32)
+            words = v_got[t // 2][:, t % 2, :].bitcast(F32)
             for u in range(2):
                 nc.tensor.transpose(
-                    vt_ps[t // 2][:, 2 * (t % 2) + u, :], pairs[:, u : SLOTS // 2 : 2], ident[:]
+                    vt_ps[t // 2][:, 2 * (t % 2) + u, :], words[:, u : SLOTS // 2 : 2], ident[:]
                 )
         for half in range(2):
             nc.scalar.copy(
                 vt_in[:, 2 * half : 2 * half + 2, :, :].bitcast(F32),
                 vt_ps[half][:].rearrange("s (tt u) p -> s tt p u", u=2),
             )
-        vd_codes = sb("vd_codes", [P, SLOTS], U32)
+
+        u_got = sb("u_got", [P, 2, SLOTS], BF16, "sv_col1")
+        for t in range(2):
+            nc.vector.tensor_copy(u_got[:, t, :], u_win[t][:].indirect(offs_sb[:]))
+        vd_codes = sb("vd_codes", [P, SLOTS], U32, "u_win1")
         vd_scales = sb("vd_scales", [P, SLOTS], U8)
         nc.vector.quantize_mx(
             out=vd_codes[:].bitcast(E4M3), scales=vd_scales[:],
             in_=vd_in[:].rearrange("p r s t -> p (r s t)"),
         )
-        u_in = [sb("u_in%d" % h, [P, HALF, LANES], BF16) for h in range(2)]
+        u_in = [sb("u_in%d" % h, [P, HALF, LANES], BF16, ("sv_col0", "u_in1")[h]) for h in range(2)]
         u_codes = sb("u_codes", [P, SLOTS], U32)
         u_scales = sb("u_scales", [P, SLOTS], U8)
-        u_got = sb("u_got", [P, 2, SLOTS], BF16, "sv_col1")
-        for t in range(2):
-            nc.vector.tensor_copy(u_got[:, t, :], u_win[t][:].indirect(offs_sb[:]))
 
         def gather_u(t, h):
             nc.vector.tensor_copy(
-                u_in[h][:, :, t], u_win[t][:].indirect(offs_sb[:, h * HALF // 16 : (h + 1) * HALF // 16])
+                u_in[h][:, :, t], u_win[t][:].indirect(entries(offs_sb, h * HALF, (h + 1) * HALF))
             )
 
         for h in range(2):
@@ -176,19 +184,19 @@ def tile_attend_gclip_sg_u_pl_kernel(
                 in_=u_in[h][:].rearrange("p i t -> p (i t)"),
             )
 
-        vt_codes = sb("vt_codes", [P, D], U32, "u_in0")
+        vt_codes = sb("vt_codes", [P, D], U32, "sv_col0")
         vt_scales = sb("vt_scales", [P, D], U8)
         nc.vector.quantize_mx(
             out=vt_codes[:].bitcast(E4M3), scales=vt_scales[:],
             in_=vt_in[:].rearrange("s t p r -> s (t p r)"),
         )
 
-        zs = [sb("zs%d" % b, [P, SLOTS], F32) for b in range(BLOCKS)]
-        sg = [sb("sg%d" % b, [P, SLOTS], F32) for b in range(BLOCKS)]
-        ny = [sb("ny%d" % b, [P, LANES, P], F32) for b in range(BLOCKS)]
+        a_sv = [sb("a_sv%d" % b, [P, SLOTS], F32) for b in range(BLOCKS)]
+        sig = [sb("sig%d" % b, [P, SLOTS], F32) for b in range(BLOCKS)]
+        neg_y = [sb("neg_y%d" % b, [P, LANES, P], F32) for b in range(BLOCKS)]
         g_in = sb("g_in", [P, LANES * SLOTS], BF16)
-        a_ps = [bank("a_ps", "a") for b in range(BLOCKS)]
-        diff = [bank("diff", "a") for b in range(BLOCKS)]
+        a_ps = [bank("a_ps", 4 + b) for b in range(BLOCKS)]
+        diff = [bank("diff", 4 + b) for b in range(BLOCKS)]
 
         def turn(b, src, first):
             for r in range(LANES):
@@ -199,26 +207,26 @@ def tile_attend_gclip_sg_u_pl_kernel(
 
         def labels(b):
             nc.scalar.activation(
-                ny[b][:].rearrange("p r s -> p s r"),
+                neg_y[b][:].rearrange("p r s -> p s r"),
                 y_sb[b][:].rearrange("p (s r) -> p s r", r=LANES),
                 ACT.Copy, scale=-1.0,
             )
 
         def score(b):
             cols = slice(b * P, (b + 1) * P)
-            flat = a_ps[b][:].rearrange("p a b -> p (a b)")
+            flat = a_ps[b][:].rearrange("p r s -> p (r s)")
             nc.tensor.matmul_mx(
                 out=flat,
                 lhsT=u_codes[:, cols].bitcast(E4M3), lhsT_scale=u_scales[:, cols],
                 rhs=vd_codes[:].bitcast(E4M3), rhs_scale=vd_scales[:],
                 start=True, stop=True,
             )
-            nc.vector.tensor_tensor(zs[b][:], flat, sv_all[:], ALU.mult)
-            nc.scalar.activation(sg[b][:], zs[b][:], ACT.Sigmoid, scale=su_col[:, b : b + 1])
+            nc.vector.tensor_tensor(a_sv[b][:], flat, sv_all[:], ALU.mult)
+            nc.scalar.activation(sig[b][:], a_sv[b][:], ACT.Sigmoid, scale=su_col[:, b : b + 1])
 
         def grad(b):
-            turn(b, ny[b][:].rearrange("p r s -> p (r s)"), True)
-            turn(b, sg[b][:], False)
+            turn(b, neg_y[b][:].rearrange("p r s -> p (r s)"), True)
+            turn(b, sig[b][:], False)
             nc.vector.tensor_tensor(
                 g_in[:, b * SLOTS : (b + 1) * SLOTS].rearrange("s (i r) -> s i r", r=LANES),
                 diff[b][:].rearrange("s r i -> s i r"),
@@ -226,15 +234,15 @@ def tile_attend_gclip_sg_u_pl_kernel(
                 ALU.mult,
             )
 
-        def quant(lo, hi):
-            cols = slice(HALF + lo // LANES, HALF + hi // LANES)
+        def quantise_g(lo, hi):
+            cols = slice(HALF + lo, HALF + hi)
             nc.vector.quantize_mx(
-                out=g_codes[:, cols].bitcast(E5M2), scales=g_scales[:, cols], in_=g_in[:, lo:hi]
+                out=g_codes[:, cols].bitcast(E5M2), scales=g_scales[:, cols],
+                in_=g_in[:, LANES * lo : LANES * hi],
             )
 
-        def product(t, first):
-            du_ps = bank("du_ps", "b")
-            flat = du_ps[:].rearrange("p a b -> p (a b)")
+        def product(t, first, number):
+            flat = bank("du_ps", number)[:].rearrange("p a b -> p (a b)")
             tcols = slice(t * P, (t + 1) * P)
             nc.tensor.matmul_mx(
                 out=flat,
@@ -246,10 +254,6 @@ def tile_attend_gclip_sg_u_pl_kernel(
             return flat
 
         du = [sb("du%d" % t, [P, SLOTS], F32) for t in range(LANES)]
-        out_tags = ["u_in1", "g_in", "du0", "du1"]
-        out_win = []
-        early = du[0][:, 0:HALF]
-
         for b in range(BLOCKS):
             labels(b)
         for b in range(BLOCKS):
@@ -257,45 +261,45 @@ def tile_attend_gclip_sg_u_pl_kernel(
         grad(0)
         grad(1)
         grad(2)
-        quant(0, 2 * SLOTS)
+        quantise_g(0, HALF)
         grad(3)
-        nc.scalar.copy(early, product(0, 0)[:, HALF:SLOTS])
-        quant(2 * SLOTS, 3 * SLOTS)
-        quant(3 * SLOTS, 4 * SLOTS)
-
+        nc.scalar.copy(du[0][:, 0:HALF], product(0, 0, 0)[:, HALF:SLOTS])
+        quantise_g(HALF, HALF + P)
+        quantise_g(HALF + P, SLOTS)
 
         out_rows = out_0.rearrange("(p t) c -> t p c", t=LANES)
-        pairs_in = sb("pairs_in", [P, 2 * TABLE], F32)
+        pairs = sb("pairs", [P, 2 * TABLE], F32)
 
-        def lane(copy, t, lo, hi):
+        def round_lane(copy, t, lo, hi):
             first = (t // 2) * TABLE
-            halves = pairs_in[:, first + lo : first + hi].bitcast(BF16)
+            halves = pairs[:, first + lo : first + hi].bitcast(BF16)
             copy(halves[:, t % 2 : 2 * (hi - lo) : 2], out_win[t][:, lo:hi])
 
-        nc.scalar.copy(du[0][:, HALF:SLOTS], product(0, HALF)[:, HALF:SLOTS])
+        nc.scalar.copy(du[0][:, HALF:SLOTS], product(0, HALF, 1)[:, HALF:SLOTS])
         for t in range(1, LANES):
-            nc.scalar.copy(du[t][:], product(t, HALF))
+            nc.scalar.copy(du[t][:], product(t, HALF, (t + 1) % LANES))
+        out_reuses = ["u_in1", "g_in", "du0", "du1"]
+        out_win = []
         for t in range(LANES):
-            out_win.append(sb("out_win%d" % t, [P, TABLE], F32, out_tags[t]))
+            out_win.append(sb("out_win%d" % t, [P, TABLE], F32, out_reuses[t]))
             nc.gpsimd.memset(out_win[t][:], 0.0)
             for lo, hi in ((0, HALF), (HALF, SLOTS)) if t == 0 else ((0, SLOTS),):
                 nc.vector.tensor_tensor(
-                    out_win[t][:].indirect(offs_sb[:, lo // 16 : hi // 16]),
-                    du[t][:, lo:hi], zero[:, lo:hi], ALU.add,
+                    out_win[t][:].indirect(entries(offs_sb, lo, hi)), du[t][:, lo:hi], zero[:, lo:hi], ALU.add
                 )
             nc.sync.dma_start(out=out_rows[t], in_=out_win[t][:])
             if t < 2:
-                lane(nc.scalar.copy, t, 0, TABLE)
+                round_lane(nc.scalar.copy, t, 0, TABLE)
             elif t == 2:
                 nc.scalar.copy(
-                    pairs_in[:, TABLE : TABLE + CHUNK].bitcast(BF16).rearrange("p (c e) -> p c e", e=2),
-                    out_win[t][:, 0:CHUNK].unsqueeze(2).to_broadcast([P, CHUNK, 2]),
+                    pairs[:, TABLE : TABLE + FIRST].bitcast(BF16).rearrange("p (c e) -> p c e", e=2),
+                    out_win[t][:, 0:FIRST].unsqueeze(2).to_broadcast([P, FIRST, 2]),
                 )
-                lane(nc.scalar.copy, t, CHUNK, TABLE)
-        lane(nc.vector.tensor_copy, LANES - 1, 0, CHUNK)
-        lane(nc.scalar.copy, LANES - 1, CHUNK, GROUP)
-        for lo in range(GROUP, TABLE, GROUP):
-            lane(nc.scalar.copy, LANES - 1, lo, lo + GROUP)
+                round_lane(nc.scalar.copy, t, FIRST, TABLE)
+        round_lane(nc.vector.tensor_copy, LANES - 1, 0, FIRST)
+        round_lane(nc.scalar.copy, LANES - 1, FIRST, STEP)
+        for lo in range(STEP, TABLE, STEP):
+            round_lane(nc.scalar.copy, LANES - 1, lo, lo + STEP)
 
         o_codes = sb("o_codes", [P, TABLE], U32)
         o_scales = sb("o_scales", [P, PLANE], U8)
@@ -307,31 +311,30 @@ def tile_attend_gclip_sg_u_pl_kernel(
             first = RANGES[k][0]
             copy(
                 o_in[k][:, lo - first : hi - first, :].bitcast(F32).rearrange("p (c e) u -> p c u e", e=2),
-                pairs_in[:].rearrange("p (u c e) -> p c u e", u=2, e=2)[:, lo // 2 : hi // 2, :, :],
+                pairs[:].rearrange("p (u c e) -> p c u e", u=2, e=2)[:, lo // 2 : hi // 2, :, :],
             )
 
         def finish(k):
             lo, hi = RANGES[k]
-            group, at = divmod(lo, PLANE)
+            plane, at = divmod(lo, PLANE)
             nc.vector.quantize_mx(
                 out=o_codes[:, lo:hi].bitcast(E4M3),
-                scales=o_scales[4 * group : P, at : at + hi - lo],
+                scales=o_scales[4 * plane : P, at : at + hi - lo],
                 in_=o_in[k][:].rearrange("p c t -> p (c t)"),
             )
             nc.sync.dma_start(out=words_out[:, lo:hi], in_=o_codes[:, lo:hi].bitcast(I32))
 
-        weave(nc.vector.tensor_copy, 0, 0, CHUNK)
-        weave(nc.vector.tensor_copy, 0, CHUNK, GROUP)
-        weave(nc.vector.tensor_copy, 1, *RANGES[1])
-        finish(0)
-        weave(nc.vector.tensor_copy, 2, *RANGES[2])
-        finish(1)
-        finish(2)
-        for k in (3, 4):
+        weave(nc.vector.tensor_copy, 0, 0, FIRST)
+        weave(nc.vector.tensor_copy, 0, FIRST, RANGES[0][1])
+        for k in range(1, ON_VECTOR):
+            weave(nc.vector.tensor_copy, k, *RANGES[k])
+            finish(k - 1)
+        finish(ON_VECTOR - 1)
+        for k in range(ON_VECTOR, len(RANGES)):
             weave(nc.scalar.copy, k, *RANGES[k])
             finish(k)
-        for quad in range(4):
-            (nc.scalar, nc.sync)[quad % 2].dma_start(
-                out=out_2[0, 4 * quad : 4 * quad + 4, :].bitcast(I32).rearrange("r (a c) -> a r c", a=2),
-                in_=o_scales[32 * quad : 32 * quad + 8, :].bitcast(I32),
+        for q in range(4):
+            (nc.scalar, nc.sync)[q % 2].dma_start(
+                out=out_2[0, 4 * q : 4 * q + 4, :].bitcast(I32).rearrange("r (a c) -> a r c", a=TABLE // PLANE),
+                in_=o_scales[32 * q : 32 * q + 4 * (TABLE // PLANE), :].bitcast(I32),
             )

@@ -27,10 +27,7 @@ ODD = TABLE // 2 - 1
 FLOPS = 2 * 2 * D * SLOTS * SLOTS
 BYTES = 4 * (3 * D * TABLE + SLOTS * SLOTS + 2 * TABLE) + D * TABLE + 16 * TABLE + 2 * 2 * P * 32
 
-RANGES = [(0, 512), (512, 1024), (1024, 1536), (1536, 1792), (1792, 2048)]
-ON_VECTOR = 3
-FIRST = 256
-STEP = 512
+SPLIT = 1152
 PLANE = 1024
 
 
@@ -106,13 +103,12 @@ def tile_attend_gclip_sg_u_pl_kernel(
         for r in range(LANES):
             nc.tensor.transpose(sv_all_ps[:, r, :], sv_cols[1][:, r : r + 1].to_broadcast([P, P]), ident[:])
 
-        g_codes = sb("g_codes", [P, HALF + SLOTS], U32, "sv_row")
-        g_scales = sb("g_scales", [P, HALF + SLOTS], U8, "su_row")
-        zero = sb("zero", [P, SLOTS], F32, "v_win0")
-        nc.vector.memset(zero[:], 0.0)
-        nc.vector.memset(g_codes[:, 0:HALF], 0)
-        nc.vector.memset(g_scales[:, 0:HALF].bitcast(U32), 0)
+        out_win = []
+        for t, spent in enumerate(("su_win", "sv_win", "v_win0", "v_win1")):
+            out_win.append(sb("out_win%d" % t, [P, TABLE], F32, spent))
         gather_v(1)
+        for t in range(LANES):
+            nc.gpsimd.memset(out_win[t][:], 0.0)
 
         sv_all = sb("sv_all", [P, SLOTS], F32)
         nc.scalar.copy(sv_all[:], sv_all_ps[:].rearrange("p r s -> p (r s)"))
@@ -157,12 +153,15 @@ def tile_attend_gclip_sg_u_pl_kernel(
         u_got = sb("u_got", [P, 2, SLOTS], BF16, "sv_col1")
         for t in range(2):
             nc.vector.tensor_copy(u_got[:, t, :], u_win[t][:].indirect(offs_sb[:]))
-        vd_codes = sb("vd_codes", [P, SLOTS], U32, "u_win1")
+        vd_codes = sb("vd_codes", [P, SLOTS], U32, "u_win2")
         vd_scales = sb("vd_scales", [P, SLOTS], U8)
-        nc.vector.quantize_mx(
-            out=vd_codes[:].bitcast(E4M3), scales=vd_scales[:],
-            in_=vd_in[:].rearrange("p r s t -> p (r s t)"),
-        )
+
+        def quantise_vd():
+            nc.vector.quantize_mx(
+                out=vd_codes[:].bitcast(E4M3), scales=vd_scales[:],
+                in_=vd_in[:].rearrange("p r s t -> p (r s t)"),
+            )
+
         u_in = [sb("u_in%d" % h, [P, HALF, LANES], BF16, ("sv_col0", "u_in1")[h]) for h in range(2)]
         u_codes = sb("u_codes", [P, SLOTS], U32)
         u_scales = sb("u_scales", [P, SLOTS], U8)
@@ -175,10 +174,15 @@ def tile_attend_gclip_sg_u_pl_kernel(
         for h in range(2):
             cols = slice(h * HALF, (h + 1) * HALF)
             nc.scalar.copy(u_in[h][:, :, 0:2], u_got[:, :, cols].rearrange("p t i -> p i t"))
-            gather_u(2, h)
+        u_late = sb("u_late", [P, 2, HALF], BF16)
+        gather_u(2, 0)
+        nc.vector.tensor_copy(u_late[:, 0, :], u_win[2][:].indirect(entries(offs_sb, HALF, SLOTS)))
+        quantise_vd()
+        gather_u(3, 0)
+        nc.scalar.activation(u_late[:, 1, :], u_win[3][:].indirect(entries(offs_sb, HALF, SLOTS)), ACT.Copy)
+        nc.scalar.copy(u_in[1][:, :, 2:4], u_late[:].rearrange("p t i -> p i t"))
         for h in range(2):
             cols = slice(h * HALF, (h + 1) * HALF)
-            gather_u(3, h)
             nc.vector.quantize_mx(
                 out=u_codes[:, cols].bitcast(E4M3), scales=u_scales[:, cols],
                 in_=u_in[h][:].rearrange("p i t -> p (i t)"),
@@ -193,8 +197,11 @@ def tile_attend_gclip_sg_u_pl_kernel(
 
         a_sv = [sb("a_sv%d" % b, [P, SLOTS], F32) for b in range(BLOCKS)]
         sig = [sb("sig%d" % b, [P, SLOTS], F32) for b in range(BLOCKS)]
-        neg_y = [sb("neg_y%d" % b, [P, LANES, P], F32) for b in range(BLOCKS)]
+        neg_late = sb("neg_late", [P, 2, LANES, P], F32, "u_in1")
+        neg_y = [sb("neg_y%d" % b, [P, LANES, P], F32)[:] for b in range(2)] + [neg_late[:, b] for b in range(2)]
         g_in = sb("g_in", [P, LANES * SLOTS], BF16)
+        g_codes = sb("g_codes", [P, SLOTS], U32)
+        g_scales = sb("g_scales", [P, SLOTS], U8)
         a_ps = [bank("a_ps", 4 + b) for b in range(BLOCKS)]
         diff = [bank("diff", 4 + b) for b in range(BLOCKS)]
 
@@ -206,11 +213,12 @@ def tile_attend_gclip_sg_u_pl_kernel(
                 )
 
         def labels(b):
-            nc.scalar.activation(
-                neg_y[b][:].rearrange("p r s -> p s r"),
-                y_sb[b][:].rearrange("p (s r) -> p s r", r=LANES),
-                ACT.Copy, scale=-1.0,
-            )
+            dealt = neg_y[b].rearrange("p r s -> p s r")
+            plain = y_sb[b][:].rearrange("p (s r) -> p s r", r=LANES)
+            if b < 2:
+                nc.scalar.activation(dealt, plain, ACT.Copy, scale=-1.0)
+            else:
+                nc.gpsimd.tensor_scalar(dealt, plain, -1.0, 0.0, ALU.mult, ALU.add)
 
         def score(b):
             cols = slice(b * P, (b + 1) * P)
@@ -225,7 +233,7 @@ def tile_attend_gclip_sg_u_pl_kernel(
             nc.scalar.activation(sig[b][:], a_sv[b][:], ACT.Sigmoid, scale=su_col[:, b : b + 1])
 
         def grad(b):
-            turn(b, neg_y[b][:].rearrange("p r s -> p (r s)"), True)
+            turn(b, neg_y[b].rearrange("p r s -> p (r s)"), True)
             turn(b, sig[b][:], False)
             nc.vector.tensor_tensor(
                 g_in[:, b * SLOTS : (b + 1) * SLOTS].rearrange("s (i r) -> s i r", r=LANES),
@@ -235,104 +243,124 @@ def tile_attend_gclip_sg_u_pl_kernel(
             )
 
         def quantise_g(lo, hi):
-            cols = slice(HALF + lo, HALF + hi)
+            cols = slice(lo, hi)
             nc.vector.quantize_mx(
                 out=g_codes[:, cols].bitcast(E5M2), scales=g_scales[:, cols],
                 in_=g_in[:, LANES * lo : LANES * hi],
             )
 
-        def product(t, first, number):
-            flat = bank("du_ps", number)[:].rearrange("p a b -> p (a b)")
+        def product(t, lo, hi, out):
             tcols = slice(t * P, (t + 1) * P)
             nc.tensor.matmul_mx(
-                out=flat,
+                out=out,
                 lhsT=vt_codes[:, tcols].bitcast(E4M3), lhsT_scale=vt_scales[:, tcols],
-                rhs=g_codes[:, first : first + SLOTS].bitcast(E5M2),
-                rhs_scale=g_scales[:, first : first + SLOTS],
+                rhs=g_codes[:, lo:hi].bitcast(E5M2), rhs_scale=g_scales[:, lo:hi],
                 start=True, stop=True,
             )
-            return flat
 
-        du = [sb("du%d" % t, [P, SLOTS], F32) for t in range(LANES)]
+        def flat_bank(number):
+            return bank("du_ps", number)[:].rearrange("p a b -> p (a b)")
+
         for b in range(BLOCKS):
             labels(b)
         for b in range(BLOCKS):
             score(b)
         grad(0)
         grad(1)
-        grad(2)
         quantise_g(0, HALF)
+        early_ps = [flat_bank(t) for t in range(2)]
+        for t in range(2):
+            product(t, 0, HALF, early_ps[t][:, 0:HALF])
+        grad(2)
         grad(3)
-        nc.scalar.copy(du[0][:, 0:HALF], product(0, 0, 0)[:, HALF:SLOTS])
+        early = [sb("early%d" % t, [P, HALF], F32) for t in range(2)]
         quantise_g(HALF, HALF + P)
         quantise_g(HALF + P, SLOTS)
 
         out_rows = out_0.rearrange("(p t) c -> t p c", t=LANES)
-        pairs = sb("pairs", [P, 2 * TABLE], F32)
+        def scatter_v(t, lo, hi, src):
+            nc.vector.tensor_copy(out_win[t][:].indirect(entries(offs_sb, lo, hi)), src)
+
+        def scatter_s(t, h, src):
+            nc.scalar.activation(
+                out_win[t][:].indirect(entries(offs_sb, h * HALF, (h + 1) * HALF)), src, ACT.Copy
+            )
+
+        def store(t):
+            nc.sync.dma_start(out=out_rows[t], in_=out_win[t][:])
+
+        first_ps, second_ps = flat_bank(2), flat_bank(3)
+        for t in range(2):
+            product(2 + t, 0, HALF, first_ps[:, t * HALF : (t + 1) * HALF])
+        late_ps = [flat_bank(4 + t) for t in range(2)]
+        for t in range(2):
+            product(t, HALF, SLOTS, late_ps[t][:, 0:HALF])
+        for t in range(2):
+            product(2 + t, HALF, SLOTS, second_ps[:, t * HALF : (t + 1) * HALF])
+        late = [sb("late%d" % t, [P, HALF], F32) for t in range(2)]
+        first = sb("first", [P, SLOTS], F32)
+
+        for t in range(2):
+            nc.scalar.copy(early[t][:], early_ps[t][:, 0:HALF])
+            scatter_s(t, 0, early[t][:])
+        nc.vector.tensor_copy(first[:], first_ps)
+        for t in range(2):
+            nc.vector.tensor_copy(late[t][:], late_ps[t][:, 0:HALF])
+        for t in range(2):
+            scatter_v(t, HALF, SLOTS, late[t][:])
+            store(t)
+        second = sb("second", [P, SLOTS], F32, "early1")
+        nc.vector.tensor_copy(second[:], second_ps)
+        for t in range(2):
+            scatter_s(2 + t, 0, first[:, t * HALF : (t + 1) * HALF])
+        for t in range(2):
+            scatter_s(2 + t, 1, second[:, t * HALF : (t + 1) * HALF])
+            store(2 + t)
+
+        pairs = sb("pairs", [P, 2 * TABLE], F32, "late1")
+        o_codes = sb("o_codes", [P, TABLE], U32)
+        o_scales = sb("o_scales", [P, PLANE], U8)
+        words_out = out_1[0].rearrange("p c l -> p (c l)").bitcast(I32)
+        o_in = sb("o_in", [P, LANES * TABLE], BF16)
 
         def round_lane(copy, t, lo, hi):
             first = (t // 2) * TABLE
             halves = pairs[:, first + lo : first + hi].bitcast(BF16)
             copy(halves[:, t % 2 : 2 * (hi - lo) : 2], out_win[t][:, lo:hi])
 
-        nc.scalar.copy(du[0][:, HALF:SLOTS], product(0, HALF, 1)[:, HALF:SLOTS])
-        for t in range(1, LANES):
-            nc.scalar.copy(du[t][:], product(t, HALF, (t + 1) % LANES))
-        out_reuses = ["u_in1", "g_in", "du0", "du1"]
-        out_win = []
-        for t in range(LANES):
-            out_win.append(sb("out_win%d" % t, [P, TABLE], F32, out_reuses[t]))
-            nc.gpsimd.memset(out_win[t][:], 0.0)
-            for lo, hi in ((0, HALF), (HALF, SLOTS)) if t == 0 else ((0, SLOTS),):
-                nc.vector.tensor_tensor(
-                    out_win[t][:].indirect(entries(offs_sb, lo, hi)), du[t][:, lo:hi], zero[:, lo:hi], ALU.add
-                )
-            nc.sync.dma_start(out=out_rows[t], in_=out_win[t][:])
-            if t < 2:
-                round_lane(nc.scalar.copy, t, 0, TABLE)
-            elif t == 2:
-                nc.scalar.copy(
-                    pairs[:, TABLE : TABLE + FIRST].bitcast(BF16).rearrange("p (c e) -> p c e", e=2),
-                    out_win[t][:, 0:FIRST].unsqueeze(2).to_broadcast([P, FIRST, 2]),
-                )
-                round_lane(nc.scalar.copy, t, FIRST, TABLE)
-        round_lane(nc.vector.tensor_copy, LANES - 1, 0, FIRST)
-        round_lane(nc.scalar.copy, LANES - 1, FIRST, STEP)
-        for lo in range(STEP, TABLE, STEP):
-            round_lane(nc.scalar.copy, LANES - 1, lo, lo + STEP)
+        for t in range(2):
+            round_lane(nc.vector.tensor_copy, t, 0, TABLE)
+        for t in range(2, LANES):
+            round_lane(nc.vector.tensor_copy, t, 0, SPLIT)
+            round_lane(nc.scalar.copy, t, SPLIT, TABLE)
 
-        o_codes = sb("o_codes", [P, TABLE], U32)
-        o_scales = sb("o_scales", [P, PLANE], U8)
-        words_out = out_1[0].rearrange("p c l -> p (c l)").bitcast(I32)
-        spent = ["u_win2", "v_win1", "v_win2", "v_win3", "u_win0"]
-        o_in = [sb("o_in%d" % k, [P, hi - lo, LANES], BF16, spent[k]) for k, (lo, hi) in enumerate(RANGES)]
-
-        def weave(copy, k, lo, hi):
-            first = RANGES[k][0]
+        def weave(copy, lo, hi):
             copy(
-                o_in[k][:, lo - first : hi - first, :].bitcast(F32).rearrange("p (c e) u -> p c u e", e=2),
+                o_in[:, LANES * lo : LANES * hi].bitcast(F32).rearrange("p (c e u) -> p c u e", e=2, u=2),
                 pairs[:].rearrange("p (u c e) -> p c u e", u=2, e=2)[:, lo // 2 : hi // 2, :, :],
             )
 
-        def finish(k):
-            lo, hi = RANGES[k]
+        def quantise_out(lo, hi):
             plane, at = divmod(lo, PLANE)
             nc.vector.quantize_mx(
                 out=o_codes[:, lo:hi].bitcast(E4M3),
                 scales=o_scales[4 * plane : P, at : at + hi - lo],
-                in_=o_in[k][:].rearrange("p c t -> p (c t)"),
+                in_=o_in[:, LANES * lo : LANES * hi],
             )
+
+        def store_codes(lo, hi):
             nc.sync.dma_start(out=words_out[:, lo:hi], in_=o_codes[:, lo:hi].bitcast(I32))
 
-        weave(nc.vector.tensor_copy, 0, 0, FIRST)
-        weave(nc.vector.tensor_copy, 0, FIRST, RANGES[0][1])
-        for k in range(1, ON_VECTOR):
-            weave(nc.vector.tensor_copy, k, *RANGES[k])
-            finish(k - 1)
-        finish(ON_VECTOR - 1)
-        for k in range(ON_VECTOR, len(RANGES)):
-            weave(nc.scalar.copy, k, *RANGES[k])
-            finish(k)
+        for lo, hi in ((SPLIT, 1536), (1536, 1792), (1792, TABLE)):
+            weave(nc.scalar.copy, lo, hi)
+        weave(nc.vector.tensor_copy, 0, 512)
+        weave(nc.vector.tensor_copy, 512, SPLIT)
+        quantise_out(0, 512)
+        quantise_out(512, 1024)
+        store_codes(0, 1024)
+        for lo, hi in ((1024, 1536), (1536, 1792), (1792, TABLE)):
+            quantise_out(lo, hi)
+            store_codes(lo, hi)
         for q in range(4):
             (nc.scalar, nc.sync)[q % 2].dma_start(
                 out=out_2[0, 4 * q : 4 * q + 4, :].bitcast(I32).rearrange("r (a c) -> a r c", a=TABLE // PLANE),

@@ -178,6 +178,13 @@ def tile_attend_gclip_sg_u_pl_kernel(
         gather_u(2, 0)
         nc.vector.tensor_copy(u_late[:, 0, :], u_win[2][:].indirect(entries(offs_sb, HALF, SLOTS)))
         quantise_vd()
+        for number in range(2):
+            nc.tensor.matmul_mx(
+                out=bank("warm_ps", number)[:].rearrange("p a b -> p (a b)"),
+                lhsT=vd_codes[:, 0:P].bitcast(E4M3), lhsT_scale=vd_scales[:, 0:P],
+                rhs=vd_codes[:].bitcast(E4M3), rhs_scale=vd_scales[:],
+                start=True, stop=True,
+            )
         gather_u(3, 0)
         nc.scalar.activation(u_late[:, 1, :], u_win[3][:].indirect(entries(offs_sb, HALF, SLOTS)), ACT.Copy)
         nc.scalar.copy(u_in[1][:, :, 2:4], u_late[:].rearrange("p t i -> p i t"))

@@ -178,13 +178,6 @@ def tile_attend_gclip_sg_u_pl_kernel(
         gather_u(2, 0)
         nc.vector.tensor_copy(u_late[:, 0, :], u_win[2][:].indirect(entries(offs_sb, HALF, SLOTS)))
         quantise_vd()
-        for number in range(2):
-            nc.tensor.matmul_mx(
-                out=bank("warm_ps", number)[:].rearrange("p a b -> p (a b)"),
-                lhsT=vd_codes[:, 0:P].bitcast(E4M3), lhsT_scale=vd_scales[:, 0:P],
-                rhs=vd_codes[:].bitcast(E4M3), rhs_scale=vd_scales[:],
-                start=True, stop=True,
-            )
         gather_u(3, 0)
         nc.scalar.activation(u_late[:, 1, :], u_win[3][:].indirect(entries(offs_sb, HALF, SLOTS)), ACT.Copy)
         nc.scalar.copy(u_in[1][:, :, 2:4], u_late[:].rearrange("p t i -> p i t"))
@@ -225,7 +218,9 @@ def tile_attend_gclip_sg_u_pl_kernel(
             if b < 2:
                 nc.scalar.activation(dealt, plain, ACT.Copy, scale=-1.0)
             else:
-                nc.gpsimd.tensor_scalar(dealt, plain, -1.0, 0.0, ALU.mult, ALU.add)
+                nc.gpsimd.tensor_scalar(
+                    neg_y[b], y_sb[b][:].rearrange("p (s r) -> p r s", r=LANES), -1.0, 0.0, ALU.mult, ALU.add
+                )
 
         def score(b):
             cols = slice(b * P, (b + 1) * P)
@@ -337,8 +332,10 @@ def tile_attend_gclip_sg_u_pl_kernel(
 
         for t in range(2):
             round_lane(nc.vector.tensor_copy, t, 0, TABLE)
+        round_lane(nc.vector.tensor_copy, 2, 0, SPLIT)
+        round_lane(nc.vector.tensor_copy, 3, 0, 512)
+        round_lane(nc.vector.tensor_copy, 3, 512, SPLIT)
         for t in range(2, LANES):
-            round_lane(nc.vector.tensor_copy, t, 0, SPLIT)
             round_lane(nc.scalar.copy, t, SPLIT, TABLE)
 
         def weave(copy, lo, hi):
@@ -358,16 +355,15 @@ def tile_attend_gclip_sg_u_pl_kernel(
         def store_codes(lo, hi):
             nc.sync.dma_start(out=words_out[:, lo:hi], in_=o_codes[:, lo:hi].bitcast(I32))
 
-        for lo, hi in ((SPLIT, 1536), (1536, 1792), (1792, TABLE)):
+        for lo, hi in ((SPLIT, 1536), (1536, TABLE)):
             weave(nc.scalar.copy, lo, hi)
         weave(nc.vector.tensor_copy, 0, 512)
-        weave(nc.vector.tensor_copy, 512, SPLIT)
-        quantise_out(0, 512)
-        quantise_out(512, 1024)
-        store_codes(0, 1024)
-        for lo, hi in ((1024, 1536), (1536, 1792), (1792, TABLE)):
-            quantise_out(lo, hi)
-            store_codes(lo, hi)
+        weave(nc.vector.tensor_copy, 512, 1024)
+        for lo in range(0, TABLE, 512):
+            if lo == 512:
+                weave(nc.vector.tensor_copy, 1024, SPLIT)
+            quantise_out(lo, lo + 512)
+            store_codes(lo, lo + 512)
         for q in range(4):
             (nc.scalar, nc.sync)[q % 2].dma_start(
                 out=out_2[0, 4 * q : 4 * q + 4, :].bitcast(I32).rearrange("r (a c) -> a r c", a=TABLE // PLANE),

@@ -27,7 +27,8 @@ ODD = TABLE // 2 - 1
 FLOPS = 2 * 2 * D * SLOTS * SLOTS
 BYTES = 4 * (3 * D * TABLE + SLOTS * SLOTS + 2 * TABLE) + D * TABLE + 16 * TABLE + 2 * 2 * P * 32
 
-SPLIT = 1152
+HELP = 1024
+SPLIT = 1312
 PLANE = 1024
 
 
@@ -109,6 +110,8 @@ def tile_attend_gclip_sg_u_pl_kernel(
         gather_v(1)
         for t in range(LANES):
             nc.gpsimd.memset(out_win[t][:], 0.0)
+        zero = sb("zero", [P, P], F32)
+        nc.gpsimd.memset(zero[:], 0.0)
 
         sv_all = sb("sv_all", [P, SLOTS], F32)
         nc.scalar.copy(sv_all[:], sv_all_ps[:].rearrange("p r s -> p (r s)"))
@@ -274,14 +277,23 @@ def tile_attend_gclip_sg_u_pl_kernel(
         for t in range(2):
             product(t, 0, HALF, early_ps[t][:, 0:HALF])
         grad(2)
-        grad(3)
-        early = [sb("early%d" % t, [P, HALF], F32) for t in range(2)]
         quantise_g(HALF, HALF + P)
+        grad(3)
+        third_ps = flat_bank(4)
+        product(0, HALF, HALF + P, third_ps[:, 0:P])
+        early = [sb("early%d" % t, [P, HALF], F32) for t in range(2)]
+        third = sb("third", [P, P], F32)
+        nc.vector.tensor_copy(third[:], third_ps[:, 0:P])
         quantise_g(HALF + P, SLOTS)
 
         out_rows = out_0.rearrange("(p t) c -> t p c", t=LANES)
         def scatter_v(t, lo, hi, src):
             nc.vector.tensor_copy(out_win[t][:].indirect(entries(offs_sb, lo, hi)), src)
+
+        def scatter_block(b, src):
+            nc.vector.tensor_tensor(
+                out_win[0][:].indirect(entries(offs_sb, b * P, (b + 1) * P)), src, zero[:], ALU.add
+            )
 
         def scatter_s(t, h, src):
             nc.scalar.activation(
@@ -294,23 +306,26 @@ def tile_attend_gclip_sg_u_pl_kernel(
         first_ps, second_ps = flat_bank(2), flat_bank(3)
         for t in range(2):
             product(2 + t, 0, HALF, first_ps[:, t * HALF : (t + 1) * HALF])
-        late_ps = [flat_bank(4 + t) for t in range(2)]
-        for t in range(2):
-            product(t, HALF, SLOTS, late_ps[t][:, 0:HALF])
+        fourth_ps, late_ps = flat_bank(5), flat_bank(6)
+        product(0, HALF + P, SLOTS, fourth_ps[:, 0:P])
+        product(1, HALF, SLOTS, late_ps[:, 0:HALF])
         for t in range(2):
             product(2 + t, HALF, SLOTS, second_ps[:, t * HALF : (t + 1) * HALF])
-        late = [sb("late%d" % t, [P, HALF], F32) for t in range(2)]
         first = sb("first", [P, SLOTS], F32)
 
         for t in range(2):
             nc.scalar.copy(early[t][:], early_ps[t][:, 0:HALF])
             scatter_s(t, 0, early[t][:])
         nc.vector.tensor_copy(first[:], first_ps)
-        for t in range(2):
-            nc.vector.tensor_copy(late[t][:], late_ps[t][:, 0:HALF])
-        for t in range(2):
-            scatter_v(t, HALF, SLOTS, late[t][:])
-            store(t)
+        fourth = sb("fourth", [P, P], F32)
+        nc.vector.tensor_copy(fourth[:], fourth_ps[:, 0:P])
+        scatter_block(2, third[:])
+        late = sb("late", [P, HALF], F32, "early0")
+        nc.vector.tensor_copy(late[:], late_ps[:, 0:HALF])
+        scatter_block(3, fourth[:])
+        store(0)
+        scatter_v(1, HALF, SLOTS, late[:])
+        store(1)
         second = sb("second", [P, SLOTS], F32, "early1")
         nc.vector.tensor_copy(second[:], second_ps)
         for t in range(2):
@@ -319,29 +334,37 @@ def tile_attend_gclip_sg_u_pl_kernel(
             scatter_s(2 + t, 1, second[:, t * HALF : (t + 1) * HALF])
             store(2 + t)
 
-        pairs = sb("pairs", [P, 2 * TABLE], F32, "late1")
+        pairs = [sb("pairs%d" % a, [P, 2 * HELP], F32, ("pairs0", "early0")[a]) for a in range(2)]
         o_codes = sb("o_codes", [P, TABLE], U32)
         o_scales = sb("o_scales", [P, PLANE], U8)
         words_out = out_1[0].rearrange("p c l -> p (c l)").bitcast(I32)
         o_in = sb("o_in", [P, LANES * TABLE], BF16)
 
         def round_lane(copy, t, lo, hi):
-            first = (t // 2) * TABLE
-            halves = pairs[:, first + lo : first + hi].bitcast(BF16)
+            a, at = divmod(lo, HELP)
+            first = (t // 2) * HELP + at
+            halves = pairs[a][:, first : first + hi - lo].bitcast(BF16)
             copy(halves[:, t % 2 : 2 * (hi - lo) : 2], out_win[t][:, lo:hi])
 
-        for t in range(2):
-            round_lane(nc.vector.tensor_copy, t, 0, TABLE)
-        round_lane(nc.vector.tensor_copy, 2, 0, SPLIT)
-        round_lane(nc.vector.tensor_copy, 3, 0, 512)
-        round_lane(nc.vector.tensor_copy, 3, 512, SPLIT)
+        nc.gpsimd.tensor_scalar(
+            pairs[0][:, 0:HELP].bitcast(BF16).rearrange("p (c e) -> p c e", e=2),
+            out_win[0][:, 0:HELP].unsqueeze(2).to_broadcast([P, HELP, 2]),
+            1.0, -0.0, ALU.mult, ALU.add,
+        )
+        round_lane(nc.vector.tensor_copy, 0, HELP, TABLE)
+        round_lane(nc.vector.tensor_copy, 1, HELP, TABLE)
+        round_lane(nc.vector.tensor_copy, 1, 0, HELP)
+        for t in range(2, LANES):
+            round_lane(nc.vector.tensor_copy, t, 0, HELP)
+            round_lane(nc.vector.tensor_copy, t, HELP, SPLIT)
         for t in range(2, LANES):
             round_lane(nc.scalar.copy, t, SPLIT, TABLE)
 
         def weave(copy, lo, hi):
+            a, at = divmod(lo, HELP)
             copy(
                 o_in[:, LANES * lo : LANES * hi].bitcast(F32).rearrange("p (c e u) -> p c u e", e=2, u=2),
-                pairs[:].rearrange("p (u c e) -> p c u e", u=2, e=2)[:, lo // 2 : hi // 2, :, :],
+                pairs[a][:].rearrange("p (u c e) -> p c u e", u=2, e=2)[:, at // 2 : (at + hi - lo) // 2, :, :],
             )
 
         def quantise_out(lo, hi):

@@ -51,18 +51,22 @@ def tile_attend_gclip_sg_u_pl_kernel(
 
         offs_sb = keep.tile([P, SLOTS // PER_COLUMN], U16, name="offs_sb")
         qoffs_sb = keep.tile([P, SLOTS // PER_COLUMN], U16, name="qoffs_sb")
-        nc.sync.dma_start(offs_sb[:], offs)
-        nc.sync.dma_start(qoffs_sb[:], qoffs)
         su_win = sb("su_win", [P, TABLE], F32)
         sv_win = sb("sv_win", [P, TABLE], F32)
         for win, src in ((su_win, su), (sv_win, sv)):
             nc.sync.dma_start(out=win[LIVE:P, :], in_=src[0:1, :])
-        v_win = [sb("v_win%d" % t, [P, TABLE], F32) for t in range(LANES)]
-        u_win = [sb("u_win%d" % t, [P, TABLE], F32) for t in range(LANES)]
-        for wins, src in ((v_win, vT), (u_win, uT)):
-            rows = src.rearrange("(p t) c -> t p c", t=LANES)
-            for t in range(LANES):
-                nc.sync.dma_start(out=wins[t][:], in_=rows[t])
+        nc.sync.dma_start(offs_sb[:], offs)
+        nc.sync.dma_start(qoffs_sb[:], qoffs)
+
+        def load_lanes(name, src, lo, hi):
+            tile = sb(name, [P, (hi - lo) * TABLE], F32)
+            nc.sync.dma_start(
+                out=tile[:], in_=src.rearrange("(p t) c -> p (t c)", t=LANES)[:, lo * TABLE : hi * TABLE]
+            )
+            return [tile[:, t * TABLE : (t + 1) * TABLE] for t in range(hi - lo)]
+
+        v_win = load_lanes("v_win01", vT, 0, 2) + load_lanes("v_win23", vT, 2, 4)
+        u_win = [load_lanes("u_win%d" % t, uT, t, t + 1)[0] for t in range(LANES)]
         y_sb = [sb("y_sb%d" % b, [P, SLOTS], F32) for b in range(BLOCKS)]
         for b in range(BLOCKS):
             nc.sync.dma_start(out=y_sb[b][:], in_=y[b * P : (b + 1) * P, :])
@@ -78,10 +82,12 @@ def tile_attend_gclip_sg_u_pl_kernel(
 
         su_row = sb("su_row", [P, SLOTS], F32)
         sv_row = sb("sv_row", [P, SLOTS], F32)
-        v_got = [sb("v_got0", [P, 2, SLOTS], BF16)]
+        v_got = [sb("v_got0", [P, 2, 2, P, 2], BF16)]
 
         def gather_v(t):
-            nc.vector.tensor_copy(v_got[t // 2][:, t % 2, :], v_win[t][:].indirect(qoffs_sb[:]))
+            nc.vector.tensor_copy(
+                v_got[t // 2][:, t % 2].rearrange("p u s e -> p s u e"), v_win[t].indirect(qoffs_sb[:])
+            )
 
         nc.vector.tensor_copy(su_row[:], su_win[:].indirect(offs_sb[:]))
         nc.vector.tensor_copy(sv_row[:], sv_win[:].indirect(qoffs_sb[:]))
@@ -105,7 +111,7 @@ def tile_attend_gclip_sg_u_pl_kernel(
             nc.tensor.transpose(sv_all_ps[:, r, :], sv_cols[1][:, r : r + 1].to_broadcast([P, P]), ident[:])
 
         out_win = []
-        for t, spent in enumerate(("su_win", "sv_win", "v_win0", "v_win1")):
+        for t, spent in enumerate(("su_win", "sv_win", "v_win01", None)):
             out_win.append(sb("out_win%d" % t, [P, TABLE], F32, spent))
         gather_v(1)
         for t in range(LANES):
@@ -127,7 +133,7 @@ def tile_attend_gclip_sg_u_pl_kernel(
 
         both_scales(0)
         both_scales(1)
-        v_got.append(sb("v_got1", [P, 2, SLOTS], BF16, "sv_col0"))
+        v_got.append(sb("v_got1", [P, 2, 2, P, 2], BF16, "sv_col0"))
         gather_v(2)
         gather_v(3)
         both_scales(2)
@@ -136,17 +142,15 @@ def tile_attend_gclip_sg_u_pl_kernel(
         vd_in = sb("vd_in", [P, LANES, P, LANES], BF16)
         for t in (0, 2):
             nc.scalar.copy(
-                vd_in[:, :, :, t : t + 2],
-                v_got[t // 2][:].rearrange("p t (s r) -> p r s t", r=LANES),
+                vd_in[:, :, :, t : t + 2].rearrange("p (u e) s t -> p u e s t", e=2),
+                v_got[t // 2][:].rearrange("p t u s e -> p u e s t"),
             )
         vt_in = sb("vt_in", [P, LANES, P, LANES], BF16)
         vt_ps = [bank("vt_ps", (3, 0)[half]) for half in range(2)]
         for t in range(LANES):
-            words = v_got[t // 2][:, t % 2, :].bitcast(F32)
             for u in range(2):
-                nc.tensor.transpose(
-                    vt_ps[t // 2][:, 2 * (t % 2) + u, :], words[:, u : SLOTS // 2 : 2], ident[:]
-                )
+                words = v_got[t // 2][:, t % 2, u].rearrange("p s e -> p (s e)").bitcast(F32)
+                nc.tensor.transpose(vt_ps[t // 2][:, 2 * (t % 2) + u, :], words, ident[:])
         for half in range(2):
             nc.scalar.copy(
                 vt_in[:, 2 * half : 2 * half + 2, :, :].bitcast(F32),
@@ -155,8 +159,8 @@ def tile_attend_gclip_sg_u_pl_kernel(
 
         u_got = sb("u_got", [P, 2, SLOTS], BF16, "sv_col1")
         for t in range(2):
-            nc.vector.tensor_copy(u_got[:, t, :], u_win[t][:].indirect(offs_sb[:]))
-        vd_codes = sb("vd_codes", [P, SLOTS], U32, "u_win2")
+            nc.vector.tensor_copy(u_got[:, t, :], u_win[t].indirect(offs_sb[:]))
+        vd_codes = sb("vd_codes", [P, SLOTS], U32, "u_win1")
         vd_scales = sb("vd_scales", [P, SLOTS], U8)
 
         def quantise_vd():
@@ -171,7 +175,7 @@ def tile_attend_gclip_sg_u_pl_kernel(
 
         def gather_u(t, h):
             nc.vector.tensor_copy(
-                u_in[h][:, :, t], u_win[t][:].indirect(entries(offs_sb, h * HALF, (h + 1) * HALF))
+                u_in[h][:, :, t], u_win[t].indirect(entries(offs_sb, h * HALF, (h + 1) * HALF))
             )
 
         for h in range(2):
@@ -179,10 +183,10 @@ def tile_attend_gclip_sg_u_pl_kernel(
             nc.scalar.copy(u_in[h][:, :, 0:2], u_got[:, :, cols].rearrange("p t i -> p i t"))
         u_late = sb("u_late", [P, 2, HALF], BF16)
         gather_u(2, 0)
-        nc.vector.tensor_copy(u_late[:, 0, :], u_win[2][:].indirect(entries(offs_sb, HALF, SLOTS)))
+        nc.vector.tensor_copy(u_late[:, 0, :], u_win[2].indirect(entries(offs_sb, HALF, SLOTS)))
         quantise_vd()
         gather_u(3, 0)
-        nc.scalar.activation(u_late[:, 1, :], u_win[3][:].indirect(entries(offs_sb, HALF, SLOTS)), ACT.Copy)
+        nc.scalar.activation(u_late[:, 1, :], u_win[3].indirect(entries(offs_sb, HALF, SLOTS)), ACT.Copy)
         nc.scalar.copy(u_in[1][:, :, 2:4], u_late[:].rearrange("p t i -> p i t"))
         for h in range(2):
             cols = slice(h * HALF, (h + 1) * HALF)

@@ -188,11 +188,11 @@ def tile_attend_gclip_sg_u_pl_kernel(
         gather_u(3, 0)
         nc.scalar.activation(u_late[:, 1, :], u_win[3].indirect(entries(offs_sb, HALF, SLOTS)), ACT.Copy)
         nc.scalar.copy(u_in[1][:, :, 2:4], u_late[:].rearrange("p t i -> p i t"))
-        for h in range(2):
-            cols = slice(h * HALF, (h + 1) * HALF)
+        for lo, hi in ((0, P), (P, HALF), (HALF, HALF + P), (HALF + P, SLOTS)):
+            h, at = divmod(lo, HALF)
             nc.vector.quantize_mx(
-                out=u_codes[:, cols].bitcast(E4M3), scales=u_scales[:, cols],
-                in_=u_in[h][:].rearrange("p i t -> p (i t)"),
+                out=u_codes[:, lo:hi].bitcast(E4M3), scales=u_scales[:, lo:hi],
+                in_=u_in[h][:, at : at + hi - lo, :].rearrange("p i t -> p (i t)"),
             )
 
         vt_codes = sb("vt_codes", [P, D], U32, "sv_col0")
@@ -276,7 +276,8 @@ def tile_attend_gclip_sg_u_pl_kernel(
             score(b)
         grad(0)
         grad(1)
-        quantise_g(0, HALF)
+        quantise_g(0, P)
+        quantise_g(P, HALF)
         early_ps = [flat_bank(t) for t in range(2)]
         for t in range(2):
             product(t, 0, HALF, early_ps[t][:, 0:HALF])

@@ -38,6 +38,7 @@ def tile_attend_gclip_sg_u_pl_kernel(
     nc = tc.nc
     with ExitStack() as ctx:
         keep = ctx.enter_context(tc.tile_pool(name="keep", bufs=1))
+        laid = ctx.enter_context(tc.tile_pool(name="laid", bufs=1))
         psum = ctx.enter_context(tc.psum_pool(name="psum", bufs=1))
 
         def sb(name, shape, dtype, reuses=None):
@@ -65,7 +66,7 @@ def tile_attend_gclip_sg_u_pl_kernel(
             )
             return [tile[:, t * TABLE : (t + 1) * TABLE] for t in range(hi - lo)]
 
-        v_win = load_lanes("v_win01", vT, 0, 2) + load_lanes("v_win23", vT, 2, 4)
+        v_win = load_lanes("v_win0", vT, 0, 1) + load_lanes("v_win1", vT, 1, 2) + load_lanes("v_win23", vT, 2, 4)
         u_win = [load_lanes("u_win%d" % t, uT, t, t + 1)[0] for t in range(LANES)]
         y_sb = [sb("y_sb%d" % b, [P, SLOTS], F32) for b in range(BLOCKS)]
         for b in range(BLOCKS):
@@ -97,21 +98,20 @@ def tile_attend_gclip_sg_u_pl_kernel(
         su_all = bank("su_all", 2)
         sv_all_ps = bank("sv_all_ps", 3)
         su_col = sb("su_col", [P, BLOCKS], F32)
-        sv_cols = [sb("sv_col%d" % h, [P, LANES], F32) for h in range(2)]
+        sv_col = sb("sv_col", [P, LANES], F32)
         for b in range(BLOCKS):
             nc.tensor.transpose(su_ps[:, b, :], su_row[:, b * P : (b + 1) * P], ident[:])
         nc.scalar.copy(su_col[:], su_ps[:, :, LIVE])
         for r in range(LANES):
             nc.tensor.transpose(sv_ps[:, r, :], sv_row[:, r:SLOTS:LANES], ident[:])
-        for h in range(2):
-            nc.scalar.copy(sv_cols[h][:], sv_ps[:, :, LIVE])
+        nc.scalar.copy(sv_col[:], sv_ps[:, :, LIVE])
         for b in range(BLOCKS):
             nc.tensor.transpose(su_all[:, b, :], su_col[:, b : b + 1].to_broadcast([P, P]), ident[:])
         for r in range(LANES):
-            nc.tensor.transpose(sv_all_ps[:, r, :], sv_cols[1][:, r : r + 1].to_broadcast([P, P]), ident[:])
+            nc.tensor.transpose(sv_all_ps[:, r, :], sv_col[:, r : r + 1].to_broadcast([P, P]), ident[:])
 
         out_win = []
-        for t, spent in enumerate(("su_win", "sv_win", "v_win01", None)):
+        for t, spent in enumerate(("su_win", "sv_win", "v_win0", None)):
             out_win.append(sb("out_win%d" % t, [P, TABLE], F32, spent))
         gather_v(1)
         for t in range(LANES):
@@ -127,17 +127,15 @@ def tile_attend_gclip_sg_u_pl_kernel(
             nc.vector.tensor_tensor(
                 both[:, b * P : (b + 1) * P, :],
                 su_all[:, b, :].unsqueeze(2).to_broadcast([P, P, LANES]),
-                sv_cols[b // 2][:].unsqueeze(1).to_broadcast([P, P, LANES]),
+                sv_col[:].unsqueeze(1).to_broadcast([P, P, LANES]),
                 ALU.mult,
             )
 
-        both_scales(0)
-        both_scales(1)
-        v_got.append(sb("v_got1", [P, 2, 2, P, 2], BF16, "sv_col0"))
+        for b in range(BLOCKS):
+            both_scales(b)
+        v_got.append(sb("v_got1", [P, 2, 2, P, 2], BF16, "sv_col"))
         gather_v(2)
         gather_v(3)
-        both_scales(2)
-        both_scales(3)
 
         vd_in = sb("vd_in", [P, LANES, P, LANES], BF16)
         for t in (0, 2):
@@ -157,54 +155,62 @@ def tile_attend_gclip_sg_u_pl_kernel(
                 vt_ps[half][:].rearrange("s (tt u) p -> s tt p u", u=2),
             )
 
-        u_got = sb("u_got", [P, 2, SLOTS], BF16, "sv_col1")
+        u_got = sb("u_got", [P, 2, SLOTS], BF16)
         for t in range(2):
             nc.vector.tensor_copy(u_got[:, t, :], u_win[t].indirect(offs_sb[:]))
-        vd_codes = sb("vd_codes", [P, SLOTS], U32, "u_win1")
+        v_codes = sb("v_codes", [P, SLOTS + D], U32, "u_win1")
+        vd_codes = v_codes[:, 0:SLOTS]
+        vt_codes = v_codes[:, SLOTS : SLOTS + D]
         vd_scales = sb("vd_scales", [P, SLOTS], U8)
 
         def quantise_vd():
             nc.vector.quantize_mx(
-                out=vd_codes[:].bitcast(E4M3), scales=vd_scales[:],
+                out=vd_codes.bitcast(E4M3), scales=vd_scales[:],
                 in_=vd_in[:].rearrange("p r s t -> p (r s t)"),
             )
 
-        u_in = [sb("u_in%d" % h, [P, HALF, LANES], BF16, ("sv_col0", "u_in1")[h]) for h in range(2)]
+        u_first = sb("u_first", [P, HALF, LANES], BF16, "sv_col")
+        u_in = [u_first[:, 0:P, :], u_first[:, P:HALF, :]]
+        for b, at in ((2, 0), (3, 7 * SLOTS)):
+            u_in.append(laid.tile([P, P, LANES], BF16, name="u_in%d" % b, offset=at, align_bytes=64)[:])
         u_codes = sb("u_codes", [P, SLOTS], U32)
         u_scales = sb("u_scales", [P, SLOTS], U8)
 
-        def gather_u(t, h):
-            nc.vector.tensor_copy(
-                u_in[h][:, :, t], u_win[t].indirect(entries(offs_sb, h * HALF, (h + 1) * HALF))
-            )
+        def gather_first(t):
+            nc.vector.tensor_copy(u_first[:, :, t], u_win[t].indirect(entries(offs_sb, 0, HALF)))
 
-        for h in range(2):
-            cols = slice(h * HALF, (h + 1) * HALF)
-            nc.scalar.copy(u_in[h][:, :, 0:2], u_got[:, :, cols].rearrange("p t i -> p i t"))
+        for b in (2, 3):
+            nc.scalar.copy(u_in[b][:, :, 0:2], u_got[:, :, b * P : (b + 1) * P].rearrange("p t i -> p i t"))
         u_late = sb("u_late", [P, 2, HALF], BF16)
-        gather_u(2, 0)
+        gather_first(2)
+        nc.scalar.copy(u_first[:, :, 0:2], u_got[:, :, 0:HALF].rearrange("p t i -> p i t"))
         nc.vector.tensor_copy(u_late[:, 0, :], u_win[2].indirect(entries(offs_sb, HALF, SLOTS)))
         quantise_vd()
-        gather_u(3, 0)
-        nc.scalar.activation(u_late[:, 1, :], u_win[3].indirect(entries(offs_sb, HALF, SLOTS)), ACT.Copy)
-        nc.scalar.copy(u_in[1][:, :, 2:4], u_late[:].rearrange("p t i -> p i t"))
-        for lo, hi in ((0, P), (P, HALF), (HALF, HALF + P), (HALF + P, SLOTS)):
-            h, at = divmod(lo, HALF)
+        gather_first(3)
+        for lo in (0, P):
+            nc.scalar.activation(
+                u_late[:, 1, lo : lo + P], u_win[3].indirect(entries(offs_sb, HALF + lo, HALF + lo + P)), ACT.Copy
+            )
+        for b in (2, 3):
+            lo = (b - 2) * P
+            nc.scalar.copy(u_in[b][:, :, 2:4], u_late[:, :, lo : lo + P].rearrange("p t i -> p i t"))
+        for b in range(BLOCKS):
+            cols = slice(b * P, (b + 1) * P)
             nc.vector.quantize_mx(
-                out=u_codes[:, lo:hi].bitcast(E4M3), scales=u_scales[:, lo:hi],
-                in_=u_in[h][:, at : at + hi - lo, :].rearrange("p i t -> p (i t)"),
+                out=u_codes[:, cols].bitcast(E4M3), scales=u_scales[:, cols],
+                in_=u_in[b].rearrange("p i t -> p (i t)"),
             )
 
-        vt_codes = sb("vt_codes", [P, D], U32, "sv_col0")
         vt_scales = sb("vt_scales", [P, D], U8)
         nc.vector.quantize_mx(
-            out=vt_codes[:].bitcast(E4M3), scales=vt_scales[:],
+            out=vt_codes.bitcast(E4M3), scales=vt_scales[:],
             in_=vt_in[:].rearrange("s t p r -> s (t p r)"),
         )
 
-        a_sv = [sb("a_sv%d" % b, [P, SLOTS], F32) for b in range(BLOCKS)]
+        a_sv = [laid.tile([P, SLOTS], F32, name="a_sv%d" % b, offset=4 * SLOTS * b, align_bytes=64)[:] for b in range(2)]
+        a_sv = a_sv + [sb("a_sv%d" % b, [P, SLOTS], F32)[:] for b in range(2, BLOCKS)]
         sig = [sb("sig%d" % b, [P, SLOTS], F32) for b in range(BLOCKS)]
-        neg_late = sb("neg_late", [P, 2, LANES, P], F32, "u_in1")
+        neg_late = laid.tile([P, 2, LANES, P], F32, name="neg_late", offset=8 * SLOTS, align_bytes=64)
         neg_y = [sb("neg_y%d" % b, [P, LANES, P], F32)[:] for b in range(2)] + [neg_late[:, b] for b in range(2)]
         g_in = sb("g_in", [P, LANES * SLOTS], BF16)
         g_codes = sb("g_codes", [P, SLOTS], U32)
@@ -235,11 +241,11 @@ def tile_attend_gclip_sg_u_pl_kernel(
             nc.tensor.matmul_mx(
                 out=flat,
                 lhsT=u_codes[:, cols].bitcast(E4M3), lhsT_scale=u_scales[:, cols],
-                rhs=vd_codes[:].bitcast(E4M3), rhs_scale=vd_scales[:],
+                rhs=vd_codes.bitcast(E4M3), rhs_scale=vd_scales[:],
                 start=True, stop=True,
             )
-            nc.vector.tensor_tensor(a_sv[b][:], flat, sv_all[:], ALU.mult)
-            nc.scalar.activation(sig[b][:], a_sv[b][:], ACT.Sigmoid, scale=su_col[:, b : b + 1])
+            nc.vector.tensor_tensor(a_sv[b], flat, sv_all[:], ALU.mult)
+            nc.scalar.activation(sig[b][:], a_sv[b], ACT.Sigmoid, scale=su_col[:, b : b + 1])
 
         def grad(b):
             turn(b, neg_y[b].rearrange("p r s -> p (r s)"), True)

@@ -27,8 +27,9 @@ ODD = TABLE // 2 - 1
 FLOPS = 2 * 2 * D * SLOTS * SLOTS
 BYTES = 4 * (3 * D * TABLE + SLOTS * SLOTS + 2 * TABLE) + D * TABLE + 16 * TABLE + 2 * 2 * P * 32
 
-HELP = 1024
-SPLIT = 1312
+RANGE = 512
+HELP = 1280
+SPLIT = 992
 PLANE = 1024
 
 
@@ -116,8 +117,6 @@ def tile_attend_gclip_sg_u_pl_kernel(
         gather_v(1)
         for t in range(LANES):
             nc.gpsimd.memset(out_win[t][:], 0.0)
-        zero = sb("zero", [P, P], F32)
-        nc.gpsimd.memset(zero[:], 0.0)
 
         sv_all = sb("sv_all", [P, SLOTS], F32)
         nc.scalar.copy(sv_all[:], sv_all_ps[:].rearrange("p r s -> p (r s)"))
@@ -155,62 +154,48 @@ def tile_attend_gclip_sg_u_pl_kernel(
                 vt_ps[half][:].rearrange("s (tt u) p -> s tt p u", u=2),
             )
 
-        u_got = sb("u_got", [P, 2, SLOTS], BF16)
-        for t in range(2):
-            nc.vector.tensor_copy(u_got[:, t, :], u_win[t].indirect(offs_sb[:]))
+        u_in = [
+            sb("u_first", [P, HALF, LANES], BF16),
+            laid.tile([P, HALF, LANES], BF16, name="u_second", offset=0, align_bytes=64),
+        ]
+
+        def gather_u(t):
+            nc.vector.tensor_copy(u_in[1][:, :, t], u_win[t].indirect(entries(offs_sb, HALF, SLOTS)))
+            step = P if t == LANES - 1 else HALF
+            for lo in range(0, HALF, step):
+                nc.scalar.activation(
+                    u_in[0][:, lo : lo + step, t], u_win[t].indirect(entries(offs_sb, lo, lo + step)), ACT.Copy
+                )
+
+        gather_u(0)
+        gather_u(1)
         v_codes = sb("v_codes", [P, SLOTS + D], U32, "u_win1")
         vd_codes = v_codes[:, 0:SLOTS]
         vt_codes = v_codes[:, SLOTS : SLOTS + D]
         vd_scales = sb("vd_scales", [P, SLOTS], U8)
-
-        def quantise_vd():
-            nc.vector.quantize_mx(
-                out=vd_codes.bitcast(E4M3), scales=vd_scales[:],
-                in_=vd_in[:].rearrange("p r s t -> p (r s t)"),
-            )
-
-        u_first = sb("u_first", [P, HALF, LANES], BF16, "sv_col")
-        u_in = [u_first[:, 0:P, :], u_first[:, P:HALF, :]]
-        for b, at in ((2, 0), (3, 7 * SLOTS)):
-            u_in.append(laid.tile([P, P, LANES], BF16, name="u_in%d" % b, offset=at, align_bytes=64)[:])
-        u_codes = sb("u_codes", [P, SLOTS], U32)
-        u_scales = sb("u_scales", [P, SLOTS], U8)
-
-        def gather_first(t):
-            nc.vector.tensor_copy(u_first[:, :, t], u_win[t].indirect(entries(offs_sb, 0, HALF)))
-
-        for b in (2, 3):
-            nc.scalar.copy(u_in[b][:, :, 0:2], u_got[:, :, b * P : (b + 1) * P].rearrange("p t i -> p i t"))
-        u_late = sb("u_late", [P, 2, HALF], BF16)
-        gather_first(2)
-        nc.scalar.copy(u_first[:, :, 0:2], u_got[:, :, 0:HALF].rearrange("p t i -> p i t"))
-        nc.vector.tensor_copy(u_late[:, 0, :], u_win[2].indirect(entries(offs_sb, HALF, SLOTS)))
-        quantise_vd()
-        gather_first(3)
-        for lo in (0, P):
-            nc.scalar.activation(
-                u_late[:, 1, lo : lo + P], u_win[3].indirect(entries(offs_sb, HALF + lo, HALF + lo + P)), ACT.Copy
-            )
-        for b in (2, 3):
-            lo = (b - 2) * P
-            nc.scalar.copy(u_in[b][:, :, 2:4], u_late[:, :, lo : lo + P].rearrange("p t i -> p i t"))
-        for b in range(BLOCKS):
-            cols = slice(b * P, (b + 1) * P)
-            nc.vector.quantize_mx(
-                out=u_codes[:, cols].bitcast(E4M3), scales=u_scales[:, cols],
-                in_=u_in[b].rearrange("p i t -> p (i t)"),
-            )
-
         vt_scales = sb("vt_scales", [P, D], U8)
+        nc.vector.quantize_mx(
+            out=vd_codes.bitcast(E4M3), scales=vd_scales[:],
+            in_=vd_in[:].rearrange("p r s t -> p (r s t)"),
+        )
         nc.vector.quantize_mx(
             out=vt_codes.bitcast(E4M3), scales=vt_scales[:],
             in_=vt_in[:].rearrange("s t p r -> s (t p r)"),
         )
+        gather_u(2)
+        gather_u(3)
+        u_codes = sb("u_codes", [P, SLOTS], U32)
+        u_scales = sb("u_scales", [P, SLOTS], U8)
+        for b in range(BLOCKS):
+            cols = slice(b * P, (b + 1) * P)
+            nc.vector.quantize_mx(
+                out=u_codes[:, cols].bitcast(E4M3), scales=u_scales[:, cols],
+                in_=u_in[b // 2][:, (b % 2) * P : (b % 2 + 1) * P, :].rearrange("p i t -> p (i t)"),
+            )
 
-        a_sv = [laid.tile([P, SLOTS], F32, name="a_sv%d" % b, offset=4 * SLOTS * b, align_bytes=64)[:] for b in range(2)]
-        a_sv = a_sv + [sb("a_sv%d" % b, [P, SLOTS], F32)[:] for b in range(2, BLOCKS)]
+        a_sv = [sb("a_sv%d" % b, [P, SLOTS], F32)[:] for b in range(BLOCKS)]
         sig = [sb("sig%d" % b, [P, SLOTS], F32) for b in range(BLOCKS)]
-        neg_late = laid.tile([P, 2, LANES, P], F32, name="neg_late", offset=8 * SLOTS, align_bytes=64)
+        neg_late = laid.tile([P, 2, LANES, P], F32, name="neg_late", offset=0, align_bytes=64)
         neg_y = [sb("neg_y%d" % b, [P, LANES, P], F32)[:] for b in range(2)] + [neg_late[:, b] for b in range(2)]
         g_in = sb("g_in", [P, LANES * SLOTS], BF16)
         g_codes = sb("g_codes", [P, SLOTS], U32)
@@ -284,27 +269,21 @@ def tile_attend_gclip_sg_u_pl_kernel(
         grad(1)
         quantise_g(0, P)
         quantise_g(P, HALF)
-        early_ps = [flat_bank(t) for t in range(2)]
-        for t in range(2):
-            product(t, 0, HALF, early_ps[t][:, 0:HALF])
         grad(2)
-        quantise_g(HALF, HALF + P)
+        early_ps = [flat_bank(t) for t in range(LANES)]
         grad(3)
-        third_ps = flat_bank(4)
-        product(0, HALF, HALF + P, third_ps[:, 0:P])
-        early = [sb("early%d" % t, [P, HALF], F32) for t in range(2)]
-        third = sb("third", [P, P], F32)
-        nc.vector.tensor_copy(third[:], third_ps[:, 0:P])
+        for t in (0, 1, 3, 2):
+            product(t, 0, HALF, early_ps[t][:, 0:HALF])
+        quantise_g(HALF, HALF + P)
         quantise_g(HALF + P, SLOTS)
+        late_ps = [flat_bank(4 + t) for t in range(LANES)]
+        for t in (0, 1, 3, 2):
+            product(t, HALF, SLOTS, late_ps[t][:, 0:HALF])
 
         out_rows = out_0.rearrange("(p t) c -> t p c", t=LANES)
+
         def scatter_v(t, lo, hi, src):
             nc.vector.tensor_copy(out_win[t][:].indirect(entries(offs_sb, lo, hi)), src)
-
-        def scatter_block(b, src):
-            nc.vector.tensor_tensor(
-                out_win[0][:].indirect(entries(offs_sb, b * P, (b + 1) * P)), src, zero[:], ALU.add
-            )
 
         def scatter_s(t, h, src):
             nc.scalar.activation(
@@ -314,90 +293,93 @@ def tile_attend_gclip_sg_u_pl_kernel(
         def store(t):
             nc.sync.dma_start(out=out_rows[t], in_=out_win[t][:])
 
-        first_ps, second_ps = flat_bank(2), flat_bank(3)
         for t in range(2):
-            product(2 + t, 0, HALF, first_ps[:, t * HALF : (t + 1) * HALF])
-        fourth_ps, late_ps = flat_bank(5), flat_bank(6)
-        product(0, HALF + P, SLOTS, fourth_ps[:, 0:P])
-        product(1, HALF, SLOTS, late_ps[:, 0:HALF])
+            early = sb("early%d" % t, [P, HALF], F32)
+            nc.scalar.copy(early[:], early_ps[t][:, 0:HALF])
+            scatter_s(t, 0, early[:])
+        early3 = sb("early3", [P, HALF], F32, "g_in")
+        nc.vector.tensor_copy(early3[:], early_ps[3][:, 0:HALF])
+        spot = 8 * SLOTS + 2 * HALF
+        places = (spot + 16 * SLOTS, spot, spot - 2 * HALF, spot + 2 * HALF)
+        late = [
+            laid.tile([P, HALF], F32, name="late%d" % t, offset=places[t], align_bytes=64) for t in range(LANES)
+        ]
         for t in range(2):
-            product(2 + t, HALF, SLOTS, second_ps[:, t * HALF : (t + 1) * HALF])
-        first = sb("first", [P, SLOTS], F32)
-
-        for t in range(2):
-            nc.scalar.copy(early[t][:], early_ps[t][:, 0:HALF])
-            scatter_s(t, 0, early[t][:])
-        nc.vector.tensor_copy(first[:], first_ps)
-        fourth = sb("fourth", [P, P], F32)
-        nc.vector.tensor_copy(fourth[:], fourth_ps[:, 0:P])
-        scatter_block(2, third[:])
-        late = sb("late", [P, HALF], F32, "early0")
-        nc.vector.tensor_copy(late[:], late_ps[:, 0:HALF])
-        scatter_block(3, fourth[:])
+            nc.vector.tensor_copy(late[t][:], late_ps[t][:, 0:HALF])
+        scatter_v(0, HALF, SLOTS, late[0][:])
         store(0)
-        scatter_v(1, HALF, SLOTS, late[:])
+        early2 = sb("early2", [P, HALF], F32, "early0")
+        scatter_v(1, HALF, SLOTS, late[1][:])
         store(1)
-        second = sb("second", [P, SLOTS], F32, "early1")
-        nc.vector.tensor_copy(second[:], second_ps)
-        for t in range(2):
-            scatter_s(2 + t, 0, first[:, t * HALF : (t + 1) * HALF])
-        for t in range(2):
-            scatter_s(2 + t, 1, second[:, t * HALF : (t + 1) * HALF])
-            store(2 + t)
+        nc.scalar.copy(early2[:], early_ps[2][:, 0:HALF])
+        scatter_s(3, 0, early3[:])
+        scatter_s(2, 0, early2[:])
+        for t in (3, 2):
+            nc.vector.tensor_copy(late[t][:], late_ps[t][:, 0:HALF])
+        scatter_v(3, HALF, SLOTS, late[3][:])
+        store(3)
+        scatter_s(2, 1, late[2][:])
+        store(2)
 
-        pairs = [sb("pairs%d" % a, [P, 2 * HELP], F32, ("pairs0", "early0")[a]) for a in range(2)]
-        o_codes = sb("o_codes", [P, TABLE], U32)
+        widths = (HELP, TABLE - HELP)
+        pairs = [sb("pairs0", [P, 2 * widths[0]], F32), laid.tile([P, 2 * widths[1]], F32, name="pairs1", offset=places[3], align_bytes=64)]
+        o_codes = [sb("o_codes%d" % k, [P, RANGE], U32, (None, None, None, "v_win0")[k]) for k in range(4)]
+
+        def codes(lo, hi):
+            return o_codes[lo // RANGE][:, lo % RANGE : lo % RANGE + hi - lo]
+
         o_scales = sb("o_scales", [P, PLANE], U8)
         words_out = out_1[0].rearrange("p c l -> p (c l)").bitcast(I32)
         o_in = sb("o_in", [P, LANES * TABLE], BF16)
 
-        def round_lane(copy, t, lo, hi):
-            a, at = divmod(lo, HELP)
-            first = (t // 2) * HELP + at
-            halves = pairs[a][:, first : first + hi - lo].bitcast(BF16)
-            copy(halves[:, t % 2 : 2 * (hi - lo) : 2], out_win[t][:, lo:hi])
+        def pieces(lo, hi):
+            cuts = [(0, lo, min(hi, HELP)), (1, max(lo, HELP), hi)]
+            return [(a, x - a * HELP, x, z) for a, x, z in cuts if x < z]
 
-        nc.gpsimd.tensor_scalar(
-            pairs[0][:, 0:HELP].bitcast(BF16).rearrange("p (c e) -> p c e", e=2),
-            out_win[0][:, 0:HELP].unsqueeze(2).to_broadcast([P, HELP, 2]),
-            1.0, -0.0, ALU.mult, ALU.add,
-        )
-        round_lane(nc.vector.tensor_copy, 0, HELP, TABLE)
-        round_lane(nc.vector.tensor_copy, 1, HELP, TABLE)
-        round_lane(nc.vector.tensor_copy, 1, 0, HELP)
-        for t in range(2, LANES):
-            round_lane(nc.vector.tensor_copy, t, 0, HELP)
-            round_lane(nc.vector.tensor_copy, t, HELP, SPLIT)
-        for t in range(2, LANES):
-            round_lane(nc.scalar.copy, t, SPLIT, TABLE)
+        def gpsimd_copy(dst, src):
+            nc.gpsimd.tensor_scalar(dst, src, 1.0, -0.0, ALU.mult, ALU.add)
+
+        def round_lane(copy, t, lo, hi):
+            for a, at, x, z in pieces(lo, hi):
+                word = (t // 2) * widths[a] + at
+                halves = pairs[a][:, word : word + z - x].bitcast(BF16)
+                copy(halves[:, t % 2 : 2 * (z - x) : 2], out_win[t][:, x:z])
 
         def weave(copy, lo, hi):
-            a, at = divmod(lo, HELP)
-            copy(
-                o_in[:, LANES * lo : LANES * hi].bitcast(F32).rearrange("p (c e u) -> p c u e", e=2, u=2),
-                pairs[a][:].rearrange("p (u c e) -> p c u e", u=2, e=2)[:, at // 2 : (at + hi - lo) // 2, :, :],
-            )
+            for a, at, x, z in pieces(lo, hi):
+                copy(
+                    o_in[:, LANES * x : LANES * z].bitcast(F32).rearrange("p (c e u) -> p c u e", e=2, u=2),
+                    pairs[a][:].rearrange("p (u c e) -> p c u e", u=2, e=2)[:, at // 2 : (at + z - x) // 2, :, :],
+                )
 
         def quantise_out(lo, hi):
             plane, at = divmod(lo, PLANE)
             nc.vector.quantize_mx(
-                out=o_codes[:, lo:hi].bitcast(E4M3),
+                out=codes(lo, hi).bitcast(E4M3),
                 scales=o_scales[4 * plane : P, at : at + hi - lo],
                 in_=o_in[:, LANES * lo : LANES * hi],
             )
 
         def store_codes(lo, hi):
-            nc.sync.dma_start(out=words_out[:, lo:hi], in_=o_codes[:, lo:hi].bitcast(I32))
+            nc.sync.dma_start(out=words_out[:, lo:hi], in_=codes(lo, hi).bitcast(I32))
 
-        for lo, hi in ((SPLIT, 1536), (1536, TABLE)):
-            weave(nc.scalar.copy, lo, hi)
-        weave(nc.vector.tensor_copy, 0, 512)
-        weave(nc.vector.tensor_copy, 512, 1024)
-        for lo in range(0, TABLE, 512):
-            if lo == 512:
-                weave(nc.vector.tensor_copy, 1024, SPLIT)
-            quantise_out(lo, lo + 512)
-            store_codes(lo, lo + 512)
+        for t in (0, 1):
+            round_lane(gpsimd_copy, t, 0, HELP)
+            round_lane(nc.vector.tensor_copy, t, HELP, TABLE)
+        for t in (3, 2):
+            round_lane(nc.vector.tensor_copy, t, 0, SPLIT)
+            round_lane(nc.scalar.copy, t, SPLIT, TABLE)
+        cuts = (0, RANGE, 2 * RANGE, 3 * RANGE, TABLE - RANGE // 2, TABLE)
+        ranges = list(zip(cuts, cuts[1:]))
+        for lo, hi in ranges:
+            if lo < SPLIT:
+                weave(nc.vector.tensor_copy, lo, min(hi, SPLIT))
+            if hi > SPLIT:
+                weave(nc.scalar.copy, max(lo, SPLIT), hi)
+        for lo, hi in ranges:
+            quantise_out(lo, hi)
+            if hi % RANGE == 0:
+                store_codes(hi - RANGE, hi)
         for q in range(4):
             (nc.scalar, nc.sync)[q % 2].dma_start(
                 out=out_2[0, 4 * q : 4 * q + 4, :].bitcast(I32).rearrange("r (a c) -> a r c", a=TABLE // PLANE),

@@ -28,8 +28,8 @@ FLOPS = 2 * 2 * D * SLOTS * SLOTS
 BYTES = 4 * (3 * D * TABLE + SLOTS * SLOTS + 2 * TABLE) + D * TABLE + 16 * TABLE + 2 * 2 * P * 32
 
 RANGE = 512
-HELP = 1280
-SPLIT = 992
+HELP = 1024
+SPLIT = 960
 PLANE = 1024
 
 
@@ -154,48 +154,62 @@ def tile_attend_gclip_sg_u_pl_kernel(
                 vt_ps[half][:].rearrange("s (tt u) p -> s tt p u", u=2),
             )
 
-        u_in = [
-            sb("u_first", [P, HALF, LANES], BF16),
-            laid.tile([P, HALF, LANES], BF16, name="u_second", offset=0, align_bytes=64),
-        ]
-
-        def gather_u(t):
-            nc.vector.tensor_copy(u_in[1][:, :, t], u_win[t].indirect(entries(offs_sb, HALF, SLOTS)))
-            step = P if t == LANES - 1 else HALF
-            for lo in range(0, HALF, step):
-                nc.scalar.activation(
-                    u_in[0][:, lo : lo + step, t], u_win[t].indirect(entries(offs_sb, lo, lo + step)), ACT.Copy
-                )
-
-        gather_u(0)
-        gather_u(1)
+        u_got = sb("u_got", [P, 2, SLOTS], BF16)
+        for t in range(2):
+            nc.vector.tensor_copy(u_got[:, t, :], u_win[t].indirect(offs_sb[:]))
         v_codes = sb("v_codes", [P, SLOTS + D], U32, "u_win1")
         vd_codes = v_codes[:, 0:SLOTS]
         vt_codes = v_codes[:, SLOTS : SLOTS + D]
         vd_scales = sb("vd_scales", [P, SLOTS], U8)
-        vt_scales = sb("vt_scales", [P, D], U8)
-        nc.vector.quantize_mx(
-            out=vd_codes.bitcast(E4M3), scales=vd_scales[:],
-            in_=vd_in[:].rearrange("p r s t -> p (r s t)"),
-        )
-        nc.vector.quantize_mx(
-            out=vt_codes.bitcast(E4M3), scales=vt_scales[:],
-            in_=vt_in[:].rearrange("s t p r -> s (t p r)"),
-        )
-        gather_u(2)
-        gather_u(3)
+
+        def quantise_vd():
+            nc.vector.quantize_mx(
+                out=vd_codes.bitcast(E4M3), scales=vd_scales[:],
+                in_=vd_in[:].rearrange("p r s t -> p (r s t)"),
+            )
+
+        u_first = sb("u_first", [P, HALF, LANES], BF16, "sv_col")
+        u_in = [u_first[:, 0:P, :], u_first[:, P:HALF, :]]
+        for b, at in ((2, 0), (3, 7 * SLOTS)):
+            u_in.append(laid.tile([P, P, LANES], BF16, name="u_in%d" % b, offset=at, align_bytes=64)[:])
         u_codes = sb("u_codes", [P, SLOTS], U32)
         u_scales = sb("u_scales", [P, SLOTS], U8)
+
+        def gather_first(t):
+            nc.vector.tensor_copy(u_first[:, :, t], u_win[t].indirect(entries(offs_sb, 0, HALF)))
+
+        for b in (2, 3):
+            nc.scalar.copy(u_in[b][:, :, 0:2], u_got[:, :, b * P : (b + 1) * P].rearrange("p t i -> p i t"))
+        u_late = sb("u_late", [P, 2, HALF], BF16)
+        gather_first(2)
+        nc.scalar.copy(u_first[:, :, 0:2], u_got[:, :, 0:HALF].rearrange("p t i -> p i t"))
+        nc.vector.tensor_copy(u_late[:, 0, :], u_win[2].indirect(entries(offs_sb, HALF, SLOTS)))
+        quantise_vd()
+        gather_first(3)
+        for lo in (0, P):
+            nc.scalar.activation(
+                u_late[:, 1, lo : lo + P], u_win[3].indirect(entries(offs_sb, HALF + lo, HALF + lo + P)), ACT.Copy
+            )
+        for b in (2, 3):
+            lo = (b - 2) * P
+            nc.scalar.copy(u_in[b][:, :, 2:4], u_late[:, :, lo : lo + P].rearrange("p t i -> p i t"))
         for b in range(BLOCKS):
             cols = slice(b * P, (b + 1) * P)
             nc.vector.quantize_mx(
                 out=u_codes[:, cols].bitcast(E4M3), scales=u_scales[:, cols],
-                in_=u_in[b // 2][:, (b % 2) * P : (b % 2 + 1) * P, :].rearrange("p i t -> p (i t)"),
+                in_=u_in[b].rearrange("p i t -> p (i t)"),
             )
 
-        a_sv = [sb("a_sv%d" % b, [P, SLOTS], F32)[:] for b in range(BLOCKS)]
+        vt_scales = sb("vt_scales", [P, D], U8)
+        nc.vector.quantize_mx(
+            out=vt_codes.bitcast(E4M3), scales=vt_scales[:],
+            in_=vt_in[:].rearrange("s t p r -> s (t p r)"),
+        )
+
+        a_sv = [laid.tile([P, SLOTS], F32, name="a_sv%d" % b, offset=4 * SLOTS * b, align_bytes=64)[:] for b in range(2)]
+        a_sv = a_sv + [sb("a_sv%d" % b, [P, SLOTS], F32)[:] for b in range(2, BLOCKS)]
         sig = [sb("sig%d" % b, [P, SLOTS], F32) for b in range(BLOCKS)]
-        neg_late = laid.tile([P, 2, LANES, P], F32, name="neg_late", offset=0, align_bytes=64)
+        neg_late = laid.tile([P, 2, LANES, P], F32, name="neg_late", offset=8 * SLOTS, align_bytes=64)
         neg_y = [sb("neg_y%d" % b, [P, LANES, P], F32)[:] for b in range(2)] + [neg_late[:, b] for b in range(2)]
         g_in = sb("g_in", [P, LANES * SLOTS], BF16)
         g_codes = sb("g_codes", [P, SLOTS], U32)
@@ -299,7 +313,7 @@ def tile_attend_gclip_sg_u_pl_kernel(
             scatter_s(t, 0, early[:])
         early3 = sb("early3", [P, HALF], F32, "g_in")
         nc.vector.tensor_copy(early3[:], early_ps[3][:, 0:HALF])
-        spot = 8 * SLOTS + 2 * HALF
+        spot = 16 * SLOTS + 2 * HALF
         places = (spot + 16 * SLOTS, spot, spot - 2 * HALF, spot + 2 * HALF)
         late = [
             laid.tile([P, HALF], F32, name="late%d" % t, offset=places[t], align_bytes=64) for t in range(LANES)

@@ -28,8 +28,7 @@ FLOPS = 2 * 2 * D * SLOTS * SLOTS
 BYTES = 4 * (3 * D * TABLE + SLOTS * SLOTS + 2 * TABLE) + D * TABLE + 16 * TABLE + 2 * 2 * P * 32
 
 RANGE = 512
-HELP = 1024
-SPLIT = 960
+SPLIT = 1280
 PLANE = 1024
 
 
@@ -335,65 +334,72 @@ def tile_attend_gclip_sg_u_pl_kernel(
         scatter_s(2, 1, late[2][:])
         store(2)
 
-        widths = (HELP, TABLE - HELP)
-        pairs = [sb("pairs0", [P, 2 * widths[0]], F32), laid.tile([P, 2 * widths[1]], F32, name="pairs1", offset=places[3], align_bytes=64)]
-        o_codes = [sb("o_codes%d" % k, [P, RANGE], U32, (None, None, None, "v_win0")[k]) for k in range(4)]
-
-        def codes(lo, hi):
-            return o_codes[lo // RANGE][:, lo % RANGE : lo % RANGE + hi - lo]
-
+        pairs = sb("pairs", [P, 2 * SPLIT], F32)
+        o_codes = sb("o_codes", [P, TABLE], U32)
         o_scales = sb("o_scales", [P, PLANE], U8)
         words_out = out_1[0].rearrange("p c l -> p (c l)").bitcast(I32)
         o_in = sb("o_in", [P, LANES * TABLE], BF16)
 
-        def pieces(lo, hi):
-            cuts = [(0, lo, min(hi, HELP)), (1, max(lo, HELP), hi)]
-            return [(a, x - a * HELP, x, z) for a, x, z in cuts if x < z]
+        def halves(t):
+            return pairs[:, (t // 2) * SPLIT : (t // 2 + 1) * SPLIT].bitcast(BF16)[:, t % 2 : 2 * SPLIT : 2]
 
-        def gpsimd_copy(dst, src):
-            nc.gpsimd.tensor_scalar(dst, src, 1.0, -0.0, ALU.mult, ALU.add)
+        for t in (0, 1):
+            nc.gpsimd.tensor_scalar(halves(t), out_win[t][:, 0:SPLIT], 1.0, -0.0, ALU.mult, ALU.add)
+        for t in (3, 2):
+            nc.vector.tensor_copy(halves(t), out_win[t][:, 0:SPLIT])
 
-        def round_lane(copy, t, lo, hi):
-            for a, at, x, z in pieces(lo, hi):
-                word = (t // 2) * widths[a] + at
-                halves = pairs[a][:, word : word + z - x].bitcast(BF16)
-                copy(halves[:, t % 2 : 2 * (z - x) : 2], out_win[t][:, x:z])
-
-        def weave(copy, lo, hi):
-            for a, at, x, z in pieces(lo, hi):
-                copy(
-                    o_in[:, LANES * x : LANES * z].bitcast(F32).rearrange("p (c e u) -> p c u e", e=2, u=2),
-                    pairs[a][:].rearrange("p (u c e) -> p c u e", u=2, e=2)[:, at // 2 : (at + z - x) // 2, :, :],
+        groups = (TABLE - SPLIT) // HALF
+        turned = [
+            laid.tile([P, 2 * groups, P, 2], BF16, name="turned0", offset=spot - 8 * groups * P, align_bytes=64),
+            sb("turned1", [P, 2 * groups, P, 2], BF16),
+        ]
+        for u in range(2):
+            there = [bank("there", groups * u + k) for k in range(groups)]
+            for e in (1, 0):
+                for j in range(2 * groups):
+                    lo = SPLIT + j * P
+                    nc.tensor.transpose(
+                        there[j // 2][:, 2 * (j % 2) + e, :], out_win[2 * u + e][:, lo : lo + P], ident[:]
+                    )
+            for k in range(groups):
+                nc.scalar.copy(
+                    turned[u][:, 2 * k : 2 * k + 2], there[k][:].rearrange("c (j e) p -> c j p e", e=2)
                 )
+        for k in range(groups):
+            back = bank("back", (2 * groups + k) % 8)
+            for u in range(2):
+                for j in range(2):
+                    words = turned[u][:, 2 * k + j].rearrange("c p e -> c (p e)").bitcast(F32)
+                    nc.tensor.transpose(back[:, 2 * j + u, :], words, ident[:])
+            lo = SPLIT + k * HALF
+            nc.scalar.copy(
+                o_in[:, LANES * lo : LANES * (lo + HALF)].bitcast(F32).rearrange("p (j c u) -> p j c u", j=2, u=2),
+                back[:].rearrange("p (j u) c -> p j c u", u=2),
+            )
+
+        def weave(lo, hi):
+            nc.vector.tensor_copy(
+                o_in[:, LANES * lo : LANES * hi].bitcast(F32).rearrange("p (c e u) -> p c u e", e=2, u=2),
+                pairs[:].rearrange("p (u c e) -> p c u e", u=2, e=2)[:, lo // 2 : hi // 2, :, :],
+            )
 
         def quantise_out(lo, hi):
             plane, at = divmod(lo, PLANE)
             nc.vector.quantize_mx(
-                out=codes(lo, hi).bitcast(E4M3),
+                out=o_codes[:, lo:hi].bitcast(E4M3),
                 scales=o_scales[4 * plane : P, at : at + hi - lo],
                 in_=o_in[:, LANES * lo : LANES * hi],
             )
 
-        def store_codes(lo, hi):
-            nc.sync.dma_start(out=words_out[:, lo:hi], in_=codes(lo, hi).bitcast(I32))
-
-        for t in (0, 1):
-            round_lane(gpsimd_copy, t, 0, HELP)
-            round_lane(nc.vector.tensor_copy, t, HELP, TABLE)
-        for t in (3, 2):
-            round_lane(nc.vector.tensor_copy, t, 0, SPLIT)
-            round_lane(nc.scalar.copy, t, SPLIT, TABLE)
-        cuts = (0, RANGE, 2 * RANGE, 3 * RANGE, TABLE - RANGE // 2, TABLE)
-        ranges = list(zip(cuts, cuts[1:]))
-        for lo, hi in ranges:
-            if lo < SPLIT:
-                weave(nc.vector.tensor_copy, lo, min(hi, SPLIT))
-            if hi > SPLIT:
-                weave(nc.scalar.copy, max(lo, SPLIT), hi)
-        for lo, hi in ranges:
+        cuts = (0, RANGE, 2 * RANGE, 3 * RANGE, TABLE - HALF, TABLE)
+        for lo in range(0, SPLIT, RANGE):
+            weave(lo, min(lo + RANGE, SPLIT))
+        stored = 0
+        for lo, hi in zip(cuts, cuts[1:]):
             quantise_out(lo, hi)
-            if hi % RANGE == 0:
-                store_codes(hi - RANGE, hi)
+            if hi in (2 * RANGE, 3 * RANGE, TABLE):
+                nc.sync.dma_start(out=words_out[:, stored:hi], in_=o_codes[:, stored:hi].bitcast(I32))
+                stored = hi
         for q in range(4):
             (nc.scalar, nc.sync)[q % 2].dma_start(
                 out=out_2[0, 4 * q : 4 * q + 4, :].bitcast(I32).rearrange("r (a c) -> a r c", a=TABLE // PLANE),

@@ -345,8 +345,9 @@ def tile_attend_gclip_sg_u_pl_kernel(
 
         for t in (0, 1):
             nc.gpsimd.tensor_scalar(halves(t), out_win[t][:, 0:SPLIT], 1.0, -0.0, ALU.mult, ALU.add)
-        for t in (3, 2):
-            nc.vector.tensor_copy(halves(t), out_win[t][:, 0:SPLIT])
+        nc.vector.tensor_copy(halves(3), out_win[3][:, 0:SPLIT])
+        for lo, hi in ((0, 2 * RANGE), (2 * RANGE, SPLIT)):
+            nc.vector.tensor_copy(halves(2)[:, lo:hi], out_win[2][:, lo:hi])
 
         groups = (TABLE - SPLIT) // HALF
         turned = [
@@ -392,10 +393,12 @@ def tile_attend_gclip_sg_u_pl_kernel(
             )
 
         cuts = (0, RANGE, 2 * RANGE, 3 * RANGE, TABLE - HALF, TABLE)
-        for lo in range(0, SPLIT, RANGE):
-            weave(lo, min(lo + RANGE, SPLIT))
+        for lo in (0, RANGE):
+            weave(lo, lo + RANGE)
         stored = 0
         for lo, hi in zip(cuts, cuts[1:]):
+            if lo == 2 * RANGE:
+                weave(lo, SPLIT)
             quantise_out(lo, hi)
             if hi in (2 * RANGE, 3 * RANGE, TABLE):
                 nc.sync.dma_start(out=words_out[:, stored:hi], in_=o_codes[:, stored:hi].bitcast(I32))

@@ -54,10 +54,8 @@ def tile_attend_gclip_sg_u_pl_kernel(
         qoffs_sb = keep.tile([P, SLOTS // PER_COLUMN], U16, name="qoffs_sb")
         su_win = sb("su_win", [P, TABLE], F32)
         sv_win = sb("sv_win", [P, TABLE], F32)
-        for win, src in ((su_win, su), (sv_win, sv)):
-            nc.sync.dma_start(out=win[LIVE:P, :], in_=src[0:1, :])
+        nc.sync.dma_start(out=su_win[LIVE:P, :], in_=su[0:1, :])
         nc.sync.dma_start(offs_sb[:], offs)
-        nc.sync.dma_start(qoffs_sb[:], qoffs)
 
         def load_lanes(name, src, lo, hi):
             tile = sb(name, [P, (hi - lo) * TABLE], F32)
@@ -66,7 +64,10 @@ def tile_attend_gclip_sg_u_pl_kernel(
             )
             return [tile[:, t * TABLE : (t + 1) * TABLE] for t in range(hi - lo)]
 
-        v_win = load_lanes("v_win0", vT, 0, 1) + load_lanes("v_win1", vT, 1, 2) + load_lanes("v_win23", vT, 2, 4)
+        v_win = load_lanes("v_win0", vT, 0, 1)
+        nc.sync.dma_start(out=sv_win[LIVE:P, :], in_=sv[0:1, :])
+        nc.sync.dma_start(qoffs_sb[:], qoffs)
+        v_win = v_win + load_lanes("v_win1", vT, 1, 2) + load_lanes("v_win23", vT, 2, 4)
         u_win = [load_lanes("u_win%d" % t, uT, t, t + 1)[0] for t in range(LANES)]
         y_sb = [sb("y_sb%d" % b, [P, SLOTS], F32) for b in range(BLOCKS)]
         for b in range(BLOCKS):

from contextlib import ExitStack

import concourse.mybir as mybir
from concourse.masks import make_identity

F32 = mybir.dt.float32
BF16 = mybir.dt.bfloat16
U32 = mybir.dt.uint32
I32 = mybir.dt.int32
U16 = mybir.dt.uint16
U8 = mybir.dt.uint8
E4M3 = mybir.dt.float8_e4m3fn_x4
E5M2 = mybir.dt.float8_e5m2_x4
ACT = mybir.ActivationFunctionType
ALU = mybir.AluOpType

P = 128
LANES = 4
BLOCKS = 4
D = 512
SLOTS = 512
TABLE = 2048
HALF = SLOTS // 2
PER_COLUMN = 16
LIVE = P - 1
ODD = TABLE // 2 - 1
FLOPS = 2 * 2 * D * SLOTS * SLOTS
BYTES = 4 * (3 * D * TABLE + SLOTS * SLOTS + 2 * TABLE) + D * TABLE + 16 * TABLE + 2 * 2 * P * 32

RANGE = 512
SPLIT = 1280
PLANE = 1024


def tile_attend_gclip_sg_u_pl_kernel(
    tc, uT, vT, su, sv, y, offs, qoffs, out_0, out_1, out_2
):
    nc = tc.nc
    with ExitStack() as ctx:
        keep = ctx.enter_context(tc.tile_pool(name="keep", bufs=1))
        laid = ctx.enter_context(tc.tile_pool(name="laid", bufs=1))
        psum = ctx.enter_context(tc.psum_pool(name="psum", bufs=1))

        def sb(name, shape, dtype, reuses=None):
            return keep.tile(shape, dtype, name=name, tag=reuses or name, align_bytes=64)

        def bank(name, number):
            return psum.tile([P, LANES, P], F32, name=name, tag="bank%d" % number)

        def entries(lst, lo, hi):
            return lst[:, lo // PER_COLUMN : hi // PER_COLUMN]

        offs_sb = keep.tile([P, SLOTS // PER_COLUMN], U16, name="offs_sb")
        qoffs_sb = keep.tile([P, SLOTS // PER_COLUMN], U16, name="qoffs_sb")
        su_win = sb("su_win", [P, TABLE], F32)
        sv_win = sb("sv_win", [P, TABLE], F32)
        nc.sync.dma_start(out=su_win[LIVE:P, :], in_=su[0:1, :])
        nc.sync.dma_start(offs_sb[:], offs)

        def load_lanes(name, src, lo, hi):
            tile = sb(name, [P, (hi - lo) * TABLE], F32)
            nc.sync.dma_start(
                out=tile[:], in_=src.rearrange("(p t) c -> p (t c)", t=LANES)[:, lo * TABLE : hi * TABLE]
            )
            return [tile[:, t * TABLE : (t + 1) * TABLE] for t in range(hi - lo)]

        v_win = load_lanes("v_win0", vT, 0, 1)
        nc.sync.dma_start(out=sv_win[LIVE:P, :], in_=sv[0:1, :])
        nc.sync.dma_start(qoffs_sb[:], qoffs)
        v_win = v_win + load_lanes("v_win1", vT, 1, 2) + load_lanes("v_win23", vT, 2, 4)
        u_win = [load_lanes("u_win%d" % t, uT, t, t + 1)[0] for t in range(LANES)]
        y_sb = [sb("y_sb%d" % b, [P, SLOTS], F32) for b in range(BLOCKS)]
        for b in range(BLOCKS):
            nc.sync.dma_start(out=y_sb[b][:], in_=y[b * P : (b + 1) * P, :])

        ident = sb("ident", [P, P], F32)
        make_identity(nc, ident[:])
        nc.gpsimd.memset(sv_win[0:LIVE, :], 0.0)
        nc.vector.memset(su_win[0:LIVE, 0:ODD], 0.0)
        nc.vector.memset(su_win[0:LIVE, ODD:TABLE], 0.0)

        warm = sb("warm", [P, 8], F32)
        nc.scalar.activation(warm[:, 0:1], ident[:, 0:1], ACT.Sigmoid)

        su_row = sb("su_row", [P, SLOTS], F32)
        sv_row = sb("sv_row", [P, SLOTS], F32)
        v_got = [sb("v_got0", [P, 2, 2, P, 2], BF16)]

        def gather_v(t):
            nc.vector.tensor_copy(
                v_got[t // 2][:, t % 2].rearrange("p u s e -> p s u e"), v_win[t].indirect(qoffs_sb[:])
            )

        nc.vector.tensor_copy(su_row[:], su_win[:].indirect(offs_sb[:]))
        nc.vector.tensor_copy(sv_row[:], sv_win[:].indirect(qoffs_sb[:]))
        gather_v(0)
        su_ps = bank("su_ps", 1)
        sv_ps = bank("sv_ps", 0)
        su_all = bank("su_all", 2)
        sv_all_ps = bank("sv_all_ps", 3)
        su_col = sb("su_col", [P, BLOCKS], F32)
        sv_col = sb("sv_col", [P, LANES], F32)
        for b in range(BLOCKS):
            nc.tensor.transpose(su_ps[:, b, :], su_row[:, b * P : (b + 1) * P], ident[:])
        nc.scalar.copy(su_col[:], su_ps[:, :, LIVE])
        for r in range(LANES):
            nc.tensor.transpose(sv_ps[:, r, :], sv_row[:, r:SLOTS:LANES], ident[:])
        nc.scalar.copy(sv_col[:], sv_ps[:, :, LIVE])
        for b in range(BLOCKS):
            nc.tensor.transpose(su_all[:, b, :], su_col[:, b : b + 1].to_broadcast([P, P]), ident[:])
        for r in range(LANES):
            nc.tensor.transpose(sv_all_ps[:, r, :], sv_col[:, r : r + 1].to_broadcast([P, P]), ident[:])

        out_win = []
        for t, spent in enumerate(("su_win", "sv_win", "v_win0", None)):
            out_win.append(sb("out_win%d" % t, [P, TABLE], F32, spent))
        gather_v(1)
        for t in range(LANES):
            nc.gpsimd.memset(out_win[t][:], 0.0)

        sv_all = sb("sv_all", [P, SLOTS], F32)
        nc.scalar.copy(sv_all[:], sv_all_ps[:].rearrange("p r s -> p (r s)"))
        both = sb("both", [P, SLOTS, LANES], F32)

        def both_scales(b):
            nc.vector.tensor_tensor(
                both[:, b * P : (b + 1) * P, :],
                su_all[:, b, :].unsqueeze(2).to_broadcast([P, P, LANES]),
                sv_col[:].unsqueeze(1).to_broadcast([P, P, LANES]),
                ALU.mult,
            )

        for b in range(BLOCKS):
            both_scales(b)
        v_got.append(sb("v_got1", [P, 2, 2, P, 2], BF16, "sv_col"))
        gather_v(2)
        gather_v(3)

        vd_in = sb("vd_in", [P, LANES, P, LANES], BF16)
        for t in (0, 2):
            nc.scalar.copy(
                vd_in[:, :, :, t : t + 2].rearrange("p (u e) s t -> p u e s t", e=2),
                v_got[t // 2][:].rearrange("p t u s e -> p u e s t"),
            )
        vt_in = sb("vt_in", [P, LANES, P, LANES], BF16)
        vt_ps = [bank("vt_ps", (3, 0)[half]) for half in range(2)]
        for t in range(LANES):
            for u in range(2):
                words = v_got[t // 2][:, t % 2, u].rearrange("p s e -> p (s e)").bitcast(F32)
                nc.tensor.transpose(vt_ps[t // 2][:, 2 * (t % 2) + u, :], words, ident[:])
        for half in range(2):
            nc.scalar.copy(
                vt_in[:, 2 * half : 2 * half + 2, :, :].bitcast(F32),
                vt_ps[half][:].rearrange("s (tt u) p -> s tt p u", u=2),
            )

        u_got = sb("u_got", [P, 2, SLOTS], BF16)
        for t in range(2):
            nc.vector.tensor_copy(u_got[:, t, :], u_win[t].indirect(offs_sb[:]))
        v_codes = sb("v_codes", [P, SLOTS + D], U32, "u_win1")
        vd_codes = v_codes[:, 0:SLOTS]
        vt_codes = v_codes[:, SLOTS : SLOTS + D]
        vd_scales = sb("vd_scales", [P, SLOTS], U8)

        def quantise_vd():
            nc.vector.quantize_mx(
                out=vd_codes.bitcast(E4M3), scales=vd_scales[:],
                in_=vd_in[:].rearrange("p r s t -> p (r s t)"),
            )

        u_first = sb("u_first", [P, HALF, LANES], BF16, "sv_col")
        u_in = [u_first[:, 0:P, :], u_first[:, P:HALF, :]]
        for b, at in ((2, 0), (3, 7 * SLOTS)):
            u_in.append(laid.tile([P, P, LANES], BF16, name="u_in%d" % b, offset=at, align_bytes=64)[:])
        u_codes = sb("u_codes", [P, SLOTS], U32)
        u_scales = sb("u_scales", [P, SLOTS], U8)

        def gather_first(t):
            nc.vector.tensor_copy(u_first[:, :, t], u_win[t].indirect(entries(offs_sb, 0, HALF)))

        for b in (2, 3):
            nc.scalar.copy(u_in[b][:, :, 0:2], u_got[:, :, b * P : (b + 1) * P].rearrange("p t i -> p i t"))
        u_late = sb("u_late", [P, 2, HALF], BF16)
        gather_first(2)
        nc.scalar.copy(u_first[:, :, 0:2], u_got[:, :, 0:HALF].rearrange("p t i -> p i t"))
        nc.vector.tensor_copy(u_late[:, 0, :], u_win[2].indirect(entries(offs_sb, HALF, SLOTS)))
        quantise_vd()
        gather_first(3)
        for lo in (0, P):
            nc.scalar.activation(
                u_late[:, 1, lo : lo + P], u_win[3].indirect(entries(offs_sb, HALF + lo, HALF + lo + P)), ACT.Copy
            )
        for b in (2, 3):
            lo = (b - 2) * P
            nc.scalar.copy(u_in[b][:, :, 2:4], u_late[:, :, lo : lo + P].rearrange("p t i -> p i t"))
        for b in range(BLOCKS):
            cols = slice(b * P, (b + 1) * P)
            nc.vector.quantize_mx(
                out=u_codes[:, cols].bitcast(E4M3), scales=u_scales[:, cols],
                in_=u_in[b].rearrange("p i t -> p (i t)"),
            )

        vt_scales = sb("vt_scales", [P, D], U8)
        nc.vector.quantize_mx(
            out=vt_codes.bitcast(E4M3), scales=vt_scales[:],
            in_=vt_in[:].rearrange("s t p r -> s (t p r)"),
        )

        a_sv = [laid.tile([P, SLOTS], F32, name="a_sv%d" % b, offset=4 * SLOTS * b, align_bytes=64)[:] for b in range(2)]
        a_sv = a_sv + [sb("a_sv%d" % b, [P, SLOTS], F32)[:] for b in range(2, BLOCKS)]
        sig = [sb("sig%d" % b, [P, SLOTS], F32) for b in range(BLOCKS)]
        neg_late = laid.tile([P, 2, LANES, P], F32, name="neg_late", offset=8 * SLOTS, align_bytes=64)
        neg_y = [sb("neg_y%d" % b, [P, LANES, P], F32)[:] for b in range(2)] + [neg_late[:, b] for b in range(2)]
        g_in = sb("g_in", [P, LANES * SLOTS], BF16)
        g_codes = sb("g_codes", [P, SLOTS], U32)
        g_scales = sb("g_scales", [P, SLOTS], U8)
        a_ps = [bank("a_ps", 4 + b) for b in range(BLOCKS)]
        diff = [bank("diff", 4 + b) for b in range(BLOCKS)]

        def turn(b, src, first):
            for r in range(LANES):
                nc.tensor.matmul(
                    diff[b][:, r, :], lhsT=src[:, r * P : (r + 1) * P], rhs=ident[:], is_transpose=True,
                    start=(first and r == 0), stop=(not first and r == LANES - 1),
                )

        def labels(b):
            dealt = neg_y[b].rearrange("p r s -> p s r")
            plain = y_sb[b][:].rearrange("p (s r) -> p s r", r=LANES)
            if b < 2:
                nc.scalar.activation(dealt, plain, ACT.Copy, scale=-1.0)
            else:
                nc.gpsimd.tensor_scalar(
                    neg_y[b], y_sb[b][:].rearrange("p (s r) -> p r s", r=LANES), -1.0, 0.0, ALU.mult, ALU.add
                )

        def score(b):
            cols = slice(b * P, (b + 1) * P)
            flat = a_ps[b][:].rearrange("p r s -> p (r s)")
            nc.tensor.matmul_mx(
                out=flat,
                lhsT=u_codes[:, cols].bitcast(E4M3), lhsT_scale=u_scales[:, cols],
                rhs=vd_codes.bitcast(E4M3), rhs_scale=vd_scales[:],
                start=True, stop=True,
            )
            nc.vector.tensor_tensor(a_sv[b], flat, sv_all[:], ALU.mult)
            nc.scalar.activation(sig[b][:], a_sv[b], ACT.Sigmoid, scale=su_col[:, b : b + 1])

        def grad(b):
            turn(b, neg_y[b].rearrange("p r s -> p (r s)"), True)
            turn(b, sig[b][:], False)
            nc.vector.tensor_tensor(
                g_in[:, b * SLOTS : (b + 1) * SLOTS].rearrange("s (i r) -> s i r", r=LANES),
                diff[b][:].rearrange("s r i -> s i r"),
                both[:, b * P : (b + 1) * P, :],
                ALU.mult,
            )

        def quantise_g(lo, hi):
            cols = slice(lo, hi)
            nc.vector.quantize_mx(
                out=g_codes[:, cols].bitcast(E5M2), scales=g_scales[:, cols],
                in_=g_in[:, LANES * lo : LANES * hi],
            )

        def product(t, lo, hi, out):
            tcols = slice(t * P, (t + 1) * P)
            nc.tensor.matmul_mx(
                out=out,
                lhsT=vt_codes[:, tcols].bitcast(E4M3), lhsT_scale=vt_scales[:, tcols],
                rhs=g_codes[:, lo:hi].bitcast(E5M2), rhs_scale=g_scales[:, lo:hi],
                start=True, stop=True,
            )

        def flat_bank(number):
            return bank("du_ps", number)[:].rearrange("p a b -> p (a b)")

        for b in range(BLOCKS):
            labels(b)
        for b in range(BLOCKS):
            score(b)
        grad(0)
        grad(1)
        quantise_g(0, P)
        quantise_g(P, HALF)
        grad(2)
        early_ps = [flat_bank(t) for t in range(LANES)]
        grad(3)
        for t in (0, 1, 3, 2):
            product(t, 0, HALF, early_ps[t][:, 0:HALF])
        quantise_g(HALF, HALF + P)
        quantise_g(HALF + P, SLOTS)
        late_ps = [flat_bank(4 + t) for t in range(LANES)]
        for t in (0, 1, 3, 2):
            product(t, HALF, SLOTS, late_ps[t][:, 0:HALF])

        out_rows = out_0.rearrange("(p t) c -> t p c", t=LANES)

        def scatter_v(t, lo, hi, src):
            nc.vector.tensor_copy(out_win[t][:].indirect(entries(offs_sb, lo, hi)), src)

        def scatter_s(t, h, src):
            nc.scalar.activation(
                out_win[t][:].indirect(entries(offs_sb, h * HALF, (h + 1) * HALF)), src, ACT.Copy
            )

        def store(t):
            nc.sync.dma_start(out=out_rows[t], in_=out_win[t][:])

        for t in range(2):
            early = sb("early%d" % t, [P, HALF], F32)
            nc.scalar.copy(early[:], early_ps[t][:, 0:HALF])
            scatter_s(t, 0, early[:])
        early3 = sb("early3", [P, HALF], F32, "g_in")
        nc.vector.tensor_copy(early3[:], early_ps[3][:, 0:HALF])
        spot = 16 * SLOTS + 2 * HALF
        places = (spot + 16 * SLOTS, spot, spot - 2 * HALF, spot + 2 * HALF)
        late = [
            laid.tile([P, HALF], F32, name="late%d" % t, offset=places[t], align_bytes=64) for t in range(LANES)
        ]
        for t in range(2):
            nc.vector.tensor_copy(late[t][:], late_ps[t][:, 0:HALF])
        scatter_v(0, HALF, SLOTS, late[0][:])
        store(0)
        early2 = sb("early2", [P, HALF], F32, "early0")
        scatter_v(1, HALF, SLOTS, late[1][:])
        store(1)
        nc.scalar.copy(early2[:], early_ps[2][:, 0:HALF])
        scatter_s(3, 0, early3[:])
        scatter_s(2, 0, early2[:])
        for t in (3, 2):
            nc.vector.tensor_copy(late[t][:], late_ps[t][:, 0:HALF])
        scatter_v(3, HALF, SLOTS, late[3][:])
        store(3)
        scatter_s(2, 1, late[2][:])
        store(2)

        pairs = sb("pairs", [P, 2 * SPLIT], F32)
        o_codes = sb("o_codes", [P, TABLE], U32)
        o_scales = sb("o_scales", [P, PLANE], U8)
        words_out = out_1[0].rearrange("p c l -> p (c l)").bitcast(I32)
        o_in = sb("o_in", [P, LANES * TABLE], BF16)

        def halves(t):
            return pairs[:, (t // 2) * SPLIT : (t // 2 + 1) * SPLIT].bitcast(BF16)[:, t % 2 : 2 * SPLIT : 2]

        for t in (0, 1):
            nc.gpsimd.tensor_scalar(halves(t), out_win[t][:, 0:SPLIT], 1.0, -0.0, ALU.mult, ALU.add)
        nc.vector.tensor_copy(halves(3), out_win[3][:, 0:SPLIT])
        for lo, hi in ((0, 2 * RANGE), (2 * RANGE, SPLIT)):
            nc.vector.tensor_copy(halves(2)[:, lo:hi], out_win[2][:, lo:hi])

        groups = (TABLE - SPLIT) // HALF
        turned = [
            laid.tile([P, 2 * groups, P, 2], BF16, name="turned0", offset=spot - 8 * groups * P, align_bytes=64),
            sb("turned1", [P, 2 * groups, P, 2], BF16),
        ]
        for u in range(2):
            there = [bank("there", groups * u + k) for k in range(groups)]
            for e in (1, 0):
                for j in range(2 * groups):
                    lo = SPLIT + j * P
                    nc.tensor.transpose(
                        there[j // 2][:, 2 * (j % 2) + e, :], out_win[2 * u + e][:, lo : lo + P], ident[:]
                    )
            for k in range(groups):
                nc.scalar.copy(
                    turned[u][:, 2 * k : 2 * k + 2], there[k][:].rearrange("c (j e) p -> c j p e", e=2)
                )
        for k in range(groups):
            back = bank("back", (2 * groups + k) % 8)
            for u in range(2):
                for j in range(2):
                    words = turned[u][:, 2 * k + j].rearrange("c p e -> c (p e)").bitcast(F32)
                    nc.tensor.transpose(back[:, 2 * j + u, :], words, ident[:])
            lo = SPLIT + k * HALF
            nc.scalar.copy(
                o_in[:, LANES * lo : LANES * (lo + HALF)].bitcast(F32).rearrange("p (j c u) -> p j c u", j=2, u=2),
                back[:].rearrange("p (j u) c -> p j c u", u=2),
            )

        def weave(lo, hi):
            nc.vector.tensor_copy(
                o_in[:, LANES * lo : LANES * hi].bitcast(F32).rearrange("p (c e u) -> p c u e", e=2, u=2),
                pairs[:].rearrange("p (u c e) -> p c u e", u=2, e=2)[:, lo // 2 : hi // 2, :, :],
            )

        def quantise_out(lo, hi):
            plane, at = divmod(lo, PLANE)
            nc.vector.quantize_mx(
                out=o_codes[:, lo:hi].bitcast(E4M3),
                scales=o_scales[4 * plane : P, at : at + hi - lo],
                in_=o_in[:, LANES * lo : LANES * hi],
            )

        cuts = (0, RANGE, 2 * RANGE, 3 * RANGE, TABLE - HALF, TABLE)
        for lo in (0, RANGE):
            weave(lo, lo + RANGE)
        stored = 0
        for lo, hi in zip(cuts, cuts[1:]):
            if lo == 2 * RANGE:
                weave(lo, SPLIT)
            quantise_out(lo, hi)
            if hi in (2 * RANGE, 3 * RANGE, TABLE):
                nc.sync.dma_start(out=words_out[:, stored:hi], in_=o_codes[:, stored:hi].bitcast(I32))
                stored = hi
        for q in range(4):
            (nc.scalar, nc.sync)[q % 2].dma_start(
                out=out_2[0, 4 * q : 4 * q + 4, :].bitcast(I32).rearrange("r (a c) -> a r c", a=TABLE // PLANE),
                in_=o_scales[32 * q : 32 * q + 4 * (TABLE // PLANE), :].bitcast(I32),
            )
